import numpy as np, ml_dtypes
CORES = [3,11,19,27,35,43,51,59]
N = 8
import mx_ref
BF = ml_dtypes.bfloat16
def gcols(t, e):
    v = np.concatenate([t.reshape(8, 16, -1, 4), np.zeros((8, 16, 1, 4), BF)], axis=2)
    return np.ascontiguousarray(np.stack([v[g][:, e[g]] for g in range(8)])).reshape(128, -1)
def tile(rs):
    return np.stack(rs, axis=2).reshape(128, -1).astype(BF)
def cut(t, i, w=512):
    return t[:, w * i:w * i + w]
def pick(q, e):
    c = np.concatenate([q[0].reshape(128, -1, 4), np.zeros((128, 1, 4), np.uint8)], axis=1); s = np.concatenate([q[1], np.ones((16, 1), np.uint8)], axis=1)
    return (np.ascontiguousarray(c[:, e].reshape(128, -1)), np.ascontiguousarray(s[:, e]))
def join(*qs):
    return (np.concatenate([q[0] for q in qs], axis=1), np.concatenate([q[1] for q in qs], axis=1))
def put(q, e, v):
    c, s = q[0].reshape(128, -1, 4).copy(), q[1].copy(); c[:, e] = v[0].reshape(128, -1, 4); s[:, e] = v[1]
    return (c.reshape(128, -1), s)
def pk(c, s):
    return (np.ascontiguousarray(c), mx_ref.live(s))
def emit(q):
    return q[0], q[1]
def packed(v, rng):
    q = [mx_ref.quantize(np.ascontiguousarray(v[r])) for r in range(N)]
    return np.stack([a for a, b in q]), np.stack([mx_ref.plane(b, rng) for a, b in q])
def values_of_codes():
    e, c = np.zeros((128, 128, 4), np.float32), np.zeros((128, 2, 4), np.uint8)
    e[np.arange(128), np.arange(128), 0] = 1
    c[:127, :, 0] = np.arange(256).reshape(2, 128).T[:127]
    return mx_ref.matmul(mx_ref.quantize(e.reshape(128, 512).astype(BF)), (c.reshape(128, 8), np.full((16, 2), 127, np.uint8))).T.reshape(-1).astype(np.float64)
CODE_VALUE, SCALE_VALUE = values_of_codes(), 2.0 ** (np.arange(256) - 127.0)
def decode(q):
    return (CODE_VALUE[q[0]].reshape(16, 8, -1, 4) * SCALE_VALUE[q[1]][:, None, :, None] + 0.0).reshape(128, -1).astype(np.float32)
def f(rng, *shape):
    return mx_ref.flush((rng.standard_normal(shape, dtype=np.float32) * np.exp2(rng.integers(-2, 3, shape[:-1] + (1,)))).astype(BF))
def wide(rng, *shape, cols=0):
    v = rng.standard_normal(shape, dtype=np.float32) * np.exp2(rng.integers(-12, 13, shape)).astype(np.float32)
    if cols: v *= np.repeat(np.exp2(rng.integers(-cols, cols + 1, shape[:-2] + (1, shape[-1] // 4))) * (rng.random(shape[:-2] + (1, shape[-1] // 4)) > 0.0625), 4, axis=-1).astype(np.float32)
    return mx_ref.flush(v.astype(BF))
S, C, L, Q1, Q2, R = 256, 192, 64, 14, 52, 3
def numbers_of(rng):
    return {"x": np.array(f(rng, N, 128, 4 * C)), "u": np.array(f(rng, N, 128, 512)), "v": np.array(f(rng, N, 128, 512))}
def weights(rng, w):
    c, p = packed(w, rng)
    return {"wc": c, "ws": p}
def shift(rng, mix=False):
    w = np.zeros((128, 4, 128, 4), np.float32)
    i = np.arange(128)
    first = i[i % 16 < 8]
    i = i[(i % 16 >= 8) & (i % 16 < 14)]
    for b in range(4):
        w[i, b, i, b] = -64
        w[i + 2, b, i, b] = 64
        if mix: w[(first + 16) % 128, b, first, b] = 64
    return weights(rng, np.stack([w.reshape(128, 2048).astype(BF)] * N))
def planned(rng, a, step, k, mix=False):
    d = numbers_of(rng)
    x = d["x"].astype(np.float32).reshape(N, 8, 16, C, 4)
    g = ((a[..., None] >> np.arange(8)) & 1) * 2.0 ** np.arange(8) * step
    x[:, :, 8:] = g.reshape(4, N, 8, C, 2, 4).transpose(1, 2, 0, 4, 3, 5).reshape(N, 8, 8, C, 4)
    u = d["u"].reshape(N, 128, 128, 4)
    u[:, :, ::16] = 0
    for h in range(0, 128, 16): u[:, h + 8:h + 10, h] = k.astype(np.float32).astype(BF)[:, None, None]
    return {"x": d["x"], "u": u.reshape(N, 128, 512), "v": d["v"], **shift(rng, mix)}, x
def with_x(d, x):
    d["x"] = x.astype(np.float32).reshape(N, 128, 4 * C).astype(BF)
    return d
def setup_inputs(rng):
    return {**numbers_of(rng), **weights(rng, f(rng, N, 128, 2048))}
def setup_inputs_ties(rng):
    o = rng.permutation(N)
    a = rng.integers(0, 3, (4, N, 8, C))
    a[:, o[0]] = 1
    d, x = planned(rng, a, 1.0, np.ones(N))
    x[o[1]] = 0
    s = rng.integers(0, 6, (4, 8, C))
    x[o[2], :, 8:] = 0
    for i in range(4):
        x[o[2], :, 8 + 2 * i, :, 0] = (8 + s[i]) * 2.0 ** -33
        x[o[2], :, 9 + 2 * i, :, 0] = (9 + s[i]) * 2.0 ** -33
    u = d["u"].reshape(N, 128, 128, 4)
    for h in range(0, 128, 16):
        u[o[2], h + 8, h] = BF(9 * 2.0 ** -33)
        u[o[2], h + 9, h] = BF(-2.0 ** -30)
    d["u"] = u.reshape(N, 128, 512)
    return with_x(d, x)
def setup_inputs_near(rng):
    k = (np.arange(N) + rng.integers(N)) % N < N // 2
    k = np.where(k, 2.0 ** -30, 1.0)
    d, x = planned(rng, rng.integers(0, 256, (4, N, 8, C)), 2.0 ** -23, k)
    x[:, :, :8] = (0.25 + 0.75 * rng.random((N, 8, 8, C, 4))) * rng.choice([-1.0, 1.0], (N, 8, 8, C, 4))
    x[:, :, 0] = 0
    x[:, :, 0, :, 0] = (rng.permutation(8) % 2 * 2.0 - 1.0)[None, :, None]
    x[k < 1] *= np.float32(2.0 ** -7)
    u = d["u"].reshape(N, 128, 128, 4)
    for h in range(0, 128, 16): u[:, h, h, 0] = k.astype(np.float32).astype(BF)
    d["u"] = u.reshape(N, 128, 512)
    return with_x(d, x)
def setup_inputs_huge(rng):
    d = numbers_of(rng)
    x = 2.0 ** 30 * (0.6 + 0.4 * rng.random((N, 128, C, 4)))
    c = np.stack([rng.permutation(C) % 2 * 2.0 - 1.0 for r in range(N)])
    c[rng.permutation(N) < N // 2] = 1
    x *= c[:, None, :, None]
    u = d["u"].reshape(N, 128, 128, 4)
    s = np.stack([rng.permutation(8) % 2 * 2.0 - 1.0 for r in range(N)])
    u[:, :, ::16] = (2.0 ** 30 * (1 - 0.25 * rng.random((N, 128, 8, 4))) * s[:, None, :, None]).astype(np.float32).astype(BF)
    w = np.zeros((128, 4, 128, 4), np.float32)
    i = np.arange(128)
    for b in range(4): w[i, b, i, b] = 2.0 ** -10
    return with_x({"x": d["x"], "u": u.reshape(N, 128, 512), "v": d["v"], **weights(rng, np.stack([w.reshape(128, 2048).astype(BF)] * N))}, x)
def entering(m, h, rng):
    n = S // 16
    w = np.zeros(n, int)
    rest = L
    if m < 2:
        o = rng.permutation(n // 4)
        w[4 * o[0]:4 * o[0] + 4] = Q1 - h
        rest -= 4 * (Q1 - h)
        for i in o[1:]:
            c = min(rest, Q2 - 4 * h + int(m == 1 and i == o[1]))
            w[4 * i + rng.integers(4)] = c
            rest -= c
    elif m == 2:
        a = int(rng.integers(n))
        w[a] = Q1 + 1 - h
        rest -= Q1 + 1 - h
        for i in rng.permutation(n):
            if i // 4 != a // 4:
                w[i] = min(rest, Q1 - h)
                rest -= w[i]
    elif m == 3: w[rng.integers(n)] = L
    else: w = np.bincount(rng.integers(0, n, L), minlength=n)
    return w
def setup_inputs_crowd(rng):
    n = S // 16
    leaf = np.arange(C) * S // C // 16
    a = rng.integers(0, 256, (4, N, 8, C))
    a[3] = rng.integers(100, 104, (N, 8, C))
    stay = np.ones((N, 8, C), bool)
    m = np.stack([rng.permutation(8) for r in range(N)])
    gone = [[[0], [0, 1], [int(rng.integers(1, n - 2)), n - 1]][i % 3] for i in rng.permutation(N)]
    for r in range(N):
        for g in range(8):
            a[0, r, g] = rng.permutation(C)
            k = np.full(n, L // n)
            if m[r, g] == 6:
                other = np.setdiff1d(np.arange(n), gone[r])
                k[gone[r]] = C // n
                k[rng.permutation(other)] = (L - len(gone[r]) * (C // n) + np.arange(len(other))) // len(other)
            for i in range(n):
                e = rng.permutation(np.flatnonzero(leaf == i))
                if i == 0: e = np.concatenate([[0], e[e > 0]])
                stay[r, g, e[:k[i]]] = False
    for r in range(N):
        for g in range(8):
            if m[r, g] == 4: e = np.zeros(L, int)
            elif m[r, g] == 5: e = np.full(L, C - 1)
            else:
                if m[r, g] == 6:
                    room = Q1 - np.bincount(leaf[stay[r, g]], minlength=n)
                    room[gone[r]] = 0
                    first = np.zeros(6, int)
                    if gone[r][0] > 0:
                        c = gone[r][0] - 1
                        room[[c, n - 2]] -= 2
                        i = int(np.flatnonzero(stay[r, g] & (leaf == c))[-1])
                        first = np.array([i, i, C - 1, C - 1])
                    w = np.bincount(rng.permutation(np.repeat(np.arange(n), room))[:L - len(first)], minlength=n)
                else:
                    w = entering(m[r, g], C // n - L // n, rng)
                    first = np.zeros(L - int(np.sum(w)), int)
                e = np.concatenate([first] + [rng.choice(np.flatnonzero(stay[r, g] & (leaf == i)), w[i]) for i in np.flatnonzero(w)])
            s = (r - 1) % N
            b = rng.integers(C, 256, C)
            b[~stay[s, g][a[0, s, g]]] = rng.permutation(e)
            a[1, s, g] = b
    d, x = planned(rng, a, 1.0, np.ones(N), True)
    return with_x(d, x)
def setup_inputs_spread(rng):
    d = setup_inputs(rng)
    d["x"] = wide(rng, N, 128, 4 * C, cols=6)
    return d
def check_inputs(d):
    b = []
    for k in ("x", "u", "v"):
        a = np.abs(d[k].astype(np.float32))
        if not (np.isfinite(a).all() and ((a == 0) | (a >= 2.0 ** -30) & (a <= 2.0 ** 30)).all()): b.append("a value of " + k)
    for r in range(N):
        if ((d["wc"][r] & 127) == 127).any(): b.append("a code of wc that is no number")
        with np.errstate(over="ignore"): a = np.abs(decode(pk(d["wc"][r], d["ws"][r])))
        if not ((a == 0) | (a >= 2.0 ** -30) & (a <= 2.0 ** 30)).all(): b.append("a value of W (wc, ws)")
    return b
def respread(h, key, new):
    n = np.searchsorted(key[h], new, side="right")
    leaf = np.where(n > 0, h[np.maximum(n - 1, 0)], 0) // 16
    k = np.concatenate([key[h], new])
    i = np.argsort(k, kind="stable")
    src = np.concatenate([h, S + np.arange(L)])[i]
    at = src.copy()
    lf = np.concatenate([h // 16, leaf])[i]
    count = np.bincount(lf, minlength=S // 16)
    size = np.where(count <= Q1, 16, np.where(np.repeat(np.sum(count.reshape(-1, 4), axis=1), 4) <= Q2, 64, S))
    size[np.bincount(leaf, minlength=S // 16) == 0] = 0
    for w in (16, 64, S):
        for s in range(0, S, w):
            if (size[s // 16:(s + w) // 16] == w).any():
                e = np.flatnonzero(lf * 16 // w == s // w)
                at[e] = s + np.arange(len(e)) * w // len(e)
    to, kept = np.full(S, -1), np.zeros(S, np.float32)
    to[at] = src
    kept[at] = k[i]
    return to, kept
def reference(x, u, v, wc, ws):
    qu = [mx_ref.quantize(u[r]) for r in range(N)]
    lay = [pk(wc[r], ws[r]) for r in range(N)]
    start = np.arange(C) * S // C
    now, key, held = [], [], []
    for r in range(N):
        p = mx_ref.matmul(qu[r], mx_ref.quantize(x[r]))[::16] + np.float32(0.0)
        o = np.argsort(p, axis=1, kind="stable")
        e, k = np.full((8, S), -1), np.zeros((8, S), np.float32)
        e[:, start] = o
        k[:, start] = np.take_along_axis(p, o, axis=1)
        now.append(gcols(x[r], e))
        key.append(k)
        held.append(e >= 0)
    y, ol = np.zeros((N, 128, S), np.float32), np.zeros((N, 8, S), np.float32)
    oc, osc = np.zeros((N, 128, 4 * S), np.uint8), np.zeros((N, 16, S), np.uint8)
    for t in range(R):
        made, new, border = [], [], []
        for r in range(N):
            q = mx_ref.quantize(now[r])
            made.append(tile([mx_ref.matmul(pick(lay[r], np.arange(128 * b, 128 * b + 128)), q) * np.float32(0.015625) + now[r][:, b::4].astype(np.float32) for b in range(4)]))
            p = mx_ref.matmul(qu[r], mx_ref.quantize(made[r]))[::16] + np.float32(0.0)
            o = np.argsort(np.where(held[r], p, np.float32(np.inf)), axis=1, kind="stable")[:, :L]
            new.append(np.take_along_axis(p, o, axis=1))
            np.put_along_axis(held[r], o, False, axis=1)
            border.append(mx_ref.quantize(gcols(made[r], o)))
        came = decode(join(*border)).astype(BF)
        for r in range(N):
            e = (r - 1) % N
            to, k = np.full((8, S), -1), np.zeros((8, S), np.float32)
            for g in range(8): to[g], k[g] = respread(np.flatnonzero(held[r][g]), key[r][g], new[e][g])
            now[r] = gcols(np.concatenate([made[r], cut(came, e, 4 * L)], axis=1), to)
            key[r], held[r], ol[r] = k, to >= 0, to
    for r in range(N):
        q = mx_ref.quantize(now[r])
        y[r] = mx_ref.matmul(mx_ref.quantize(v[r]), q)
        oc[r], osc[r] = emit(q)
    return {"y": y, "ol": ol, "oc": oc, "osc": osc}

@@ -1,0 +1,590 @@
+from concourse.mybir import dt, AluOpType, AxisListType, ActivationFunctionType
+
+A = AluOpType
+COPY = ActivationFunctionType.Copy
+IDENT = ActivationFunctionType.Identity
+RELU = ActivationFunctionType.Relu
+SIGN = ActivationFunctionType.Sign
+BIG = 2.0 ** 96
+ROUNDS = 3
+W64 = 4 * 256
+UP_ = 0.5 - 1.0 / 512
+ON_SCALAR = 3
+
+SCRATCH = {}
+
+
+def _decl(names, where, shape, dtype):
+    for n in names.split():
+        SCRATCH[n] = (where, shape, dtype)
+
+
+_decl("XT", "sbuf", [128, 832], "bfloat16")
+_decl("UT VT E0 E1 E2 E3 ONEB", "sbuf", [128, 512], "bfloat16")
+_decl("TI FA FB", "sbuf", [128, 1024], "bfloat16")
+_decl("TP0 TP1 TP2 TP3", "sbuf", [128, 528], "bfloat16")
+_decl("AD0 AD1 AD2 AD3 G0 G1 G2 G3", "sbuf", [128, 256], "bfloat16")
+_decl("CMP", "sbuf", [128, 2304], "bfloat16")
+_decl("JNK", "sbuf", [128, 1536], "bfloat16")
+_decl("CMQ", "sbuf", [128, 768], "float32")
+_decl("CMN", "sbuf", [128, 768], "bfloat16")
+_decl("QX", "sbuf", [128, 192], "float8_e4m3fn_x4")
+_decl("QXS", "sbuf", [128, 192], "uint8")
+_decl("QU QVC UR UP EQ0 EQ1 EQ2 EQ3", "sbuf", [128, 128], "float8_e4m3fn_x4")
+_decl("QUS QVS URS UPS EQS0 EQS1 EQS2 EQS3", "sbuf", [128, 128], "uint8")
+_decl("WQ", "sbuf", [128, 512], "float8_e4m3fn_x4")
+_decl("WS", "sbuf", [128, 512], "uint8")
+_decl("QF QT0 QT1 QT2 LQ0 LQ1 LQ2", "sbuf", [128, 256], "float8_e4m3fn_x4")
+_decl("QFS QTS0 QTS1 QTS2 LS0 LS1 LS2", "sbuf", [128, 256], "uint8")
+_decl("PS0 PS1 PS2 PS3 PP PQ PD0 PD1", "psum", [128, 512], "float32")
+_decl("IOTA HRA HRB", "sbuf", [128, 512], "float32")
+_decl("JM MASK DMASK RST RMIN ONE ZERO TMP TMY YS PR PPR FLB SFP CSP XWS OLR HROL YO", "sbuf", [128, 256], "float32")
+_decl("KA KB SEQ SEQO", "sbuf", [128, 448], "float32")
+_decl("SEQS XC", "sbuf", [128, 208], "float32")
+_decl("SC Z EQR LROW SF CCS KST LBM LBK", "sbuf", [128, 192], "float32")
+_decl("ARR64", "sbuf", [128, 256], "float32")
+_decl("KW XCW HW", "sbuf", [128, 16], "float32")
+SMALL = ("EB D1 ARB CSMB GM B32 B32T X2 PAR C1C D0A D0B UA UB I0 I1 UX C64I UY C12 RST4 C16 IW C257 M16 M17 CNT RK LFN KWB "
+         "LF3 TB XM XV NCM TH HBP AX BA S4 E64 EQD EP1 CE3 EP3 VL NI ENI EN2 TT JW1 KI0 ENC INV AC0 SP PH LB AR1 S256 HBB HB1 "
+         "S16 S161 CN4 BAD4 ZX4").split()
+_decl("SMALLS", "sbuf", [128, 40 * len(SMALL)], "float32")
+_decl("INTS", "sbuf", [128, 16 * 11], "int32")
+_decl("LW0 LW1 LW2 LP0 LP1 LP2", "sbuf", [128, 4], "uint16")
+_decl("LISTS", "sbuf", [128, 16 * 12], "uint16")
+_decl("OFF", "sbuf", [128, 64], "uint16")
+PIECE = {n: ("SMALLS", 40 * i) for i, n in enumerate(SMALL)}
+PIECE.update({n: ("INTS", 16 * i) for i, n in enumerate("PI SI PHI I2 KI KA4 KB4 UI QI HBI H3".split())})
+PIECE.update({n: ("LISTS", 16 * i) for i, n in enumerate("RKU HUA HUB QVA QVB QDU TU XL AL UL OFY".split())})
+PIECE.update({n: ("ARR64", 64 * i) for i, n in enumerate("LL AOS ARC BIGS".split())})
+
+SEMAPHORES = ["sv", "ss", "st", "sg", "dx", "du", "dw", "dws", "dv", "dout", "loc", "au", "fk", "fx", "fh",
+              "aq0", "aq1", "aq2", "al0", "al1", "al2"]
+
+
+def R(name, a=0, b=16, st=1, off=None, bc=None):
+    n, k = PIECE.get(name, (name, 0))
+    return (n, k + a, k + b, st, off, bc)
+
+
+def rank_program(g, core, T, topo):
+    rank = T.rank_of(core)
+    if rank is None:
+        return
+    nxt = T.cores[(rank + 1) % len(T.cores)]
+
+    Q = {"v": g.vector, "s": g.scalar, "t": g.tensor, "g": g, "y": g.sync}
+    sem_of = {"v": "sv", "s": "ss", "t": "st", "g": "sg"}
+    cnt = {q: 0 for q in Q}
+    known = {q: {} for q in Q}
+    clocks = {}
+    hist = {}
+
+    def ap(r):
+        n, a, b, st, off, bc = r
+        x = T[n][:, a:b] if st == 1 else T[n][:, a:b:st]
+        if bc is not None:
+            x = x.bitcast(bc)
+        if off is not None:
+            x = x.indirect(ap(off))
+        return x
+
+    def meet(h, r):
+        if h[0] >= r[2] or r[1] >= h[1]:
+            return False
+        return not (h[2] > 1 and h[2] == r[3] and (h[0] - r[1]) % h[2])
+
+    def wait(q, src, val):
+        if known[q].get(src, 0) >= val:
+            return
+        Q[q].wait_ge(T.sem[sem_of.get(src, src)], val)
+        for s, v in clocks[(src, val)].items():
+            if known[q].get(s, 0) < v:
+                known[q][s] = v
+
+    def psum(n):
+        return n in SCRATCH and SCRATCH[n][0] == "psum"
+
+    def note(src, val, writes, reads):
+        for w in writes:
+            h = hist.setdefault(w[0], [])
+            if w[3] == 1 and w[4] is None:
+                h[:] = [e for e in h if not (w[1] <= e[0] and e[1] <= w[2])]
+            h.append((w[1], w[2], w[3], True, src, val))
+        for r in reads:
+            hist.setdefault(r[0], []).append((r[1], r[2], r[3], psum(r[0]), src, val))
+
+    def emit(q, call, writes, reads, event=None):
+        reads = list(reads)
+        for r in list(reads) + list(writes):
+            if r[4] is not None:
+                reads.append(r[4])
+        need = {}
+        for r in reads:
+            for h in hist.get(r[0], ()):
+                if meet(h, r) and h[3] and not (psum(r[0]) and h[4] == q):
+                    need[h[4]] = max(need.get(h[4], 0), h[5])
+        for w in writes:
+            for h in hist.get(w[0], ()):
+                if meet(h, w):
+                    need[h[4]] = max(need.get(h[4], 0), h[5])
+        for src in sorted(need, key=lambda s: -len(clocks[(s, need[s])])):
+            wait(q, src, need[src])
+        i = call()
+        if event is None:
+            cnt[q] += 1
+            i.then_inc(T.sem[sem_of[q]], 1)
+            src, val = q, cnt[q]
+        else:
+            src, val, inc = event
+            i.then_inc(T.sem[src], inc)
+        clocks[(src, val)] = dict(known[q])
+        clocks[(src, val)][src] = val
+        note(src, val, writes, reads)
+
+    def lands(src, val, writes):
+        clocks[(src, val)] = {src: val}
+        note(src, val, writes, [])
+
+    def isr(x):
+        return isinstance(x, tuple)
+
+    def val(x):
+        return ap(x) if isr(x) else x
+
+    def tt(o, a, b, op):
+        emit("v", lambda: g.vector.tensor_tensor(ap(o), ap(a), ap(b), op), [o], [a, b])
+
+    def ts(o, a, s1, s2, op0, op1=None):
+        rd = [a] + [x for x in (s1, s2) if isr(x)]
+        if op1 is None:
+            emit("v", lambda: g.vector.tensor_scalar(ap(o), ap(a), val(s1), None, op0), [o], rd)
+        else:
+            emit("v", lambda: g.vector.tensor_scalar(ap(o), ap(a), val(s1), val(s2), op0, op1), [o], rd)
+
+    def cp(o, a):
+        emit("v", lambda: g.vector.tensor_copy(ap(o), ap(a)), [o], [a])
+
+    def scan(o, d0, d1, op0=A.mult, op1=A.add, init=0.0):
+        emit("v", lambda: g.vector.tensor_tensor_scan(ap(o), ap(d0), ap(d1), init, op0, op1), [o], [d0, d1])
+
+    def red(o, a, op):
+        emit("v", lambda: g.vector.tensor_reduce(ap(o), ap(a), AxisListType.X, op), [o], [a])
+
+    def fill(o, c):
+        emit("v", lambda: g.vector.memset(ap(o), c), [o], [])
+
+    def turn(o, a):
+        emit("v", lambda: g.vector.transpose(ap(o), ap(a)), [o], [a])
+
+    def quant(o, s, a, n):
+        o, s, a = R(o, 0, n), R(s, 0, n), R(a, 0, 4 * n)
+        emit("v", lambda: g.vector.quantize_mx(ap(o), ap(s), ap(a)), [o, s], [a])
+
+    def act(o, a, func=COPY, scale=1.0, bias=0.0):
+        rd = [a] + [x for x in (scale, bias) if isr(x)]
+        if func == COPY and not isr(scale) and scale == 1.0:
+            emit("s", lambda: g.scalar.activation(ap(o), ap(a), COPY), [o], rd)
+        elif func == COPY:
+            emit("s", lambda: g.scalar.activation(ap(o), ap(a), COPY, scale=val(scale)), [o], rd)
+        else:
+            emit("s", lambda: g.scalar.activation(ap(o), ap(a), func, bias=val(bias), scale=val(scale)), [o], rd)
+
+    turns = [0]
+
+    def total(o, a, n, func=COPY):
+        j = R("JNK", 192 * (turns[0] % 8), 192 * (turns[0] % 8) + n)
+        turns[0] += 1
+        emit("s", lambda: g.scalar.activation(ap(j), ap(a), func, accum_out=ap(o)), [j, o], [a])
+
+    def mm(o, l, ls, r, rs, n=256, c=0):
+        o, l, ls, r, rs = R(o, 0, n), R(l, c, c + 128), R(ls, c, c + 128), R(r, 0, n), R(rs, 0, n)
+        emit("t", lambda: g.tensor.matmul_mx(ap(o), ap(l), ap(ls), ap(r), ap(rs), True, True), [o], [l, ls, r, rs])
+
+    def iota(o, pattern, base=0, cm=0):
+        if SCRATCH[o[0]][2] == "int32":
+            emit("g", lambda: g.iota(ap(o), pattern, base, cm), [o], [])
+        else:
+            emit("g", lambda: g.iota(ap(o), pattern, base, cm, allow_small_or_imprecise_dtypes=True), [o], [])
+
+    def load(q, o, src, sem):
+        emit(q, lambda: Q[q].dma_start(ap(o), src), [o], [], (sem, 16, 16))
+
+    folded = {n: 0 for n in ("fk", "fx", "fh")}
+
+    def dma_fold(o, a, n, sem):
+        folded[sem] += n
+        for c in range(n // 16):
+            src = T[a][0:128:16, 16 * c:16 * c + 16]
+            emit("y", lambda: g.sync.dma_start(ap(R(o, c, c + 1)), src), [R(o, c, c + 1)], [R(a, 16 * c, 16 * c + 16)], (sem, folded[sem], 16))
+
+    sent = [0]
+    engines = len(topo.engines(core, nxt))
+    rid, pid = topo.addr(nxt)[:2]
+
+    def send(o, a, sem):
+        need = {}
+        for h in hist.get(a[0], ()):
+            if meet(h, a) and h[3]:
+                need[h[4]] = max(need.get(h[4], 0), h[5])
+        for src in need:
+            wait("g", src, need[src])
+        g.remote_dma(out_ap=ap(o), in_ap=ap(a), remote_sem=T.sem[sem], local_sem=T.sem["loc"], pid=pid, routing_id=rid,
+                     dma_engine_mask=topo.mask(core, nxt))
+        sent[0] += engines
+
+    def send_codes(o, os, a, s, n, sem):
+        send(R(o, 0, n, 1, None, dt.uint8), R(a, 0, n, 1, None, dt.uint8), sem)
+        send(R(os, 0, n), R(s, 0, n), sem)
+
+    lands("au", 2 * engines, [R("UP", 0, 128), R("UPS", 0, 128)])
+    for r in range(ROUNDS):
+        lands("aq%d" % r, 2 * engines, [R("LQ%d" % r, 0, 256), R("LS%d" % r, 0, 256)])
+        lands("al%d" % r, engines, [R("LP%d" % r, 0, 4)])
+
+    load("y", R("XT", 0, 768), T.x[:], "dx")
+    load("s", R("UT", 0, 512), T.u[:], "du")
+    load("y", R("WQ", 0, 512, 1, None, dt.uint8), T.wc[:], "dw")
+    load("s", R("WS", 0, 512), T.ws[:], "dws")
+    load("y", R("VT", 0, 512), T.v[:], "dv")
+
+    x = R
+    iota(R("JM", 0, 256), [[0, 16], [1, 16]])
+    iota(x("PI", 0, 1), [[1, 1]], 0, 1)
+    iota(x("UI", 0, 8), [[16, 8]])
+    iota(x("M16"), [[16, 16]])
+    iota(R("IOTA", 0, 512), [[1, 512]])
+    iota(R("HRA", 0, 192), [[4, 64], [1, 3]])
+    iota(x("GM", 0, 32), [[1, 2], [0, 16]])
+    iota(x("PAR", 0, 32), [[0, 16], [1, 2]])
+    iota(x("C1C", 0, 32), [[0, 8], [1, 4]])
+    iota(x("C12"), [[12, 16]], -192)
+    iota(x("C16"), [[16, 16]], 16)
+    iota(x("HBP"), [[-4, 16]], -4 - 192)
+    iota(R("SEQ", 192, 208), [[0, 16]], 512)
+    iota(R("SEQO", 192, 208), [[0, 16]], -1)
+    iota(R("XC", 192, 208), [[0, 16]])
+    iota(x("CSMB", 0, 8), [[0, 8]], -192)
+    for n in ("ARB", "D1", "I0", "EB", "C64I"):
+        iota(x(n, 0, 40), [[0, 40]])
+    iota(R("ONE", 0, 256), [[0, 256]], 1)
+    iota(R("ZERO", 0, 256), [[0, 256]])
+    fill(R("ONEB", 0, 512), 1.0)
+
+    def unit(b):
+        o = R("E%d" % b, 0, 512)
+        emit("g", lambda: g.affine_select(ap(o), ap(R("ONEB", 0, 512)), [[-1, 512]], A.is_equal, 0.0, b, 4), [o], [R("ONEB", 0, 512)])
+
+    for b in range(4):
+        unit(b)
+
+    ts(R("RST", 0, 256), R("JM", 0, 256), 0.0, None, A.not_equal)
+    ts(x("SI", 0, 1), x("PI", 0, 1), 15, None, A.bitwise_and)
+    cp(x("UL", 0, 8), x("UI", 0, 8))
+    cp(x("SP", 0, 1), x("SI", 0, 1))
+    s = x("SP", 0, 1)
+    ts(R("RMIN", 0, 192), R("RST", 0, 192), 2 * BIG, -BIG, A.mult, A.add)
+    ts(R("MASK", 0, 256), R("JM", 0, 256), s, None, A.is_equal)
+    fill(R("SEQS", 192, 208), 192.0)
+    ts(R("DMASK", 0, 192), R("MASK", 0, 192), 2 * BIG, -BIG, A.mult, A.add)
+    fill(R("BIGS", 0, 64), BIG)
+
+    MASK = lambda n: R("MASK", 0, n)
+    RST = lambda n: R("RST", 0, n)
+
+    def own(o, n=192):
+        return R(o, 15, n, 16)
+
+    act(x("IW"), x("M16"), IDENT, 1.0, s)
+    quant("QU", "QUS", "UT", 128)
+    quant("QX", "QXS", "XT", 192)
+    cp(R("UR", 0, 128, 1, None, dt.uint32), R("QU", 0, 128, 1, R("UL", 0, 8), dt.uint32))
+    cp(R("URS", 0, 128), R("QUS", 0, 128, 1, R("UL", 0, 8)))
+    mm("PP", "UR", "URS", "QX", "QXS", 192)
+    send_codes("UP", "UPS", "UR", "URS", 128, "au")
+    act(R("SC", 0, 192), R("PP", 0, 192))
+    cp(x("KI"), x("IW"))
+    fill(R("XT", 768, 832), 0.0)
+    ts(x("KA4"), x("KI"), 2, None, A.arith_shift_right)
+    ts(x("KB4"), x("KI"), 3, None, A.bitwise_and)
+    ts(x("KI0"), x("KA4"), 3.0, -192.0, A.mult, A.add)
+    ts(x("INV"), x("KB4"), 2.5, None, A.is_lt)
+    tt(x("ENC"), x("KI0"), x("KB4"), A.add)
+    ts(x("H3"), x("IW"), 1.0 / 3, -1.0 / 3, A.mult, A.add)
+    tt(x("EN2"), x("ENC"), x("INV"), A.mult)
+    tt(x("M17"), x("IW"), x("H3"), A.add)
+    ts(x("QVA"), x("EN2"), 192.0, None, A.add)
+    tt(R("TMP", 0, 192), R("SC", 0, 192), R("DMASK", 0, 192), A.min)
+
+    def ranks(others=()):
+        scan(R("Z", 0, 192), R("RMIN", 0, 192), R("TMP", 0, 192), A.min, A.max, -BIG)
+        for c in range(12):
+            k = R("Z", 16 * c + 15, 16 * c + 16)
+            e = 16 * c + 16
+            ts(R("CMP", 192 * c, 192 * c + e), R("SC", 0, e), k, None, A.is_le)
+            if e < 192:
+                ts(R("CMP", 192 * c + e, 192 * c + 192), R("SC", e, 192), k, None, A.is_lt)
+            total(x("CNT", c, c + 1), R("CMP", 192 * c, 192 * c + 192), 192)
+            if c < len(others):
+                others[c]()
+        tt(R("EQR", 0, 192), R("Z", 0, 192), R("SC", 0, 192), A.is_equal)
+
+    def ranks_end():
+        tt(x("RK", 0, 12), x("CNT", 0, 12), own("YS"), A.subtract)
+        cp(x("RKU", 0, 12), x("RK", 0, 12))
+
+    ranks()
+    cp(x("HUA", 0, 12), x("M17", 0, 12))
+    scan(R("YS", 0, 192), RST(192), R("EQR", 0, 192))
+    ts(x("PHI", 0, 1), x("PI", 0, 1), 4, 1, A.arith_shift_right, A.bitwise_and)
+    ts(x("I2", 0, 1), x("SI", 0, 1), 12, None, A.bitwise_and)
+    cp(x("PH", 0, 1), x("PHI", 0, 1))
+    cp(x("XL", 0, 1), x("I2", 0, 1))
+    ts(x("XL", 1, 2), x("I2", 0, 1), 4.0, None, A.add)
+    ts(x("AL", 0, 1), x("I2", 0, 1), 3.0, None, A.add)
+    ts(x("GM", 0, 32), x("GM", 0, 32), x("PH", 0, 1), None, A.is_equal)
+    ranks_end()
+    cp(R("SEQS", 0, 192, 1, x("RKU", 0, 12)), R("IOTA", 0, 192))
+    tt(R("TMY", 0, 256), R("SEQS", 0, 208, 1, x("QVA")), MASK(256), A.mult)
+    scan(R("YS", 0, 256), RST(256), R("TMY", 0, 256))
+    for t in range(4):
+        ts(R("OFF", 16 * t, 16 * t + 16), own("YS", 256), 4.0, float(t), A.mult, A.add)
+    for t in range(4):
+        o, a = R("FA", t, W64, 4), R("XT", 0, 784, 1, R("OFF", 16 * t, 16 * t + 16))
+        if t < 2:
+            act(o, a)
+        else:
+            cp(o, a)
+
+    F, Fn = "FA", "FB"
+    HR, HRn = "HRA", "HRB"
+    HU, HUn = "HUA", "HUB"
+    QV, QVn = "QVA", "QVB"
+    KA, KAn = "KA", "KB"
+
+    def scalar_constants():
+        for n in range(4):
+            act(R("TP%d" % n, 512, 528), R("ZERO", 0, 16))
+        act(x("RST4"), x("C1C"), SIGN)
+        act(x("C1C", 16, 32), x("C1C", 16, 32), COPY, 0.25)
+        act(x("C1C", 0, 16), x("C1C", 0, 16), IDENT, -0.25, 1.0)
+        act(x("C257"), x("IW"), IDENT, -1.0 / BIG, -257.0 / BIG)
+        act(x("JW1", 0, 4), x("IW", 0, 4), IDENT, 1.0, 1.0)
+        act(x("S16", 0, 1), s, COPY, 1.0 / 16)
+        act(x("S161", 0, 1), s, IDENT, 1.0 / 16, 1.0 / 16)
+        act(x("D0A", 0, 32), x("PAR", 0, 32), COPY, x("S16", 0, 1))
+        act(x("D0B", 0, 32), x("PAR", 0, 32), COPY, x("S161", 0, 1))
+        act(x("C64I", 1, 32, 2), x("IW"), IDENT, 1.0, 64.0)
+        act(x("HBB", 0, 1), s, IDENT, 12.0 * BIG, 11.5 * BIG)
+
+    keys = [lambda: cp(R("KA", 0, 192, 1, x("RKU", 0, 12)), R("SC", 0, 192))]
+
+    for r in range(ROUNDS):
+        last = r == ROUNDS - 1
+        qt, qts, lq, ls, lw, lp = ["%s%d" % (n, r) for n in ("QT", "QTS", "LQ", "LS", "LW", "LP")]
+        quant("QF", "QFS", F, 256)
+        for b in range(4):
+            mm("PS%d" % b, "WQ", "WS", "QF", "QFS", 256, 128 * b)
+        for b in range(4):
+            if b < 2:
+                ts(R("G%d" % b, 0, 256), R(F, b, W64, 4), 64.0, None, A.mult)
+            else:
+                act(R("G%d" % b, 0, 256), R(F, b, W64, 4), COPY, 64.0)
+        for b in range(4):
+            tt(R("AD%d" % b, 0, 256), R("PS%d" % b, 0, 256), R("G%d" % b, 0, 256), A.add)
+            if b < 2:
+                act(R("TI", b, W64, 4), R("AD%d" % b, 0, 256), COPY, 0.015625)
+        for b in (2, 3):
+            ts(R("TI", b, W64, 4), R("AD%d" % b, 0, 256), 0.015625, None, A.mult)
+
+        def plane(b):
+            act(R("TP%d" % b, 0, 256), R("AD%d" % b, 0, 256), COPY, 0.015625)
+
+        def unpack(b):
+            mm("PD%d" % (b % 2), "EQ%d" % b, "EQS%d" % b, lq, ls)
+            act(R("TP%d" % b, 256, 512), R("PD%d" % (b % 2), 0, 256))
+
+        quant(qt, qts, "TI", 256)
+        mm("PP", "UR", "URS", qt, qts)
+        send_codes(lq, ls, qt, qts, 256, "aq%d" % r)
+        keys[0]()
+        dma_fold("KW", KA, 192, "fk")
+        if r > 0:
+            cp(x(HU, 0, 12), x("HW", 0, 12))
+        plane(0)
+        plane(1)
+        act(R("PR", 0, 256), R("PP", 0, 256))
+        hu = x(HU, 0, 12)
+        tt(R("TMP", 0, 192), R("PR", 0, 256, 1, hu), R("DMASK", 0, 192), A.min)
+        act(R("SC", 0, 192), R("PR", 0, 256, 1, hu))
+        plane(2)
+        plane(3)
+        ranks(keys[1:])
+        scan(R("YS", 0, 192), RST(192), R("EQR", 0, 192))
+        act(R("FLB", 0, 256), R("ZERO", 0, 256))
+        if r == 0:
+            scalar_constants()
+            for b in range(4):
+                quant("EQ%d" % b, "EQS%d" % b, "E%d" % b, 128)
+        act(R("LBM", 0, 192), R("IOTA", 0, 192), IDENT, -BIG, x("HBB", 0, 1))
+        mm("PQ", "UP", "UPS", lq, ls)
+        act(R("PPR", 0, 256), R("PQ", 0, 256))
+        unpack(0)
+        unpack(1)
+        ranks_end()
+        cp(R("LROW", 0, 192, 1, x("RKU", 0, 12)), R(HR, 0, 192))
+        ts(x("LFN", 0, 12), x("RK", 0, 12), 63.5, -BIG, A.is_lt, A.mult)
+        tt(R("TMP", 0, 64), R("LROW", 0, 64), MASK(64), A.mult)
+        tt(x("LF3", 0, 12), x("LFN", 0, 12), x("C257", 0, 12), A.mult)
+        scan(R("LL", 0, 64), RST(64), R("TMP", 0, 64))
+        cp(R(lw, 0, 4), own("LL", 64))
+        send(R(lp, 0, 4), R(lw, 0, 4), "al%d" % r)
+        cp(R("FLB", 0, 256, 1, R(lw, 0, 4)), R("BIGS", 0, 64))
+        act(R("SF", 0, 192), R("FLB", 0, 256, 1, hu), IDENT, -1.0 / BIG, 1.0)
+        act(R("SFP", 0, 256), R("FLB", 0, 256), IDENT, -1.0 / BIG, 1.0)
+        tt(R("KST", 0, 192), R("FLB", 0, 256, 1, hu), R(KA, 0, 192), A.add)
+        unpack(2)
+        unpack(3)
+        tt(R("LBK", 0, 192), R("LBM", 0, 192), R("KST", 0, 192), A.max)
+        scan(R("CCS", 0, 192), R("ONE", 0, 192), R("SF", 0, 192))
+        red(x("LB", 0, 1), R("LBK", 0, 192), A.min)
+        tt(R("XC", 0, 192), R("CCS", 0, 192), R("SF", 0, 192), A.mult)
+        dma_fold("XCW", "XC", 192, "fx")
+        scan(R("CSP", 0, 256), R("ONE", 0, 256), R("SFP", 0, 256))
+        tt(R("TMY", 0, 256), R("XC", 0, 208, 1, x(QV)), MASK(256), A.mult)
+        tt(x("CSMB", 1, 17), own("CSP", 256), x("HBP"), A.add)
+        scan(R("XWS", 0, 256), RST(256), R("TMY", 0, 256))
+        tt(x("NCM"), x("CSMB"), x("CSMB", 1, 17), A.subtract)
+        tt(x("KWB", 0, 12), x("KW", 0, 12), x("LFN", 0, 12), A.add)
+        if last:
+            quant("QVC", "QVS", "VT", 128)
+        lpo = R(lp, 0, 4)
+        arr = R(KA, 192, 256)
+        act(arr, R("PPR", 0, 256, 1, lpo))
+        act(x("TH"), x("NCM"), RELU, 1.0, 14.0)
+        tt(R("TMP", 0, 64), R("PPR", 0, 256, 1, lpo), MASK(64), A.mult)
+        ts(R("ARC", 0, 64), arr, x("LB", 0, 1), None, A.is_lt)
+        scan(R("AOS", 0, 64), RST(64), R("TMP", 0, 64))
+        red(x("AR1", 0, 1), R("ARC", 0, 64), A.add)
+
+        def cmp_stay(c):
+            ts(R("CMN", 192 * c, 192 * c + 192), R("KST", 0, 192), R("AOS", 16 * c + 15, 16 * c + 16), None, A.is_le)
+            total(x("TT", 12 + c, 13 + c), R("CMN", 192 * c, 192 * c + 192), 192)
+
+        def cmp_arr(c):
+            q = R("CMQ", 64 * c, 64 * c + 64)
+            if c >= 12 - ON_SCALAR:
+                act(q, arr, RELU, -1.0, x("KWB", c, c + 1))
+                total(x("AC0", c, c + 1), q, 64, SIGN)
+            else:
+                ts(q, arr, x("KWB", c, c + 1), None, A.is_lt)
+                total(x("AC0", c, c + 1), q, 64)
+
+        compares = [lambda c=c: cmp_stay(c) for c in range(4)] + [lambda c=c: cmp_arr(c) for c in range(12)]
+        sel = R("S4", 0, 16, 1, x("AL", 0, 1))
+        tu = x("TU")
+        windows = [
+            lambda: ts(x("B32", 0, 32), x("GM", 0, 32), x("AR1", 0, 1), None, A.mult),
+            lambda: turn(x("B32T", 0, 32), x("B32", 0, 32)),
+            lambda: tt(x("ARB", 1, 17), x("B32T", 0, 16), x("B32T", 16, 32), A.add),
+            lambda: tt(x("EB", 0, 17), x("ARB", 0, 17), x("CSMB", 0, 17), A.add),
+            lambda: tt(x("AX"), x("ARB", 1, 17), x("ARB", 0, 16), A.subtract),
+            lambda: tt(x("X2", 0, 32), R("EB", 0, 24, 1, x("XL", 0, 2)), x("C1C", 0, 32), A.mult),
+            lambda: tt(x("BA"), x("AX"), x("TH"), A.is_gt),
+            lambda: tt(x("CN4", 0, 4), x("EB", 4, 17, 4), x("EB", 0, 13, 4), A.subtract),
+            lambda: tt(x("E64"), x("X2", 0, 16), x("X2", 16, 32), A.add),
+            lambda: scan(x("S4"), x("RST4"), x("BA"), A.mult, A.max),
+            lambda: ts(x("BAD4", 0, 4), x("CN4", 0, 4), 52.5, None, A.is_gt),
+            lambda: tt(x("EQD"), x("E64"), x("EB", 0, 16), A.subtract),
+            lambda: tt(x("ZX4", 0, 4), x("BAD4", 0, 4), x("S4", 3, 16, 4), A.mult),
+            lambda: act(x("XM"), own("XWS", 256), IDENT, 1.0, -193.0),
+            lambda: act(x("XV"), own("XWS", 256), SIGN),
+            lambda: tt(x("EP1"), sel, x("EQD"), A.mult),
+            lambda: tt(x("NI"), sel, x("AX"), A.add),
+            lambda: red(x("S256", 0, 1), x("ZX4", 0, 4), A.max),
+            lambda: tt(x("EP1"), x("EP1"), x("EB", 0, 16), A.add),
+            lambda: ts(x("I0", 1, 32, 2), x("NI"), x("S256", 0, 1), 0.0, A.add, A.is_equal),
+            lambda: tt(x("CE3"), x("C12"), x("EP1"), A.subtract),
+            lambda: tt(x("ENI"), x("ARB", 0, 16), x("XM"), A.add),
+            lambda: ts(x("EP3"), x("CE3"), x("S256", 0, 1), None, A.mult),
+            lambda: tt(x("EN2"), x("ENI"), x("XV"), A.mult),
+            lambda: tt(x("D1", 1, 33, 2), x("EP1"), x("EP3"), A.add),
+            lambda: tt(x("TB", 0, 12), x("XCW", 0, 12), x("LF3", 0, 12), A.add),
+            lambda: tt(x("D1", 0, 32, 2), x("D1", 3, 35, 2), x("D1", 1, 33, 2), A.subtract),
+            lambda: tt(x("TT", 12, 16), x("JW1", 0, 4), x("TT", 12, 16), A.add),
+            lambda: scan(x("UA", 0, 32), x("D0A", 0, 32), x("D1", 0, 32)),
+            lambda: scan(x("UB", 0, 32), x("D0B", 0, 32), x("D1", 0, 32)),
+            lambda: ts(x("QI"), x("UA", 1, 32, 2), UP_, None, A.add),
+            lambda: tt(x("TT", 0, 12), x("TB", 0, 12), x("AC0", 0, 12), A.add),
+            lambda: tt(x("VL"), x("UB", 1, 32, 2), x("QI"), A.is_gt),
+            lambda: ts(tu, x("TT"), -1.0, None, A.add),
+            lambda: tt(x("I1", 1, 32, 2), x("VL"), x("QI"), A.mult),
+            lambda: cp(R("SEQ", 0, 448, 1, tu), R(HR, 0, 256)),
+            lambda: tt(x("I1", 0, 32, 2), x("EN2"), x("I1", 1, 32, 2), A.subtract),
+            lambda: scan(x("UX", 0, 32), x("I0", 0, 32), x("I1", 0, 32)),
+            lambda: ts(x(QVn), x("UX", 1, 32, 2), 192.0, None, A.add),
+        ]
+        act(R(HR, 192, 256), R("IOTA", 256, 512, 1, lpo))
+        while compares or windows:
+            if windows:
+                windows.pop(0)()
+            if compares:
+                compares.pop(0)()
+        if last:
+            act(R("HROL", 0, 192), R(HR, 0, 192))
+            act(R("HROL", 192, 256), R("IOTA", 256, 320))
+        else:
+            ts(x("UX", 0, 32, 2), x("UX", 1, 32, 2), 0.0, None, A.is_equal)
+        tt(R("TMY", 0, 256), R("SEQ", 0, 208, 1, x(QVn)), MASK(256), A.mult)
+        if not last:
+            scan(x("UY", 0, 32), x("C64I", 0, 32), x("UX", 0, 32))
+        scan(R("YS", 0, 256), RST(256), R("TMY", 0, 256))
+        if not last:
+            ts(x("QDU"), x("UY", 1, 32, 2), 192.0, None, A.add)
+        cp(x("OFY"), own("YS", 256))
+        for t in range(3):
+            act(R(Fn, t, W64, 4), R("TP%d" % t, 0, 528, 1, x("OFY")))
+        if not last:
+            cp(R(HRn, 0, 512, 1, x("QDU")), R("IOTA", 0, 256))
+            dma_fold("HW", HRn, 192, "fh")
+        cp(R(Fn, 3, W64, 4), R("TP3", 0, 528, 1, x("OFY")))
+        keys = [
+            lambda KA=KA, KAn=KAn: cp(R(KAn, 0, 448, 1, x("TU")), R(KA, 0, 256)),
+            lambda: ts(x("HBI"), x("D1", 3, 35, 2), UP_, None, A.add),
+            lambda: tt(x("HBP"), x("HBI"), x("C16"), A.subtract),
+            lambda: tt(x("M17"), x("HBI"), MASK(16), A.mult),
+            lambda: red(x("HB1", 0, 1), x("M17"), A.add),
+            lambda: ts(x("HBB", 0, 1), x("HB1", 0, 1), 191.5, BIG, A.add, A.mult),
+        ]
+        F, Fn, HR, HRn, HU, HUn, QV, QVn, KA, KAn = Fn, F, HRn, HR, HUn, HU, QVn, QV, KAn, KA
+
+    stored = [0]
+
+    def store(q, dst, a, src):
+        stored[0] += 1
+        emit(q, lambda: Q[q].dma_start(dst, src), [], [a], ("dout", 16 * stored[0], 16))
+
+    cp(R("SEQO", 0, 448, 1, x("TU")), R("HROL", 0, 256))
+    quant("QF", "QFS", F, 256)
+    mm("PP", "QVC", "QVS", "QF", "QFS")
+    cp(R("OLR", 0, 256), R("SEQO", 0, 208, 1, x(QV)))
+    act(R("YO", 0, 256), R("PP", 0, 256))
+    qf = R("QF", 0, 256, 1, None, dt.uint8)
+    store("y", T.oc[:, 0:W64], qf, ap(qf))
+    for k in range(4):
+        store("y", T.osc[4 * k:4 * k + 4, 0:256], R("QFS", 0, 256), T.QFS[32 * k:32 * k + 4, 0:256])
+    store("s", T.y[:, 0:256], R("YO", 0, 256), ap(R("YO", 0, 256)))
+    store("y", T.ol[:, 0:256], R("OLR", 0, 256), T.OLR[0:128:16, 0:256])
+
+    for q in ("v", "s", "t", "g"):
+        if known["g"].get(q, 0) < cnt[q]:
+            g.wait_ge(T.sem[sem_of[q]], cnt[q])
+    for n in ("dx", "du", "dw", "dws", "dv"):
+        g.wait_ge(T.sem[n], 16)
+    for n in ("fk", "fx", "fh"):
+        g.wait_ge(T.sem[n], folded[n])
+    g.wait_ge(T.sem["dout"], 16 * stored[0])
+    g.wait_ge(T.sem["loc"], sent[0])
+    g.wait_ge(T.sem["au"], 2 * engines)
+    for r in range(ROUNDS):
+        g.wait_ge(T.sem["aq%d" % r], 2 * engines)
+        g.wait_ge(T.sem["al%d" % r], engines)

@@ -1,3 +1,4 @@
+import math
 from concourse.mybir import dt, AluOpType, AxisListType, ActivationFunctionType
 
 A = AluOpType
@@ -9,7 +10,8 @@ BIG = 2.0 ** 96
 ROUNDS = 3
 W64 = 4 * 256
 UP_ = 0.5 - 1.0 / 512
-ON_SCALAR = 3
+WHOLE = 1.5 * 2.0 ** 23
+ON_SCALAR = 10
 
 SCRATCH = {}
 
@@ -20,14 +22,14 @@ def _decl(names, where, shape, dtype):
 
 
 _decl("XT", "sbuf", [128, 832], "bfloat16")
-_decl("UT VT E0 E1 E2 E3 ONEB", "sbuf", [128, 512], "bfloat16")
-_decl("TI FA FB", "sbuf", [128, 1024], "bfloat16")
-_decl("TP0 TP1 TP2 TP3", "sbuf", [128, 528], "bfloat16")
-_decl("AD0 AD1 AD2 AD3 G0 G1 G2 G3", "sbuf", [128, 256], "bfloat16")
+_decl("UT VT", "sbuf", [128, 512], "bfloat16")
+_decl("EA EB ONEB AD0 AD1 AD2 AD3", "sbuf", [128, 528], "bfloat16")
+_decl("TI FA FB GI", "sbuf", [128, 1024], "bfloat16")
 _decl("CMP", "sbuf", [128, 2304], "bfloat16")
-_decl("JNK", "sbuf", [128, 1536], "bfloat16")
-_decl("CMQ", "sbuf", [128, 768], "float32")
-_decl("CMN", "sbuf", [128, 768], "bfloat16")
+_decl("JNK", "sbuf", [128, 8 * 272], "bfloat16")
+_decl("CMN", "sbuf", [128, 4 * 272], "bfloat16")
+_decl("RST SFP C75 EQR YB TMB", "sbuf", [128, 256], "bfloat16")
+_decl("CSP", "sbuf", [128, 272], "bfloat16")
 _decl("QX", "sbuf", [128, 192], "float8_e4m3fn_x4")
 _decl("QXS", "sbuf", [128, 192], "uint8")
 _decl("QU QVC UR UP EQ0 EQ1 EQ2 EQ3", "sbuf", [128, 128], "float8_e4m3fn_x4")
@@ -37,27 +39,29 @@ _decl("WS", "sbuf", [128, 512], "uint8")
 _decl("QF QT0 QT1 QT2 LQ0 LQ1 LQ2", "sbuf", [128, 256], "float8_e4m3fn_x4")
 _decl("QFS QTS0 QTS1 QTS2 LS0 LS1 LS2", "sbuf", [128, 256], "uint8")
 _decl("PS0 PS1 PS2 PS3 PP PQ PD0 PD1", "psum", [128, 512], "float32")
-_decl("IOTA HRA HRB", "sbuf", [128, 512], "float32")
-_decl("JM MASK DMASK RST RMIN ONE ZERO TMP TMY YS PR PPR FLB SFP CSP XWS OLR HROL YO", "sbuf", [128, 256], "float32")
-_decl("KA KB SEQ SEQO", "sbuf", [128, 448], "float32")
-_decl("SEQS XC", "sbuf", [128, 208], "float32")
-_decl("SC Z EQR LROW SF CCS KST LBM LBK", "sbuf", [128, 192], "float32")
-_decl("ARR64", "sbuf", [128, 256], "float32")
-_decl("KW XCW HW", "sbuf", [128, 16], "float32")
-SMALL = ("EB D1 ARB CSMB GM B32 B32T X2 PAR C1C D0A D0B UA UB I0 I1 UX C64I UY C12 RST4 C16 IW C257 M16 M17 CNT RK LFN KWB "
-         "LF3 TB XM XV NCM TH HBP AX BA S4 E64 EQD EP1 CE3 EP3 VL NI ENI EN2 TT JW1 KI0 ENC INV AC0 SP PH LB AR1 S256 HBB HB1 "
-         "S16 S161 CN4 BAD4 ZX4").split()
-_decl("SMALLS", "sbuf", [128, 40 * len(SMALL)], "float32")
-_decl("INTS", "sbuf", [128, 16 * 11], "int32")
+_decl("IOTA", "sbuf", [128, 512], "float32")
+_decl("KA KB OLT", "sbuf", [128, 528], "float32")
+_decl("SRC SEQ HR O2", "sbuf", [128, 640], "float32")
+_decl("JM MASK DMASK RMIN TRIW LBM LBK TMP TMY YS PR XWS OLR YO", "sbuf", [128, 256], "float32")
+_decl("SEQS SC", "sbuf", [128, 208], "float32")
+_decl("Z LROW KST", "sbuf", [128, 192], "float32")
+_decl("CF", "sbuf", [128, 256], "float32")
+_decl("ARS", "sbuf", [128, 64], "float32")
+_decl("C8 X8 S2A", "sbuf", [128, 128], "float32")
+_decl("O1 S3A O3", "sbuf", [128, 80], "float32")
+_decl("LL AOS ARC BIGS NR C4 X4 S1A J64", "sbuf", [128, 64], "float32")
+SMALL = ("RB C1C C12 IW M16 M17 CNT RK KI0 ENC INV EN2 SP AR1 RST4 CN S4 CN4 ZX ZM C45 HC WT TB CT AX NI TTA AC C2I TTS IW5 "
+         "S16 S161 N16 N161 CA CB PA PB PC PD C4C C8C LB0 OFS").split()
+_decl("SMALLS", "sbuf", [128, 32 * len(SMALL)], "float32")
+_decl("INTS", "sbuf", [128, 16 * 10], "int32")
 _decl("LW0 LW1 LW2 LP0 LP1 LP2", "sbuf", [128, 4], "uint16")
 _decl("LISTS", "sbuf", [128, 16 * 12], "uint16")
 _decl("OFF", "sbuf", [128, 64], "uint16")
-PIECE = {n: ("SMALLS", 40 * i) for i, n in enumerate(SMALL)}
-PIECE.update({n: ("INTS", 16 * i) for i, n in enumerate("PI SI PHI I2 KI KA4 KB4 UI QI HBI H3".split())})
-PIECE.update({n: ("LISTS", 16 * i) for i, n in enumerate("RKU HUA HUB QVA QVB QDU TU XL AL UL OFY".split())})
-PIECE.update({n: ("ARR64", 64 * i) for i, n in enumerate("LL AOS ARC BIGS".split())})
+PIECE = {n: ("SMALLS", 32 * i) for i, n in enumerate(SMALL)}
+PIECE.update({n: ("INTS", 16 * i) for i, n in enumerate("PI SI I2 I3 I4 I8 KI KA4 KB4 UI".split())})
+PIECE.update({n: ("LISTS", 16 * i) for i, n in enumerate("RKU HU QV0 QD TU TBU AL UL OFY AU L4 L8".split())})
 
-SEMAPHORES = ["sv", "ss", "st", "sg", "dx", "du", "dw", "dws", "dv", "dout", "loc", "au", "fk", "fx", "fh",
+SEMAPHORES = ["sv", "ss", "st", "sg", "dx", "du", "dw", "dws", "dv", "dout", "loc", "au",
               "aq0", "aq1", "aq2", "al0", "al1", "al2"]
 
 
@@ -91,7 +95,7 @@ def rank_program(g, core, T, topo):
     def meet(h, r):
         if h[0] >= r[2] or r[1] >= h[1]:
             return False
-        return not (h[2] > 1 and h[2] == r[3] and (h[0] - r[1]) % h[2])
+        return (h[0] - r[1]) % math.gcd(h[2], r[3]) == 0
 
     def wait(q, src, val):
         if known[q].get(src, 0) >= val:
@@ -173,11 +177,8 @@ def rank_program(g, core, T, topo):
     def fill(o, c):
         emit("v", lambda: g.vector.memset(ap(o), c), [o], [])
 
-    def turn(o, a):
-        emit("v", lambda: g.vector.transpose(ap(o), ap(a)), [o], [a])
-
-    def quant(o, s, a, n):
-        o, s, a = R(o, 0, n), R(s, 0, n), R(a, 0, 4 * n)
+    def quant(o, s, a, n, at=0):
+        o, s, a = R(o, 0, n), R(s, 0, n), R(a, at, at + 4 * n)
         emit("v", lambda: g.vector.quantize_mx(ap(o), ap(s), ap(a)), [o, s], [a])
 
     def act(o, a, func=COPY, scale=1.0, bias=0.0):
@@ -191,10 +192,13 @@ def rank_program(g, core, T, topo):
 
     turns = [0]
 
-    def total(o, a, n, func=COPY):
-        j = R("JNK", 192 * (turns[0] % 8), 192 * (turns[0] % 8) + n)
+    def total(o, a, n, bias=None):
+        j = R("JNK", 272 * (turns[0] % 8), 272 * (turns[0] % 8) + n)
         turns[0] += 1
-        emit("s", lambda: g.scalar.activation(ap(j), ap(a), func, accum_out=ap(o)), [j, o], [a])
+        if bias is None:
+            emit("s", lambda: g.scalar.activation(ap(j), ap(a), COPY, accum_out=ap(o)), [j, o], [a])
+        else:
+            emit("s", lambda: g.scalar.activation(ap(j), ap(a), SIGN, bias=ap(bias), scale=-1.0, accum_out=ap(o)), [j, o], [a, bias])
 
     def mm(o, l, ls, r, rs, n=256, c=0):
         o, l, ls, r, rs = R(o, 0, n), R(l, c, c + 128), R(ls, c, c + 128), R(r, 0, n), R(rs, 0, n)
@@ -208,14 +212,6 @@ def rank_program(g, core, T, topo):
 
     def load(q, o, src, sem):
         emit(q, lambda: Q[q].dma_start(ap(o), src), [o], [], (sem, 16, 16))
-
-    folded = {n: 0 for n in ("fk", "fx", "fh")}
-
-    def dma_fold(o, a, n, sem):
-        folded[sem] += n
-        for c in range(n // 16):
-            src = T[a][0:128:16, 16 * c:16 * c + 16]
-            emit("y", lambda: g.sync.dma_start(ap(R(o, c, c + 1)), src), [R(o, c, c + 1)], [R(a, 16 * c, 16 * c + 16)], (sem, folded[sem], 16))
 
     sent = [0]
     engines = len(topo.engines(core, nxt))
@@ -244,78 +240,144 @@ def rank_program(g, core, T, topo):
     load("y", R("XT", 0, 768), T.x[:], "dx")
     load("s", R("UT", 0, 512), T.u[:], "du")
     load("y", R("WQ", 0, 512, 1, None, dt.uint8), T.wc[:], "dw")
-    load("s", R("WS", 0, 512), T.ws[:], "dws")
+    load("y", R("WS", 0, 512), T.ws[:], "dws")
     load("y", R("VT", 0, 512), T.v[:], "dv")
 
     x = R
-    iota(R("JM", 0, 256), [[0, 16], [1, 16]])
-    iota(x("PI", 0, 1), [[1, 1]], 0, 1)
-    iota(x("UI", 0, 8), [[16, 8]])
-    iota(x("M16"), [[16, 16]])
-    iota(R("IOTA", 0, 512), [[1, 512]])
-    iota(R("HRA", 0, 192), [[4, 64], [1, 3]])
-    iota(x("GM", 0, 32), [[1, 2], [0, 16]])
-    iota(x("PAR", 0, 32), [[0, 16], [1, 2]])
-    iota(x("C1C", 0, 32), [[0, 8], [1, 4]])
-    iota(x("C12"), [[12, 16]], -192)
-    iota(x("C16"), [[16, 16]], 16)
-    iota(x("HBP"), [[-4, 16]], -4 - 192)
-    iota(R("SEQ", 192, 208), [[0, 16]], 512)
-    iota(R("SEQO", 192, 208), [[0, 16]], -1)
-    iota(R("XC", 192, 208), [[0, 16]])
-    iota(x("CSMB", 0, 8), [[0, 8]], -192)
-    for n in ("ARB", "D1", "I0", "EB", "C64I"):
-        iota(x(n, 0, 40), [[0, 40]])
-    iota(R("ONE", 0, 256), [[0, 256]], 1)
-    iota(R("ZERO", 0, 256), [[0, 256]])
-    fill(R("ONEB", 0, 512), 1.0)
-
-    def unit(b):
-        o = R("E%d" % b, 0, 512)
-        emit("g", lambda: g.affine_select(ap(o), ap(R("ONEB", 0, 512)), [[-1, 512]], A.is_equal, 0.0, b, 4), [o], [R("ONEB", 0, 512)])
-
-    for b in range(4):
-        unit(b)
-
-    ts(R("RST", 0, 256), R("JM", 0, 256), 0.0, None, A.not_equal)
-    ts(x("SI", 0, 1), x("PI", 0, 1), 15, None, A.bitwise_and)
-    cp(x("UL", 0, 8), x("UI", 0, 8))
-    cp(x("SP", 0, 1), x("SI", 0, 1))
-    s = x("SP", 0, 1)
-    ts(R("RMIN", 0, 192), R("RST", 0, 192), 2 * BIG, -BIG, A.mult, A.add)
-    ts(R("MASK", 0, 256), R("JM", 0, 256), s, None, A.is_equal)
-    fill(R("SEQS", 192, 208), 192.0)
-    ts(R("DMASK", 0, 192), R("MASK", 0, 192), 2 * BIG, -BIG, A.mult, A.add)
-    fill(R("BIGS", 0, 64), BIG)
-
+    ONE = lambda n: R("ONEB", 0, n)
     MASK = lambda n: R("MASK", 0, n)
     RST = lambda n: R("RST", 0, n)
+    IOTA = lambda a, b, off=None: R("IOTA", a, b, 1, off)
 
     def own(o, n=192):
         return R(o, 15, n, 16)
 
+    def const(o, n, c):
+        iota(R(o, *n), [[0, n[1] - n[0]]], c)
+
+    iota(x("PI", 0, 1), [[1, 1]], 0, 1)
+    iota(R("JM", 0, 256), [[0, 16], [1, 16]])
+    iota(x("UI", 0, 8), [[16, 8]])
+    iota(x("M16"), [[16, 16]])
+    iota(x("C12"), [[12, 16]])
+    fill(ONE(528), 1.0)
+    for n, b in (("EA", 2), ("EB", 3)):
+        o = R(n, 0, 516)
+        emit("g", lambda: g.affine_select(ap(o), ap(ONE(516)), [[-1, 516]], A.is_equal, 0.0, b, 4), [o], [ONE(516)])
+    iota(R("HR", 0, 192), [[4, 64], [1, 3]])
+    iota(x("C1C"), [[0, 4], [1, 4]])
+    iota(x("C4C", 0, 4), [[4, 4]])
+    iota(x("C8C", 0, 8), [[8, 8]])
+    iota(x("CT"), [[28, 16]], 192)
+    iota(R("S1A", 0, 64), [[0, 16], [1, 4]])
+    iota(R("S2A", 0, 128), [[0, 64], [1, 2]])
+    iota(R("J64", 0, 64), [[1, 64]])
+    const("S3A", (0, 80), 0)
+    const("RB", (0, 24), 0)
+    const("O1", (64, 68), 0)
+    const("O1", (68, 72), 1)
+    const("C4", (0, 64), 1)
+    const("CSP", (0, 16), 0)
+    for b in range(4):
+        const("AD%d" % b, (512, 528), 0)
+
+    scan(IOTA(0, 512), ONE(512), ONE(512), A.mult, A.add, -1.0)
+    ts(x("SI", 0, 1), x("PI", 0, 1), 15, None, A.bitwise_and)
+    ts(RST(256), R("JM", 0, 256), 0.0, None, A.not_equal)
+    cp(x("SP", 0, 1), x("SI", 0, 1))
+    s = x("SP", 0, 1)
+    cp(x("UL", 0, 8), x("UI", 0, 8))
+    ts(MASK(256), R("JM", 0, 256), s, None, A.is_equal)
     act(x("IW"), x("M16"), IDENT, 1.0, s)
-    quant("QU", "QUS", "UT", 128)
-    quant("QX", "QXS", "XT", 192)
-    cp(R("UR", 0, 128, 1, None, dt.uint32), R("QU", 0, 128, 1, R("UL", 0, 8), dt.uint32))
-    cp(R("URS", 0, 128), R("QUS", 0, 128, 1, R("UL", 0, 8)))
-    mm("PP", "UR", "URS", "QX", "QXS", 192)
-    send_codes("UP", "UPS", "UR", "URS", 128, "au")
-    act(R("SC", 0, 192), R("PP", 0, 192))
+    act(R("RMIN", 0, 192), RST(192), IDENT, 2 * BIG, -BIG)
+    act(R("DMASK", 0, 192), MASK(192), IDENT, 2 * BIG, -BIG)
+    ts(R("TRIW", 0, 256), R("JM", 0, 256), s, None, A.is_lt)
+    tt(R("TMY", 0, 256), MASK(256), IOTA(192, 448), A.mult)
     cp(x("KI"), x("IW"))
     fill(R("XT", 768, 832), 0.0)
     ts(x("KA4"), x("KI"), 2, None, A.arith_shift_right)
     ts(x("KB4"), x("KI"), 3, None, A.bitwise_and)
+    tt(R("TRIW", 0, 256), R("TRIW", 0, 256), R("TMY", 0, 256), A.subtract)
+
+    def tables_a():
+        act(x("LB0", 0, 1), s, IDENT, 16.0, 15.5)
+        act(x("S16", 0, 1), s, COPY, 1.0 / 16)
+        act(x("N16", 0, 1), s, IDENT, -1.0 / 16, 1.0)
+        act(x("S161", 0, 1), s, IDENT, 1.0 / 16, 1.0 / 16)
+        act(x("N161", 0, 1), s, IDENT, -1.0 / 16, 15.0 / 16)
+        act(x("CA", 0, 1), s, IDENT, 0.75, UP_)
+        act(x("CB", 0, 1), s, IDENT, 0.75, 0.75 + UP_)
+        act(R("LBM", 0, 256), IOTA(0, 256), SIGN, -1.0, x("LB0", 0, 1))
+        act(R("SC", 192, 208), ONE(16), COPY, BIG)
+
+    def tables_b():
+        for i, n in ((0, "S16"), (1, "N16"), (4, "S161"), (5, "N161")):
+            act(R("C8", i, 128, 8), ONE(16), COPY, x(n, 0, 1))
+        act(R("C8", 2, 128, 8), x("C12"), IDENT, 1.0, x("CA", 0, 1))
+        act(R("C8", 6, 128, 8), x("C12"), IDENT, 1.0, x("CB", 0, 1))
+        act(R("C8", 3, 128, 4), ONE(32), COPY, WHOLE)
+        act(R("LBM", 0, 256), R("LBM", 0, 256), COPY, BIG)
+
+    def tables_c():
+        act(R("BIGS", 0, 64), ONE(64), COPY, BIG)
+        act(R("C75", 0, 256), ONE(256), COPY, -0.75)
+        for n in ("KA", "KB"):
+            act(R(n, 512, 528), ONE(16), COPY, BIG)
+        act(R("CMN", 192, 4 * 208, 208), x("IW", 0, 4))
+        act(R("XWS", 0, 256), MASK(256), COPY, -4096.0)
+        act(R("SRC", 0, 1), ONE(1), COPY, 0.0)
+        act(R("SRC", 1, 257), MASK(256), COPY, 1024.0)
+        act(x("IW5", 0, 8), x("IW", 0, 8), IDENT, 1.0, 0.5)
+        act(x("C2I", 0, 8), x("IW", 0, 8), IDENT, 2.0, 64.0)
+        act(x("RST4"), x("C1C"), SIGN)
+
+    def tables_d():
+        act(R("C4", 0, 64, 4), x("C1C"), COPY, 0.25)
+        act(R("C4", 1, 64, 4), x("C1C"), IDENT, -0.25, 1.0)
+        act(R("S1A", 2, 64, 4), ONE(16), COPY, -1.0)
+        act(R("S3A", 2, 80, 5), ONE(16), COPY, -1.0)
+        act(R("O2", 7, 640, 40), x("IW"), IDENT, 1.0, 192.0)
+        act(R("O2", 39, 640, 40), ONE(16))
+        act(x("C45", 0, 32), ONE(32), COPY, -4.5)
+        act(R("SEQ", 192, 640), ONE(448), COPY, 512.0)
+
+    def lists():
+        tt(R("CF", 0, 256), R("XWS", 0, 256), R("SRC", 0, 256), A.add)
+        ts(x("OFS", 0, 1), s, 14.5, -1024.0, A.is_lt, A.mult)
+        ts(x("CT"), x("CT"), s, WHOLE, A.add, A.add)
+        ts(x("I2", 0, 1), x("SI", 0, 1), 12, None, A.bitwise_and)
+        ts(x("I3", 0, 1), x("SI", 0, 1), 3, None, A.bitwise_and)
+        ts(x("I4", 0, 1), x("SI", 0, 1), 2, None, A.arith_shift_right)
+        ts(x("I8", 0, 1), x("SI", 0, 1), 8, None, A.bitwise_and)
+        ts(x("AL", 0, 1), x("I2", 0, 1), 3.0, None, A.add)
+        ts(x("PA", 0, 1), x("I3", 0, 1), 0.0, 4.0, A.is_equal, A.mult)
+        ts(x("PB", 0, 1), x("I3", 0, 1), 1.5, None, A.is_gt)
+        ts(x("PD", 0, 1), x("I3", 0, 1), 1.5, None, A.is_lt)
+        ts(x("PC", 0, 1), x("I8", 0, 1), 0.5, -65.0, A.mult, A.add)
+        ts(x("INV", 0, 1), x("I4", 0, 1), x("PB", 0, 1), x("PA", 0, 1), A.mult, A.add)
+        ts(x("EN2", 0, 8), x("C8C", 0, 8), x("PC", 0, 1), x("PA", 0, 1), A.add, A.add)
+        ts(x("L4", 0, 4), x("C4C", 0, 4), x("INV", 0, 1), None, A.add)
+        ts(x("L8", 0, 8), x("EN2", 0, 8), x("PD", 0, 1), 68.0, A.mult, A.add)
+
+    tables_a()
+    quant("QU", "QUS", "UT", 128)
+    cp(R("UR", 0, 128, 1, None, dt.uint32), R("QU", 0, 128, 1, R("UL", 0, 8), dt.uint32))
+    act(R("URS", 0, 128), R("QUS", 0, 128, 1, R("UL", 0, 8)))
+    quant("QX", "QXS", "XT", 192)
+    mm("PP", "UR", "URS", "QX", "QXS", 192)
+    send_codes("UP", "UPS", "UR", "URS", 128, "au")
+    act(R("SC", 0, 192), R("PP", 0, 192))
+    tables_b()
     ts(x("KI0"), x("KA4"), 3.0, -192.0, A.mult, A.add)
     ts(x("INV"), x("KB4"), 2.5, None, A.is_lt)
     tt(x("ENC"), x("KI0"), x("KB4"), A.add)
-    ts(x("H3"), x("IW"), 1.0 / 3, -1.0 / 3, A.mult, A.add)
+    fill(R("SEQS", 192, 208), 192.0)
     tt(x("EN2"), x("ENC"), x("INV"), A.mult)
-    tt(x("M17"), x("IW"), x("H3"), A.add)
-    ts(x("QVA"), x("EN2"), 192.0, None, A.add)
+    ts(x("KI"), x("IW"), 1.0 / 3, -1.0 / 3, A.mult, A.add)
+    ts(x("QV0"), x("EN2"), 192.0, None, A.add)
     tt(R("TMP", 0, 192), R("SC", 0, 192), R("DMASK", 0, 192), A.min)
 
-    def ranks(others=()):
+    def ranks():
         scan(R("Z", 0, 192), R("RMIN", 0, 192), R("TMP", 0, 192), A.min, A.max, -BIG)
         for c in range(12):
             k = R("Z", 16 * c + 15, 16 * c + 16)
@@ -323,60 +385,47 @@ def rank_program(g, core, T, topo):
             ts(R("CMP", 192 * c, 192 * c + e), R("SC", 0, e), k, None, A.is_le)
             if e < 192:
                 ts(R("CMP", 192 * c + e, 192 * c + 192), R("SC", e, 192), k, None, A.is_lt)
-            total(x("CNT", c, c + 1), R("CMP", 192 * c, 192 * c + 192), 192)
-            if c < len(others):
-                others[c]()
+            if c < ON_SCALAR:
+                total(x("CNT", c, c + 1), R("CMP", 192 * c, 192 * c + 192), 192)
         tt(R("EQR", 0, 192), R("Z", 0, 192), R("SC", 0, 192), A.is_equal)
+        for c in range(ON_SCALAR, 12):
+            red(x("CNT", c, c + 1), R("CMP", 192 * c, 192 * c + 192), A.add)
+            if c == ON_SCALAR:
+                scan(R("YB", 0, 192), RST(192), R("EQR", 0, 192))
 
     def ranks_end():
-        tt(x("RK", 0, 12), x("CNT", 0, 12), own("YS"), A.subtract)
+        tt(x("RK", 0, 12), x("CNT", 0, 12), own("YB"), A.subtract)
         cp(x("RKU", 0, 12), x("RK", 0, 12))
 
+    def fold(o, y, a, n):
+        scan(R(y, 0, n), R("CF", 0, n), R(a, 0, n), A.add, A.max)
+        ts(o, own(y, n), x("OFS", 0, 1), None, A.add)
+
     ranks()
-    cp(x("HUA", 0, 12), x("M17", 0, 12))
-    scan(R("YS", 0, 192), RST(192), R("EQR", 0, 192))
-    ts(x("PHI", 0, 1), x("PI", 0, 1), 4, 1, A.arith_shift_right, A.bitwise_and)
-    ts(x("I2", 0, 1), x("SI", 0, 1), 12, None, A.bitwise_and)
-    cp(x("PH", 0, 1), x("PHI", 0, 1))
-    cp(x("XL", 0, 1), x("I2", 0, 1))
-    ts(x("XL", 1, 2), x("I2", 0, 1), 4.0, None, A.add)
-    ts(x("AL", 0, 1), x("I2", 0, 1), 3.0, None, A.add)
-    ts(x("GM", 0, 32), x("GM", 0, 32), x("PH", 0, 1), None, A.is_equal)
+    tt(x("M17"), x("IW"), x("KI"), A.add)
+    cp(x("HU", 0, 12), x("M17", 0, 12))
     ranks_end()
-    cp(R("SEQS", 0, 192, 1, x("RKU", 0, 12)), R("IOTA", 0, 192))
-    tt(R("TMY", 0, 256), R("SEQS", 0, 208, 1, x("QVA")), MASK(256), A.mult)
-    scan(R("YS", 0, 256), RST(256), R("TMY", 0, 256))
-    for t in range(4):
-        ts(R("OFF", 16 * t, 16 * t + 16), own("YS", 256), 4.0, float(t), A.mult, A.add)
+    tables_c()
+    cp(R("SEQS", 0, 192, 1, x("RKU", 0, 12)), IOTA(0, 192))
+    tt(R("TMB", 0, 256), R("SEQS", 0, 208, 1, x("QV0")), MASK(256), A.mult)
+    scan(R("YB", 0, 256), RST(256), R("TMB", 0, 256))
+    for t in (0, 2, 1, 3):
+        ts(R("OFF", 16 * t, 16 * t + 16), own("YB", 256), 4.0, float(t), A.mult, A.add)
     for t in range(4):
         o, a = R("FA", t, W64, 4), R("XT", 0, 784, 1, R("OFF", 16 * t, 16 * t + 16))
         if t < 2:
             act(o, a)
         else:
             cp(o, a)
+    cp(x("OFY"), own("YB", 256))
 
     F, Fn = "FA", "FB"
-    HR, HRn = "HRA", "HRB"
-    HU, HUn = "HUA", "HUB"
-    QV, QVn = "QVA", "QVB"
-    KA, KAn = "KA", "KB"
-
-    def scalar_constants():
-        for n in range(4):
-            act(R("TP%d" % n, 512, 528), R("ZERO", 0, 16))
-        act(x("RST4"), x("C1C"), SIGN)
-        act(x("C1C", 16, 32), x("C1C", 16, 32), COPY, 0.25)
-        act(x("C1C", 0, 16), x("C1C", 0, 16), IDENT, -0.25, 1.0)
-        act(x("C257"), x("IW"), IDENT, -1.0 / BIG, -257.0 / BIG)
-        act(x("JW1", 0, 4), x("IW", 0, 4), IDENT, 1.0, 1.0)
-        act(x("S16", 0, 1), s, COPY, 1.0 / 16)
-        act(x("S161", 0, 1), s, IDENT, 1.0 / 16, 1.0 / 16)
-        act(x("D0A", 0, 32), x("PAR", 0, 32), COPY, x("S16", 0, 1))
-        act(x("D0B", 0, 32), x("PAR", 0, 32), COPY, x("S161", 0, 1))
-        act(x("C64I", 1, 32, 2), x("IW"), IDENT, 1.0, 64.0)
-        act(x("HBB", 0, 1), s, IDENT, 12.0 * BIG, 11.5 * BIG)
-
-    keys = [lambda: cp(R("KA", 0, 192, 1, x("RKU", 0, 12)), R("SC", 0, 192))]
+    K, Kn = "KA", "KB"
+    keys = R("SC", 0, 208, 1, x("OFY"))
+    hu = x("HU", 0, 12)
+    h0, h1 = R("CSP", 15, 256, 16), R("CSP", 31, 272, 16)
+    r0, r1 = x("RB", 0, 16), x("RB", 1, 17)
+    nsel = R("S1A", 3, 64, 4)
 
     for r in range(ROUNDS):
         last = r == ROUNDS - 1
@@ -384,178 +433,124 @@ def rank_program(g, core, T, topo):
         quant("QF", "QFS", F, 256)
         for b in range(4):
             mm("PS%d" % b, "WQ", "WS", "QF", "QFS", 256, 128 * b)
+        if r == 0:
+            act(R("GI", 0, 384), R(F, 0, 384), COPY, 64.0)
+            ts(R("GI", 384, W64), R(F, 384, W64), 64.0, None, A.mult)
+        else:
+            act(R("GI", 0, W64), R(F, 0, W64), COPY, 64.0)
+            cp(R("HR", 0, 640, 1, x("QD")), IOTA(0, 256))
         for b in range(4):
-            if b < 2:
-                ts(R("G%d" % b, 0, 256), R(F, b, W64, 4), 64.0, None, A.mult)
-            else:
-                act(R("G%d" % b, 0, 256), R(F, b, W64, 4), COPY, 64.0)
-        for b in range(4):
-            tt(R("AD%d" % b, 0, 256), R("PS%d" % b, 0, 256), R("G%d" % b, 0, 256), A.add)
+            tt(R("AD%d" % b, 0, 256), R("PS%d" % b, 0, 256), R("GI", b, W64, 4), A.add)
             if b < 2:
                 act(R("TI", b, W64, 4), R("AD%d" % b, 0, 256), COPY, 0.015625)
         for b in (2, 3):
             ts(R("TI", b, W64, 4), R("AD%d" % b, 0, 256), 0.015625, None, A.mult)
 
-        def plane(b):
-            act(R("TP%d" % b, 0, 256), R("AD%d" % b, 0, 256), COPY, 0.015625)
-
-        def unpack(b):
-            mm("PD%d" % (b % 2), "EQ%d" % b, "EQS%d" % b, lq, ls)
-            act(R("TP%d" % b, 256, 512), R("PD%d" % (b % 2), 0, 256))
-
         quant(qt, qts, "TI", 256)
         mm("PP", "UR", "URS", qt, qts)
         send_codes(lq, ls, qt, qts, 256, "aq%d" % r)
-        keys[0]()
-        dma_fold("KW", KA, 192, "fk")
-        if r > 0:
-            cp(x(HU, 0, 12), x("HW", 0, 12))
-        plane(0)
-        plane(1)
+        act(R(K, 0, 256), keys)
         act(R("PR", 0, 256), R("PP", 0, 256))
-        hu = x(HU, 0, 12)
+        if r == 0:
+            for b in range(4):
+                quant("EQ%d" % b, "EQS%d" % b, "EB" if b % 2 else "EA", 128, 2 - b // 2 * 2)
+        else:
+            fold(hu, "YS", "HR", 192)
         tt(R("TMP", 0, 192), R("PR", 0, 256, 1, hu), R("DMASK", 0, 192), A.min)
         act(R("SC", 0, 192), R("PR", 0, 256, 1, hu))
-        plane(2)
-        plane(3)
-        ranks(keys[1:])
-        scan(R("YS", 0, 192), RST(192), R("EQR", 0, 192))
-        act(R("FLB", 0, 256), R("ZERO", 0, 256))
-        if r == 0:
-            scalar_constants()
-            for b in range(4):
-                quant("EQ%d" % b, "EQS%d" % b, "E%d" % b, 128)
-        act(R("LBM", 0, 192), R("IOTA", 0, 192), IDENT, -BIG, x("HBB", 0, 1))
+        ranks()
         mm("PQ", "UP", "UPS", lq, ls)
-        act(R("PPR", 0, 256), R("PQ", 0, 256))
+        for b, p in enumerate(("PD0", "PD1", "PS2", "PS3")):
+            mm(p, "EQ%d" % b, "EQS%d" % b, lq, ls)
+        if r == 0:
+            tables_d()
+            lists()
+        act(R(K, 256, 512), R("PQ", 0, 256))
+        ranks_end()
+        cp(R("LROW", 0, 192, 1, x("RKU", 0, 12)), R("HR", 0, 192))
+        fold(R(lw, 0, 4), "LL", "LROW", 64)
+        send(R(lp, 0, 4), R(lw, 0, 4), "al%d" % r)
+
+        def unpack(b):
+            act(R("AD%d" % b, 256, 512), R(("PD0", "PD1", "PS2", "PS3")[b], 0, 256), COPY, 64.0)
+
         unpack(0)
         unpack(1)
-        ranks_end()
-        cp(R("LROW", 0, 192, 1, x("RKU", 0, 12)), R(HR, 0, 192))
-        ts(x("LFN", 0, 12), x("RK", 0, 12), 63.5, -BIG, A.is_lt, A.mult)
-        tt(R("TMP", 0, 64), R("LROW", 0, 64), MASK(64), A.mult)
-        tt(x("LF3", 0, 12), x("LFN", 0, 12), x("C257", 0, 12), A.mult)
-        scan(R("LL", 0, 64), RST(64), R("TMP", 0, 64))
-        cp(R(lw, 0, 4), own("LL", 64))
-        send(R(lp, 0, 4), R(lw, 0, 4), "al%d" % r)
-        cp(R("FLB", 0, 256, 1, R(lw, 0, 4)), R("BIGS", 0, 64))
-        act(R("SF", 0, 192), R("FLB", 0, 256, 1, hu), IDENT, -1.0 / BIG, 1.0)
-        act(R("SFP", 0, 256), R("FLB", 0, 256), IDENT, -1.0 / BIG, 1.0)
-        tt(R("KST", 0, 192), R("FLB", 0, 256, 1, hu), R(KA, 0, 192), A.add)
         unpack(2)
+        lpo = R(lp, 0, 4)
+        arr = R(K, 256, 512, 1, lpo)
+
+        def before(c):
+            ts(R("CMN", 208 * c, 208 * c + 192), R("KST", 0, 192), R("AOS", 16 * c + 15, 16 * c + 16), None, A.is_le)
+            total(x("TTA", c, c + 1), R("CMN", 208 * c, 208 * c + 193), 193)
+
+        cp(R(K, 0, 256, 1, R(lw, 0, 4)), R("BIGS", 0, 64))
+        act(R("KST", 0, 192), R(K, 0, 256, 1, hu))
         unpack(3)
-        tt(R("LBK", 0, 192), R("LBM", 0, 192), R("KST", 0, 192), A.max)
-        scan(R("CCS", 0, 192), R("ONE", 0, 192), R("SF", 0, 192))
-        red(x("LB", 0, 1), R("LBK", 0, 192), A.min)
-        tt(R("XC", 0, 192), R("CCS", 0, 192), R("SF", 0, 192), A.mult)
-        dma_fold("XCW", "XC", 192, "fx")
-        scan(R("CSP", 0, 256), R("ONE", 0, 256), R("SFP", 0, 256))
-        tt(R("TMY", 0, 256), R("XC", 0, 208, 1, x(QV)), MASK(256), A.mult)
-        tt(x("CSMB", 1, 17), own("CSP", 256), x("HBP"), A.add)
-        scan(R("XWS", 0, 256), RST(256), R("TMY", 0, 256))
-        tt(x("NCM"), x("CSMB"), x("CSMB", 1, 17), A.subtract)
-        tt(x("KWB", 0, 12), x("KW", 0, 12), x("LFN", 0, 12), A.add)
         if last:
             quant("QVC", "QVS", "VT", 128)
-        lpo = R(lp, 0, 4)
-        arr = R(KA, 192, 256)
-        act(arr, R("PPR", 0, 256, 1, lpo))
-        act(x("TH"), x("NCM"), RELU, 1.0, 14.0)
-        tt(R("TMP", 0, 64), R("PPR", 0, 256, 1, lpo), MASK(64), A.mult)
-        ts(R("ARC", 0, 64), arr, x("LB", 0, 1), None, A.is_lt)
+        ts(R("SFP", 0, 256), R(K, 0, 256), BIG / 2, None, A.is_lt)
+        scan(R("LBK", 0, 256), R(K, 0, 256), R("LBM", 0, 256), A.min, A.max, BIG)
+        tt(R("TMY", 0, 256), R("SFP", 0, 256), R("TRIW", 0, 256), A.mult)
+        scan(R("CSP", 16, 272), R("C75", 0, 256), R("SFP", 0, 256), A.add, A.add)
+        scan(R("XWS", 0, 256), RST(256), R("TMY", 0, 256))
+        tt(x("HC"), h1, h0, A.subtract)
+        act(R("ARS", 0, 64), IOTA(256, 512, lpo))
+        tt(R("TMP", 0, 64), arr, MASK(64), A.mult)
+        ts(R("ARC", 0, 64), arr, R("LBK", 255, 256), None, A.is_lt)
+        tt(x("WT"), own("XWS", 256), x("CT"), A.add)
         scan(R("AOS", 0, 64), RST(64), R("TMP", 0, 64))
         red(x("AR1", 0, 1), R("ARC", 0, 64), A.add)
-
-        def cmp_stay(c):
-            ts(R("CMN", 192 * c, 192 * c + 192), R("KST", 0, 192), R("AOS", 16 * c + 15, 16 * c + 16), None, A.is_le)
-            total(x("TT", 12 + c, 13 + c), R("CMN", 192 * c, 192 * c + 192), 192)
-
-        def cmp_arr(c):
-            q = R("CMQ", 64 * c, 64 * c + 64)
-            if c >= 12 - ON_SCALAR:
-                act(q, arr, RELU, -1.0, x("KWB", c, c + 1))
-                total(x("AC0", c, c + 1), q, 64, SIGN)
-            else:
-                ts(q, arr, x("KWB", c, c + 1), None, A.is_lt)
-                total(x("AC0", c, c + 1), q, 64)
-
-        compares = [lambda c=c: cmp_stay(c) for c in range(4)] + [lambda c=c: cmp_arr(c) for c in range(12)]
-        sel = R("S4", 0, 16, 1, x("AL", 0, 1))
-        tu = x("TU")
-        windows = [
-            lambda: ts(x("B32", 0, 32), x("GM", 0, 32), x("AR1", 0, 1), None, A.mult),
-            lambda: turn(x("B32T", 0, 32), x("B32", 0, 32)),
-            lambda: tt(x("ARB", 1, 17), x("B32T", 0, 16), x("B32T", 16, 32), A.add),
-            lambda: tt(x("EB", 0, 17), x("ARB", 0, 17), x("CSMB", 0, 17), A.add),
-            lambda: tt(x("AX"), x("ARB", 1, 17), x("ARB", 0, 16), A.subtract),
-            lambda: tt(x("X2", 0, 32), R("EB", 0, 24, 1, x("XL", 0, 2)), x("C1C", 0, 32), A.mult),
-            lambda: tt(x("BA"), x("AX"), x("TH"), A.is_gt),
-            lambda: tt(x("CN4", 0, 4), x("EB", 4, 17, 4), x("EB", 0, 13, 4), A.subtract),
-            lambda: tt(x("E64"), x("X2", 0, 16), x("X2", 16, 32), A.add),
-            lambda: scan(x("S4"), x("RST4"), x("BA"), A.mult, A.max),
-            lambda: ts(x("BAD4", 0, 4), x("CN4", 0, 4), 52.5, None, A.is_gt),
-            lambda: tt(x("EQD"), x("E64"), x("EB", 0, 16), A.subtract),
-            lambda: tt(x("ZX4", 0, 4), x("BAD4", 0, 4), x("S4", 3, 16, 4), A.mult),
-            lambda: act(x("XM"), own("XWS", 256), IDENT, 1.0, -193.0),
-            lambda: act(x("XV"), own("XWS", 256), SIGN),
-            lambda: tt(x("EP1"), sel, x("EQD"), A.mult),
-            lambda: tt(x("NI"), sel, x("AX"), A.add),
-            lambda: red(x("S256", 0, 1), x("ZX4", 0, 4), A.max),
-            lambda: tt(x("EP1"), x("EP1"), x("EB", 0, 16), A.add),
-            lambda: ts(x("I0", 1, 32, 2), x("NI"), x("S256", 0, 1), 0.0, A.add, A.is_equal),
-            lambda: tt(x("CE3"), x("C12"), x("EP1"), A.subtract),
-            lambda: tt(x("ENI"), x("ARB", 0, 16), x("XM"), A.add),
-            lambda: ts(x("EP3"), x("CE3"), x("S256", 0, 1), None, A.mult),
-            lambda: tt(x("EN2"), x("ENI"), x("XV"), A.mult),
-            lambda: tt(x("D1", 1, 33, 2), x("EP1"), x("EP3"), A.add),
-            lambda: tt(x("TB", 0, 12), x("XCW", 0, 12), x("LF3", 0, 12), A.add),
-            lambda: tt(x("D1", 0, 32, 2), x("D1", 3, 35, 2), x("D1", 1, 33, 2), A.subtract),
-            lambda: tt(x("TT", 12, 16), x("JW1", 0, 4), x("TT", 12, 16), A.add),
-            lambda: scan(x("UA", 0, 32), x("D0A", 0, 32), x("D1", 0, 32)),
-            lambda: scan(x("UB", 0, 32), x("D0B", 0, 32), x("D1", 0, 32)),
-            lambda: ts(x("QI"), x("UA", 1, 32, 2), UP_, None, A.add),
-            lambda: tt(x("TT", 0, 12), x("TB", 0, 12), x("AC0", 0, 12), A.add),
-            lambda: tt(x("VL"), x("UB", 1, 32, 2), x("QI"), A.is_gt),
-            lambda: ts(tu, x("TT"), -1.0, None, A.add),
-            lambda: tt(x("I1", 1, 32, 2), x("VL"), x("QI"), A.mult),
-            lambda: cp(R("SEQ", 0, 448, 1, tu), R(HR, 0, 256)),
-            lambda: tt(x("I1", 0, 32, 2), x("EN2"), x("I1", 1, 32, 2), A.subtract),
-            lambda: scan(x("UX", 0, 32), x("I0", 0, 32), x("I1", 0, 32)),
-            lambda: ts(x(QVn), x("UX", 1, 32, 2), 192.0, None, A.add),
-        ]
-        act(R(HR, 192, 256), R("IOTA", 256, 512, 1, lpo))
-        while compares or windows:
-            if windows:
-                windows.pop(0)()
-            if compares:
-                compares.pop(0)()
+        tt(x("TB"), x("WT"), h0, A.add)
+        before(0)
+        cp(x("AU", 0, 1), x("AR1", 0, 1))
+        before(1)
+        tt(r1, IOTA(0, 72, x("AU", 0, 1)), h1, A.add)
+        before(2)
+        tt(x("CN"), r1, r0, A.subtract)
+        before(3)
+        scan(x("S4"), x("RST4"), x("CN"), A.mult, A.max)
+        tt(R("X4", 0, 64), R("RB", 0, 24, 1, x("L4", 0, 4)), R("C4", 0, 64), A.mult)
+        ts(x("TBU"), x("TB"), -WHOLE, None, A.add)
+        ts(nsel, R("S4", 0, 16, 1, x("AL", 0, 1)), 2.5, -1.0, A.is_gt, A.mult)
+        tt(x("CN4", 0, 4), x("RB", 4, 17, 4), x("RB", 0, 13, 4), A.subtract)
+        cp(x("TU", 8, 12), x("TTA", 0, 4))
+        tt(x("AX"), x("CN"), x("HC"), A.subtract)
+        scan(R("O1", 0, 64), R("S1A", 0, 64), R("X4", 0, 64))
+        tt(x("ZX", 0, 4), x("CN4", 0, 4), R("S1A", 3, 64, 16), A.mult)
+        tt(R("NR", 0, 64), IOTA(0, 192, x("TU", 8, 12)), R("J64", 0, 64), A.subtract)
+        for c in range(8):
+            total(x("AC", c, c + 1), R("NR", 0, 64), 64, x("IW5", c, c + 1))
+        red(x("ZM", 0, 1), x("ZX", 0, 4), A.min)
+        tt(R("X8", 0, 128), R("O1", 0, 72, 1, x("L8", 0, 8)), R("C8", 0, 128), A.mult)
+        ts(R("S2A", 2, 128, 4), x("C45", 0, 32), x("ZM", 0, 1), None, A.is_lt)
+        cp(R("SEQ", 0, 192, 1, x("TU", 8, 12)), R("ARS", 0, 64))
+        scan(R("O2", 0, 640, 5), R("S2A", 0, 128), R("X8", 0, 128))
+        tt(x("NI"), x("AX"), nsel, A.subtract)
+        tt(R("O2", 23, 640, 40), x("WT"), r0, A.add)
+        tt(R("O2", 31, 640, 40), x("WT"), r0, A.add)
+        tt(R("S3A", 1, 80, 5), R("O2", 35, 640, 40), R("O2", 15, 640, 40), A.is_le)
+        ts(R("S3A", 3, 80, 5), x("NI"), R("S2A", 2, 3), -1.0, A.is_ge, A.mult)
+        cp(R("SRC", 0, 640, 1, x("TBU")), IOTA(0, 256))
         if last:
-            act(R("HROL", 0, 192), R(HR, 0, 192))
-            act(R("HROL", 192, 256), R("IOTA", 256, 320))
-        else:
-            ts(x("UX", 0, 32, 2), x("UX", 1, 32, 2), 0.0, None, A.is_equal)
-        tt(R("TMY", 0, 256), R("SEQ", 0, 208, 1, x(QVn)), MASK(256), A.mult)
-        if not last:
-            scan(x("UY", 0, 32), x("C64I", 0, 32), x("UX", 0, 32))
-        scan(R("YS", 0, 256), RST(256), R("TMY", 0, 256))
-        if not last:
-            ts(x("QDU"), x("UY", 1, 32, 2), 192.0, None, A.add)
-        cp(x("OFY"), own("YS", 256))
-        for t in range(3):
-            act(R(Fn, t, W64, 4), R("TP%d" % t, 0, 528, 1, x("OFY")))
-        if not last:
-            cp(R(HRn, 0, 512, 1, x("QDU")), R("IOTA", 0, 256))
-            dma_fold("HW", HRn, 192, "fh")
-        cp(R(Fn, 3, W64, 4), R("TP3", 0, 528, 1, x("OFY")))
-        keys = [
-            lambda KA=KA, KAn=KAn: cp(R(KAn, 0, 448, 1, x("TU")), R(KA, 0, 256)),
-            lambda: ts(x("HBI"), x("D1", 3, 35, 2), UP_, None, A.add),
-            lambda: tt(x("HBP"), x("HBI"), x("C16"), A.subtract),
-            lambda: tt(x("M17"), x("HBI"), MASK(16), A.mult),
-            lambda: red(x("HB1", 0, 1), x("M17"), A.add),
-            lambda: ts(x("HBB", 0, 1), x("HB1", 0, 1), 191.5, BIG, A.add, A.mult),
-        ]
-        F, Fn, HR, HRn, HU, HUn, QV, QVn, KA, KAn = Fn, F, HRn, HR, HUn, HU, QVn, QV, KAn, KA
+            act(R("OLT", 0, 512), IOTA(0, 512))
+            act(R("OLT", 512, 528), ONE(16), COPY, -1.0)
+        tt(x("TTS", 0, 8), x("AC", 0, 8), x("C2I", 0, 8), A.add)
+        scan(R("O3", 0, 80), R("S3A", 0, 80), R("O2", 7, 640, 8))
+        ts(x("TU", 0, 8), x("TTS", 0, 8), 0.5, None, A.mult)
+        ts(x("QD"), R("O3", 3, 80, 5), -WHOLE, None, A.add)
+        cp(R("SEQ", 0, 192, 1, x("TU", 0, 8)), R("SRC", 0, 128))
+        cp(R("TMY", 0, 128), R("SEQ", 0, 640, 1, x("QD", 0, 8)))
+        act(R("TMY", 128, 256), R("SEQ", 0, 640, 1, x("QD", 8, 16)))
+        fold(x("OFY"), "YS", "TMY", 256)
+        for t in range(4):
+            o, a = R(Fn, t, W64, 4), R("AD%d" % t, 0, 528, 1, x("OFY"))
+            if t < 2:
+                act(o, a, COPY, 0.015625)
+            else:
+                ts(o, a, 0.015625, None, A.mult)
+        keys = R(K, 0, 528, 1, x("OFY"))
+        F, Fn, K, Kn = Fn, F, Kn, K
 
     stored = [0]
 
@@ -563,25 +558,23 @@ def rank_program(g, core, T, topo):
         stored[0] += 1
         emit(q, lambda: Q[q].dma_start(dst, src), [], [a], ("dout", 16 * stored[0], 16))
 
-    cp(R("SEQO", 0, 448, 1, x("TU")), R("HROL", 0, 256))
     quant("QF", "QFS", F, 256)
     mm("PP", "QVC", "QVS", "QF", "QFS")
-    cp(R("OLR", 0, 256), R("SEQO", 0, 208, 1, x(QV)))
-    act(R("YO", 0, 256), R("PP", 0, 256))
+    cp(R("OLT", 256, 512, 1, lpo), IOTA(256, 320))
+    cp(R("YO", 0, 256), R("PP", 0, 256))
+    act(R("OLR", 0, 256), R("OLT", 0, 528, 1, x("OFY")))
     qf = R("QF", 0, 256, 1, None, dt.uint8)
     store("y", T.oc[:, 0:W64], qf, ap(qf))
     for k in range(4):
         store("y", T.osc[4 * k:4 * k + 4, 0:256], R("QFS", 0, 256), T.QFS[32 * k:32 * k + 4, 0:256])
-    store("s", T.y[:, 0:256], R("YO", 0, 256), ap(R("YO", 0, 256)))
-    store("y", T.ol[:, 0:256], R("OLR", 0, 256), T.OLR[0:128:16, 0:256])
+    store("y", T.y[:, 0:256], R("YO", 0, 256), ap(R("YO", 0, 256)))
+    store("s", T.ol[:, 0:256], R("OLR", 0, 256), T.OLR[0:128:16, 0:256])
 
     for q in ("v", "s", "t", "g"):
         if known["g"].get(q, 0) < cnt[q]:
             g.wait_ge(T.sem[sem_of[q]], cnt[q])
     for n in ("dx", "du", "dw", "dws", "dv"):
         g.wait_ge(T.sem[n], 16)
-    for n in ("fk", "fx", "fh"):
-        g.wait_ge(T.sem[n], folded[n])
     g.wait_ge(T.sem["dout"], 16 * stored[0])
     g.wait_ge(T.sem["loc"], sent[0])
     g.wait_ge(T.sem["au"], 2 * engines)

@@ -12,6 +12,8 @@ W64 = 4 * 256
 UP_ = 0.5 - 1.0 / 512
 WHOLE = 1.5 * 2.0 ** 23
 ON_SCALAR = 10
+SUMS_ON_SCALAR = 3
+SIGNS_ON_VECTOR = 3
 
 SCRATCH = {}
 
@@ -21,15 +23,15 @@ def _decl(names, where, shape, dtype):
         SCRATCH[n] = (where, shape, dtype)
 
 
-_decl("XT", "sbuf", [128, 832], "bfloat16")
+_decl("XT", "sbuf", [128, 768], "bfloat16")
 _decl("UT VT", "sbuf", [128, 512], "bfloat16")
 _decl("EA EB ONEB AD0 AD1 AD2 AD3", "sbuf", [128, 528], "bfloat16")
 _decl("TI FA FB GI", "sbuf", [128, 1024], "bfloat16")
 _decl("CMP", "sbuf", [128, 2304], "bfloat16")
 _decl("JNK", "sbuf", [128, 8 * 272], "bfloat16")
 _decl("CMN", "sbuf", [128, 4 * 272], "bfloat16")
-_decl("RST SFP C75 EQR YB TMB", "sbuf", [128, 256], "bfloat16")
-_decl("CSP", "sbuf", [128, 272], "bfloat16")
+_decl("RST SFP CFB EQR YB TMB CSP", "sbuf", [128, 256], "bfloat16")
+_decl("CUM", "sbuf", [128, 4 * 192], "bfloat16")
 _decl("QX", "sbuf", [128, 192], "float8_e4m3fn_x4")
 _decl("QXS", "sbuf", [128, 192], "uint8")
 _decl("QU QVC UR UP EQ0 EQ1 EQ2 EQ3", "sbuf", [128, 128], "float8_e4m3fn_x4")
@@ -51,14 +53,17 @@ _decl("C8 X8 S2A", "sbuf", [128, 128], "float32")
 _decl("O1 S3A O3", "sbuf", [128, 80], "float32")
 _decl("LL AOS ARC BIGS NR C4 X4 S1A J64", "sbuf", [128, 64], "float32")
 SMALL = ("RB C1C C12 IW M16 M17 CNT RK KI0 ENC INV EN2 SP AR1 RST4 CN S4 CN4 ZX ZM C45 HC WT TB CT AX NI TTA AC C2I TTS IW5 "
-         "S16 S161 N16 N161 CA CB PA PB PC PD C4C C8C LB0 OFS").split()
+         "S16 S161 N16 N161 CA CB PA PB PC PD C4C C8C LB0 OFS O16 O17 T1 C12P P1 P2 HB HW").split()
 _decl("SMALLS", "sbuf", [128, 32 * len(SMALL)], "float32")
-_decl("INTS", "sbuf", [128, 16 * 10], "int32")
+_decl("INTS", "sbuf", [128, 16 * 11], "int32")
 _decl("LW0 LW1 LW2 LP0 LP1 LP2", "sbuf", [128, 4], "uint16")
 _decl("LISTS", "sbuf", [128, 16 * 12], "uint16")
-_decl("OFF", "sbuf", [128, 64], "uint16")
+_decl("XP0 XP1 XP2 XP3", "sbuf", [128, 208], "bfloat16")
+_decl("CMQ", "sbuf", [128, 512], "bfloat16")
+_decl("STEP", "sbuf", [128, 192], "float32")
+_decl("FLT", "sbuf", [128, 640], "float32")
 PIECE = {n: ("SMALLS", 32 * i) for i, n in enumerate(SMALL)}
-PIECE.update({n: ("INTS", 16 * i) for i, n in enumerate("PI SI I2 I3 I4 I8 KI KA4 KB4 UI".split())})
+PIECE.update({n: ("INTS", 16 * i) for i, n in enumerate("PI SI I2 I3 I4 I8 KI KA4 KB4 UI H3".split())})
 PIECE.update({n: ("LISTS", 16 * i) for i, n in enumerate("RKU HU QV0 QD TU TBU AL UL OFY AU L4 L8".split())})
 
 SEMAPHORES = ["sv", "ss", "st", "sg", "dx", "du", "dw", "dws", "dv", "dout", "loc", "au",
@@ -177,8 +182,8 @@ def rank_program(g, core, T, topo):
     def fill(o, c):
         emit("v", lambda: g.vector.memset(ap(o), c), [o], [])
 
-    def quant(o, s, a, n, at=0):
-        o, s, a = R(o, 0, n), R(s, 0, n), R(a, at, at + 4 * n)
+    def quant(o, s, a, n, at=0, to=0):
+        o, s, a = R(o, to, to + n), R(s, to, to + n), R(a, at, at + 4 * n)
         emit("v", lambda: g.vector.quantize_mx(ap(o), ap(s), ap(a)), [o, s], [a])
 
     def act(o, a, func=COPY, scale=1.0, bias=0.0):
@@ -200,8 +205,8 @@ def rank_program(g, core, T, topo):
         else:
             emit("s", lambda: g.scalar.activation(ap(j), ap(a), SIGN, bias=ap(bias), scale=-1.0, accum_out=ap(o)), [j, o], [a, bias])
 
-    def mm(o, l, ls, r, rs, n=256, c=0):
-        o, l, ls, r, rs = R(o, 0, n), R(l, c, c + 128), R(ls, c, c + 128), R(r, 0, n), R(rs, 0, n)
+    def mm(o, l, ls, r, rs, n=256, c=0, at=0):
+        o, l, ls, r, rs = R(o, 0, n), R(l, c, c + 128), R(ls, c, c + 128), R(r, at, at + n), R(rs, at, at + n)
         emit("t", lambda: g.tensor.matmul_mx(ap(o), ap(l), ap(ls), ap(r), ap(rs), True, True), [o], [l, ls, r, rs])
 
     def iota(o, pattern, base=0, cm=0):
@@ -260,15 +265,13 @@ def rank_program(g, core, T, topo):
     iota(x("UI", 0, 8), [[16, 8]])
     iota(x("M16"), [[16, 16]])
     iota(x("C12"), [[12, 16]])
-    fill(ONE(528), 1.0)
-    for n, b in (("EA", 2), ("EB", 3)):
-        o = R(n, 0, 516)
-        emit("g", lambda: g.affine_select(ap(o), ap(ONE(516)), [[-1, 516]], A.is_equal, 0.0, b, 4), [o], [ONE(516)])
-    iota(R("HR", 0, 192), [[4, 64], [1, 3]])
-    iota(x("C1C"), [[0, 4], [1, 4]])
     iota(x("C4C", 0, 4), [[4, 4]])
     iota(x("C8C", 0, 8), [[8, 8]])
-    iota(x("CT"), [[28, 16]], 192)
+    iota(x("C1C"), [[0, 4], [1, 4]])
+    for b in range(4):
+        const("XP%d" % b, (192, 208), 0)
+    fill(ONE(528), 1.0)
+    iota(R("HR", 0, 192), [[4, 64], [1, 3]])
     iota(R("S1A", 0, 64), [[0, 16], [1, 4]])
     iota(R("S2A", 0, 128), [[0, 64], [1, 2]])
     iota(R("J64", 0, 64), [[1, 64]])
@@ -277,9 +280,14 @@ def rank_program(g, core, T, topo):
     const("O1", (64, 68), 0)
     const("O1", (68, 72), 1)
     const("C4", (0, 64), 1)
-    const("CSP", (0, 16), 0)
+    const("HB", (0, 8), 0)
+    const("FLT", (192, 640), 0)
+    const("SEQ", (192, 640), 512)
     for b in range(4):
         const("AD%d" % b, (512, 528), 0)
+    for n, b in (("EA", 2), ("EB", 3)):
+        o = R(n, 0, 516)
+        emit("g", lambda: g.affine_select(ap(o), ap(ONE(516)), [[-1, 516]], A.is_equal, 0.0, b, 4), [o], [ONE(516)])
 
     scan(IOTA(0, 512), ONE(512), ONE(512), A.mult, A.add, -1.0)
     ts(x("SI", 0, 1), x("PI", 0, 1), 15, None, A.bitwise_and)
@@ -291,13 +299,6 @@ def rank_program(g, core, T, topo):
     act(x("IW"), x("M16"), IDENT, 1.0, s)
     act(R("RMIN", 0, 192), RST(192), IDENT, 2 * BIG, -BIG)
     act(R("DMASK", 0, 192), MASK(192), IDENT, 2 * BIG, -BIG)
-    ts(R("TRIW", 0, 256), R("JM", 0, 256), s, None, A.is_lt)
-    tt(R("TMY", 0, 256), MASK(256), IOTA(192, 448), A.mult)
-    cp(x("KI"), x("IW"))
-    fill(R("XT", 768, 832), 0.0)
-    ts(x("KA4"), x("KI"), 2, None, A.arith_shift_right)
-    ts(x("KB4"), x("KI"), 3, None, A.bitwise_and)
-    tt(R("TRIW", 0, 256), R("TRIW", 0, 256), R("TMY", 0, 256), A.subtract)
 
     def tables_a():
         act(x("LB0", 0, 1), s, IDENT, 16.0, 15.5)
@@ -309,6 +310,9 @@ def rank_program(g, core, T, topo):
         act(x("CB", 0, 1), s, IDENT, 0.75, 0.75 + UP_)
         act(R("LBM", 0, 256), IOTA(0, 256), SIGN, -1.0, x("LB0", 0, 1))
         act(R("SC", 192, 208), ONE(16), COPY, BIG)
+        act(R("XWS", 0, 256), MASK(256), COPY, -4096.0)
+        act(R("SRC", 0, 1), ONE(1), COPY, 0.0)
+        act(R("SRC", 1, 257), MASK(256), COPY, 1024.0)
 
     def tables_b():
         for i, n in ((0, "S16"), (1, "N16"), (4, "S161"), (5, "N161")):
@@ -320,31 +324,34 @@ def rank_program(g, core, T, topo):
 
     def tables_c():
         act(R("BIGS", 0, 64), ONE(64), COPY, BIG)
-        act(R("C75", 0, 256), ONE(256), COPY, -0.75)
         for n in ("KA", "KB"):
             act(R(n, 512, 528), ONE(16), COPY, BIG)
         act(R("CMN", 192, 4 * 208, 208), x("IW", 0, 4))
-        act(R("XWS", 0, 256), MASK(256), COPY, -4096.0)
-        act(R("SRC", 0, 1), ONE(1), COPY, 0.0)
-        act(R("SRC", 1, 257), MASK(256), COPY, 1024.0)
         act(x("IW5", 0, 8), x("IW", 0, 8), IDENT, 1.0, 0.5)
-        act(x("C2I", 0, 8), x("IW", 0, 8), IDENT, 2.0, 64.0)
+        act(x("C2I", 0, SIGNS_ON_VECTOR), x("IW", 0, SIGNS_ON_VECTOR), COPY, 2.0)
+        act(x("C2I", SIGNS_ON_VECTOR, 8), x("IW", SIGNS_ON_VECTOR, 8), IDENT, 2.0, 64.0)
         act(x("RST4"), x("C1C"), SIGN)
+        act(R("STEP", 0, 64), ONE(64), COPY, 0.0)
+        act(R("STEP", 64, 192), ONE(128))
 
     def tables_d():
+        act(x("O17", 0, 1), x("O16", 0, 1), IDENT, 1.0, 1.0)
+        act(x("T1"), x("IW"), IDENT, 1.0, 192.0)
+        act(x("C12P"), x("C12"), IDENT, 1.0, 12.0)
+        act(x("CT"), x("T1"), COPY, x("O17", 0, 1))
+        act(x("T1"), x("IW"), IDENT, 1.0, 193.0)
         act(R("C4", 0, 64, 4), x("C1C"), COPY, 0.25)
         act(R("C4", 1, 64, 4), x("C1C"), IDENT, -0.25, 1.0)
         act(R("S1A", 2, 64, 4), ONE(16), COPY, -1.0)
         act(R("S3A", 2, 80, 5), ONE(16), COPY, -1.0)
         act(R("O2", 7, 640, 40), x("IW"), IDENT, 1.0, 192.0)
-        act(R("O2", 39, 640, 40), ONE(16))
+        act(R("O2", 23, 640, 40), ONE(16), COPY, WHOLE)
+        act(R("S3A", 3, 80, 5), ONE(16))
         act(x("C45", 0, 32), ONE(32), COPY, -4.5)
-        act(R("SEQ", 192, 640), ONE(448), COPY, 512.0)
 
     def lists():
-        tt(R("CF", 0, 256), R("XWS", 0, 256), R("SRC", 0, 256), A.add)
         ts(x("OFS", 0, 1), s, 14.5, -1024.0, A.is_lt, A.mult)
-        ts(x("CT"), x("CT"), s, WHOLE, A.add, A.add)
+        ts(x("O16", 0, 1), s, 14.5, 16.0, A.is_lt, A.mult)
         ts(x("I2", 0, 1), x("SI", 0, 1), 12, None, A.bitwise_and)
         ts(x("I3", 0, 1), x("SI", 0, 1), 3, None, A.bitwise_and)
         ts(x("I4", 0, 1), x("SI", 0, 1), 2, None, A.arith_shift_right)
@@ -359,73 +366,90 @@ def rank_program(g, core, T, topo):
         ts(x("L4", 0, 4), x("C4C", 0, 4), x("INV", 0, 1), None, A.add)
         ts(x("L8", 0, 8), x("EN2", 0, 8), x("PD", 0, 1), 68.0, A.mult, A.add)
 
+    lists()
+    cp(x("KI"), x("IW"))
+    fill(R("SEQS", 192, 208), 192.0)
+    ts(x("H3"), x("IW"), 1.0 / 3, -1.0 / 3, A.mult, A.add)
+    ts(x("KA4"), x("KI"), 2, None, A.arith_shift_right)
+    ts(x("KB4"), x("KI"), 3, None, A.bitwise_and)
     tables_a()
     quant("QU", "QUS", "UT", 128)
+    tt(x("M17"), x("IW"), x("H3"), A.add)
+    ts(x("KI0"), x("KA4"), 3.0, -192.0, A.mult, A.add)
+    ts(x("INV"), x("KB4"), 2.5, None, A.is_lt)
     cp(R("UR", 0, 128, 1, None, dt.uint32), R("QU", 0, 128, 1, R("UL", 0, 8), dt.uint32))
     act(R("URS", 0, 128), R("QUS", 0, 128, 1, R("UL", 0, 8)))
     quant("QX", "QXS", "XT", 192)
     mm("PP", "UR", "URS", "QX", "QXS", 192)
     send_codes("UP", "UPS", "UR", "URS", 128, "au")
-    act(R("SC", 0, 192), R("PP", 0, 192))
+    for b in range(4):
+        act(R("XP%d" % b, 0, 192), R("XT", b, 768, 4))
     tables_b()
-    ts(x("KI0"), x("KA4"), 3.0, -192.0, A.mult, A.add)
-    ts(x("INV"), x("KB4"), 2.5, None, A.is_lt)
     tt(x("ENC"), x("KI0"), x("KB4"), A.add)
-    fill(R("SEQS", 192, 208), 192.0)
+    cp(x("HU", 0, 12), x("M17", 0, 12))
     tt(x("EN2"), x("ENC"), x("INV"), A.mult)
-    ts(x("KI"), x("IW"), 1.0 / 3, -1.0 / 3, A.mult, A.add)
-    ts(x("QV0"), x("EN2"), 192.0, None, A.add)
-    tt(R("TMP", 0, 192), R("SC", 0, 192), R("DMASK", 0, 192), A.min)
 
-    def ranks():
-        scan(R("Z", 0, 192), R("RMIN", 0, 192), R("TMP", 0, 192), A.min, A.max, -BIG)
-        for c in range(12):
+    def ranks(row, diag):
+        for a in (0, 96):
+            tt(R("TMP", a, a + 96), diag(a), R("DMASK", 0, 96), A.min)
+        for a in (0, 96):
+            scan(R("Z", a, a + 96), R("RMIN", 0, 96), R("TMP", a, a + 96), A.min, A.max, -BIG)
+        for i in range(12):
+            c = (i + 12 - ON_SCALAR) % 12
             k = R("Z", 16 * c + 15, 16 * c + 16)
             e = 16 * c + 16
-            ts(R("CMP", 192 * c, 192 * c + e), R("SC", 0, e), k, None, A.is_le)
+            ts(R("CMP", 192 * c, 192 * c + e), R(row, 0, e), k, None, A.is_le)
             if e < 192:
-                ts(R("CMP", 192 * c + e, 192 * c + 192), R("SC", e, 192), k, None, A.is_lt)
-            if c < ON_SCALAR:
+                ts(R("CMP", 192 * c + e, 192 * c + 192), R(row, e, 192), k, None, A.is_lt)
+            if i < ON_SCALAR:
                 total(x("CNT", c, c + 1), R("CMP", 192 * c, 192 * c + 192), 192)
-        tt(R("EQR", 0, 192), R("Z", 0, 192), R("SC", 0, 192), A.is_equal)
-        for c in range(ON_SCALAR, 12):
-            red(x("CNT", c, c + 1), R("CMP", 192 * c, 192 * c + 192), A.add)
-            if c == ON_SCALAR:
+            if i == 4:
+                tt(R("EQR", 0, 192), R("Z", 0, 192), R(row, 0, 192), A.is_equal)
+            if i == 5:
                 scan(R("YB", 0, 192), RST(192), R("EQR", 0, 192))
+        for c in range(12 - ON_SCALAR):
+            scan(R("CUM", 192 * c, 192 * c + 192), ONE(192), R("CMP", 192 * c, 192 * c + 192))
 
     def ranks_end():
-        tt(x("RK", 0, 12), x("CNT", 0, 12), own("YB"), A.subtract)
-        cp(x("RKU", 0, 12), x("RK", 0, 12))
+        n = 12 - ON_SCALAR
+        tt(x("RK", n, 11), x("CNT", n, 11), R("YB", 16 * n + 15, 176, 16), A.subtract)
+        for c in range(n):
+            ts(x("RKU", c, c + 1), R("CUM", 192 * c + 191, 192 * c + 192), R("YB", 16 * c + 15, 16 * c + 16), None, A.subtract)
+        cp(x("RKU", n, 11), x("RK", n, 11))
+        ts(x("RKU", 11, 12), x("CNT", 11, 12), R("YB", 191, 192), None, A.subtract)
 
     def fold(o, y, a, n):
         scan(R(y, 0, n), R("CF", 0, n), R(a, 0, n), A.add, A.max)
         ts(o, own(y, n), x("OFS", 0, 1), None, A.add)
 
-    ranks()
-    tt(x("M17"), x("IW"), x("KI"), A.add)
-    cp(x("HU", 0, 12), x("M17", 0, 12))
+    ranks("PP", lambda a: R("PP", a, a + 96))
+    act(R("SC", 0, 192), R("PP", 0, 192))
+    ts(x("QD"), x("EN2"), 192.0, None, A.add)
     ranks_end()
     tables_c()
+    tables_d()
     cp(R("SEQS", 0, 192, 1, x("RKU", 0, 12)), IOTA(0, 192))
-    tt(R("TMB", 0, 256), R("SEQS", 0, 208, 1, x("QV0")), MASK(256), A.mult)
+    tt(R("TMB", 0, 256), R("SEQS", 0, 208, 1, x("QD")), MASK(256), A.mult)
     scan(R("YB", 0, 256), RST(256), R("TMB", 0, 256))
-    for t in (0, 2, 1, 3):
-        ts(R("OFF", 16 * t, 16 * t + 16), own("YB", 256), 4.0, float(t), A.mult, A.add)
+    cp(x("OFY"), own("YB", 256))
     for t in range(4):
-        o, a = R("FA", t, W64, 4), R("XT", 0, 784, 1, R("OFF", 16 * t, 16 * t + 16))
+        o, a = R("FA", t, W64, 4), R("XP%d" % t, 0, 208, 1, x("OFY"))
         if t < 2:
             act(o, a)
         else:
             cp(o, a)
-    cp(x("OFY"), own("YB", 256))
 
     F, Fn = "FA", "FB"
     K, Kn = "KA", "KB"
     keys = R("SC", 0, 208, 1, x("OFY"))
     hu = x("HU", 0, 12)
-    h0, h1 = R("CSP", 15, 256, 16), R("CSP", 31, 272, 16)
+    h0, h1 = x("HB", 0, 16), x("HB", 1, 17)
     r0, r1 = x("RB", 0, 16), x("RB", 1, 17)
     nsel = R("S1A", 3, 64, 4)
+
+    def places(a, b, skip=False):
+        if not skip:
+            cp(R("HR", 0, 640, 1, x("QD", a, b)), IOTA(16 * a, 16 * b))
 
     for r in range(ROUNDS):
         last = r == ROUNDS - 1
@@ -433,122 +457,161 @@ def rank_program(g, core, T, topo):
         quant("QF", "QFS", F, 256)
         for b in range(4):
             mm("PS%d" % b, "WQ", "WS", "QF", "QFS", 256, 128 * b)
-        if r == 0:
-            act(R("GI", 0, 384), R(F, 0, 384), COPY, 64.0)
-            ts(R("GI", 384, W64), R(F, 384, W64), 64.0, None, A.mult)
-        else:
-            act(R("GI", 0, W64), R(F, 0, W64), COPY, 64.0)
-            cp(R("HR", 0, 640, 1, x("QD")), IOTA(0, 256))
         for b in range(4):
+            act(R("GI", b, W64, 4), R(F, b, W64, 4), COPY, 64.0)
+        if r == 0:
+            tt(R("CF", 0, 256), R("XWS", 0, 256), R("SRC", 0, 256), A.add)
+        else:
+            places(8, 16)
+        for b in range(3):
             tt(R("AD%d" % b, 0, 256), R("PS%d" % b, 0, 256), R("GI", b, W64, 4), A.add)
             if b < 2:
                 act(R("TI", b, W64, 4), R("AD%d" % b, 0, 256), COPY, 0.015625)
-        for b in (2, 3):
-            ts(R("TI", b, W64, 4), R("AD%d" % b, 0, 256), 0.015625, None, A.mult)
+        for h in range(2):
+            tt(R("AD3", 128 * h, 128 * h + 128), R("PS3", 128 * h, 128 * h + 128), R("GI", 512 * h + 3, 512 * h + 512, 4), A.add)
+        ts(R("TI", 2, W64, 4), R("AD2", 0, 256), 0.015625, None, A.mult)
+        for h in range(2):
+            ts(R("TI", 512 * h + 3, 512 * h + 512, 4), R("AD3", 128 * h, 128 * h + 128), 0.015625, None, A.mult)
+        if r > 0:
+            scan(R("YS", 0, 192), R("CF", 0, 192), R("HR", 0, 192), A.add, A.max)
 
-        quant(qt, qts, "TI", 256)
-        mm("PP", "UR", "URS", qt, qts)
+        for h, p in enumerate(("PP", "PQ")):
+            quant(qt, qts, "TI", 128, 512 * h, 128 * h)
+            mm(p, "UR", "URS", qt, qts, 128, 0, 128 * h)
         send_codes(lq, ls, qt, qts, 256, "aq%d" % r)
         act(R(K, 0, 256), keys)
-        act(R("PR", 0, 256), R("PP", 0, 256))
+        act(R("PR", 0, 128), R("PP", 0, 128))
         if r == 0:
-            for b in range(4):
-                quant("EQ%d" % b, "EQS%d" % b, "EB" if b % 2 else "EA", 128, 2 - b // 2 * 2)
+            act(R("CFB", 0, 256), R("CF", 0, 256), COPY, 1.0 / 64)
         else:
-            fold(hu, "YS", "HR", 192)
-        tt(R("TMP", 0, 192), R("PR", 0, 256, 1, hu), R("DMASK", 0, 192), A.min)
+            ts(hu, own("YS"), x("OFS", 0, 1), None, A.add)
+        cp(R("PR", 128, 256), R("PQ", 0, 128))
         act(R("SC", 0, 192), R("PR", 0, 256, 1, hu))
-        ranks()
-        mm("PQ", "UP", "UPS", lq, ls)
-        for b, p in enumerate(("PD0", "PD1", "PS2", "PS3")):
-            mm(p, "EQ%d" % b, "EQS%d" % b, lq, ls)
-        if r == 0:
-            tables_d()
-            lists()
-        act(R(K, 256, 512), R("PQ", 0, 256))
+        ranks("SC", lambda a: R("PR", 0, 256, 1, x("HU", a // 16, a // 16 + 6)))
         ranks_end()
-        cp(R("LROW", 0, 192, 1, x("RKU", 0, 12)), R("HR", 0, 192))
-        fold(R(lw, 0, 4), "LL", "LROW", 64)
-        send(R(lp, 0, 4), R(lw, 0, 4), "al%d" % r)
-
-        def unpack(b):
-            act(R("AD%d" % b, 256, 512), R(("PD0", "PD1", "PS2", "PS3")[b], 0, 256), COPY, 64.0)
-
-        unpack(0)
-        unpack(1)
-        unpack(2)
         lpo = R(lp, 0, 4)
         arr = R(K, 256, 512, 1, lpo)
 
+        def units(b):
+            if r == 0:
+                quant("EQ%d" % b, "EQS%d" % b, "EB" if b % 2 else "EA", 128, 2 - b // 2 * 2)
+
+        def unpack(b):
+            p = ("PD0", "PD1", "PS2", "PS3")[b]
+            mm(p, "EQ%d" % b, "EQS%d" % b, lq, ls)
+            act(R("AD%d" % b, 256, 512), R(p, 0, 256), COPY, 64.0)
+
         def before(c):
             ts(R("CMN", 208 * c, 208 * c + 192), R("KST", 0, 192), R("AOS", 16 * c + 15, 16 * c + 16), None, A.is_le)
-            total(x("TTA", c, c + 1), R("CMN", 208 * c, 208 * c + 193), 193)
+            if c >= 4 - SUMS_ON_SCALAR:
+                total(x("TTA", c, c + 1), R("CMN", 208 * c, 208 * c + 193), 193)
 
-        cp(R(K, 0, 256, 1, R(lw, 0, 4)), R("BIGS", 0, 64))
-        act(R("KST", 0, 192), R(K, 0, 256, 1, hu))
-        unpack(3)
+        def before_sum(c):
+            if c < 4 - SUMS_ON_SCALAR:
+                red(x("TTA", c, c + 1), R("CMN", 208 * c, 208 * c + 193), A.add)
+
+        def behind(c):
+            if c < SIGNS_ON_VECTOR:
+                ts(R("CMQ", 64 * c, 64 * c + 64), R("NR", 0, 64), x("IW5", c, c + 1), 2.0, A.is_lt, A.mult)
+
+        def behind_sum(c):
+            if c < SIGNS_ON_VECTOR:
+                red(x("AC", c, c + 1), R("CMQ", 64 * c, 64 * c + 64), A.add)
+
+        units(0)
+        cp(R("LROW", 0, 192, 1, x("RKU", 0, 12)), R("HR", 0, 192))
+        act(R("FLT", 0, 192), R("STEP", 0, 192, 1, x("RKU", 0, 12)))
+        act(R("SFP", 0, 256), R("FLT", 0, 640, 1, x("QD")))
+        mm("PQ", "UP", "UPS", lq, ls)
+        act(R(K, 256, 512), R("PQ", 0, 256))
+        units(1)
+        scan(R("LL", 0, 64), R("CF", 0, 64), R("LROW", 0, 64), A.add, A.max)
+        units(2)
+        ts(R(lw, 0, 4), own("LL", 64), x("OFS", 0, 1), None, A.add)
+        send(R(lp, 0, 4), R(lw, 0, 4), "al%d" % r)
+        units(3)
         if last:
             quant("QVC", "QVS", "VT", 128)
-        ts(R("SFP", 0, 256), R(K, 0, 256), BIG / 2, None, A.is_lt)
+        scan(R("CSP", 0, 256), ONE(256), R("SFP", 0, 256))
+        cp(R(K, 0, 256, 1, R(lw, 0, 4)), R("BIGS", 0, 64))
+        act(R("KST", 0, 192), R(K, 0, 256, 1, hu))
+        unpack(0)
+        unpack(1)
+        scan(R("TMB", 0, 256), R("CFB", 0, 256), R("CSP", 0, 256), A.add, A.max)
+        scan(R("YB", 0, 256), R("CFB", 0, 256), R("SFP", 0, 256), A.add, A.max)
+        tt(h1, own("CSP", 256), x("C12P"), A.subtract)
+        tt(x("P2"), own("TMB", 256), x("CT"), A.add)
+        tt(x("P1"), own("YB", 256), x("T1"), A.mult)
         scan(R("LBK", 0, 256), R(K, 0, 256), R("LBM", 0, 256), A.min, A.max, BIG)
-        tt(R("TMY", 0, 256), R("SFP", 0, 256), R("TRIW", 0, 256), A.mult)
-        scan(R("CSP", 16, 272), R("C75", 0, 256), R("SFP", 0, 256), A.add, A.add)
-        scan(R("XWS", 0, 256), RST(256), R("TMY", 0, 256))
+        tt(x("TB"), x("P2"), x("P1"), A.subtract)
         tt(x("HC"), h1, h0, A.subtract)
-        act(R("ARS", 0, 64), IOTA(256, 512, lpo))
+        cp(x("TBU"), x("TB"))
+        tt(x("WT"), x("TB"), h0, A.subtract)
+        cp(R("SRC", 0, 640, 1, x("TBU")), IOTA(0, 256))
         tt(R("TMP", 0, 64), arr, MASK(64), A.mult)
         ts(R("ARC", 0, 64), arr, R("LBK", 255, 256), None, A.is_lt)
-        tt(x("WT"), own("XWS", 256), x("CT"), A.add)
         scan(R("AOS", 0, 64), RST(64), R("TMP", 0, 64))
         red(x("AR1", 0, 1), R("ARC", 0, 64), A.add)
-        tt(x("TB"), x("WT"), h0, A.add)
-        before(0)
-        cp(x("AU", 0, 1), x("AR1", 0, 1))
-        before(1)
-        tt(r1, IOTA(0, 72, x("AU", 0, 1)), h1, A.add)
-        before(2)
-        tt(x("CN"), r1, r0, A.subtract)
+        act(R("ARS", 0, 64), IOTA(256, 512, lpo))
         before(3)
+        cp(x("AU", 0, 1), x("AR1", 0, 1))
+        before(2)
+        tt(r1, IOTA(0, 72, x("AU", 0, 1)), h1, A.add)
+        before(1)
+        tt(x("CN"), r1, r0, A.subtract)
+        before(0)
         scan(x("S4"), x("RST4"), x("CN"), A.mult, A.max)
-        tt(R("X4", 0, 64), R("RB", 0, 24, 1, x("L4", 0, 4)), R("C4", 0, 64), A.mult)
-        ts(x("TBU"), x("TB"), -WHOLE, None, A.add)
+        before_sum(1)
+        before_sum(0)
+        unpack(2)
         ts(nsel, R("S4", 0, 16, 1, x("AL", 0, 1)), 2.5, -1.0, A.is_gt, A.mult)
-        tt(x("CN4", 0, 4), x("RB", 4, 17, 4), x("RB", 0, 13, 4), A.subtract)
+        tt(R("X4", 0, 64), R("RB", 0, 24, 1, x("L4", 0, 4)), R("C4", 0, 64), A.mult)
         cp(x("TU", 8, 12), x("TTA", 0, 4))
+        tt(x("CN4", 0, 4), x("RB", 4, 17, 4), x("RB", 0, 13, 4), A.subtract)
         tt(x("AX"), x("CN"), x("HC"), A.subtract)
         scan(R("O1", 0, 64), R("S1A", 0, 64), R("X4", 0, 64))
-        tt(x("ZX", 0, 4), x("CN4", 0, 4), R("S1A", 3, 64, 16), A.mult)
         tt(R("NR", 0, 64), IOTA(0, 192, x("TU", 8, 12)), R("J64", 0, 64), A.subtract)
-        for c in range(8):
+        for c in range(SIGNS_ON_VECTOR, 8):
             total(x("AC", c, c + 1), R("NR", 0, 64), 64, x("IW5", c, c + 1))
-        red(x("ZM", 0, 1), x("ZX", 0, 4), A.min)
+        unpack(3)
+        tt(x("ZX", 0, 4), x("CN4", 0, 4), R("S1A", 3, 64, 16), A.mult)
         tt(R("X8", 0, 128), R("O1", 0, 72, 1, x("L8", 0, 8)), R("C8", 0, 128), A.mult)
+        red(x("ZM", 0, 1), x("ZX", 0, 4), A.min)
+        for c in range(3):
+            behind(c)
         ts(R("S2A", 2, 128, 4), x("C45", 0, 32), x("ZM", 0, 1), None, A.is_lt)
-        cp(R("SEQ", 0, 192, 1, x("TU", 8, 12)), R("ARS", 0, 64))
+        for c in range(3):
+            behind_sum(c)
         scan(R("O2", 0, 640, 5), R("S2A", 0, 128), R("X8", 0, 128))
-        tt(x("NI"), x("AX"), nsel, A.subtract)
-        tt(R("O2", 23, 640, 40), x("WT"), r0, A.add)
-        tt(R("O2", 31, 640, 40), x("WT"), r0, A.add)
+        tt(x("TTS", 0, 7), x("AC", 0, 7), x("C2I", 0, 7), A.add)
         tt(R("S3A", 1, 80, 5), R("O2", 35, 640, 40), R("O2", 15, 640, 40), A.is_le)
-        ts(R("S3A", 3, 80, 5), x("NI"), R("S2A", 2, 3), -1.0, A.is_ge, A.mult)
-        cp(R("SRC", 0, 640, 1, x("TBU")), IOTA(0, 256))
+        tt(x("NI"), x("AX"), nsel, A.subtract)
+        tt(R("O2", 39, 640, 40), x("WT"), r0, A.add)
+        ts(x("TU", 0, 7), x("TTS", 0, 7), 0.5, None, A.mult)
+        ts(x("TU", 7, 8), x("AC", 7, 8), x("C2I", 7, 8), 0.5, A.add, A.mult)
+        ts(R("S3A", 4, 80, 5), x("NI"), R("S2A", 2, 3), -1.0, A.is_ge, A.mult)
+        tt(R("O2", 31, 640, 40), x("WT"), r0, A.add)
         if last:
             act(R("OLT", 0, 512), IOTA(0, 512))
             act(R("OLT", 512, 528), ONE(16), COPY, -1.0)
-        tt(x("TTS", 0, 8), x("AC", 0, 8), x("C2I", 0, 8), A.add)
+        cp(R("SEQ", 0, 192, 1, x("TU", 8, 12)), R("ARS", 0, 64))
         scan(R("O3", 0, 80), R("S3A", 0, 80), R("O2", 7, 640, 8))
-        ts(x("TU", 0, 8), x("TTS", 0, 8), 0.5, None, A.mult)
-        ts(x("QD"), R("O3", 3, 80, 5), -WHOLE, None, A.add)
         cp(R("SEQ", 0, 192, 1, x("TU", 0, 8)), R("SRC", 0, 128))
+        cp(x("QD"), R("O3", 4, 80, 5))
         cp(R("TMY", 0, 128), R("SEQ", 0, 640, 1, x("QD", 0, 8)))
         act(R("TMY", 128, 256), R("SEQ", 0, 640, 1, x("QD", 8, 16)))
-        fold(x("OFY"), "YS", "TMY", 256)
+        places(0, 2, last)
+        scan(R("YS", 0, 256), R("CF", 0, 256), R("TMY", 0, 256), A.add, A.max)
+        places(2, 4, last)
+        ts(x("OFY"), own("YS", 256), x("OFS", 0, 1), None, A.add)
+        places(4, 6, last)
         for t in range(4):
             o, a = R(Fn, t, W64, 4), R("AD%d" % t, 0, 528, 1, x("OFY"))
             if t < 2:
                 act(o, a, COPY, 0.015625)
             else:
                 ts(o, a, 0.015625, None, A.mult)
+        places(6, 8, last)
         keys = R(K, 0, 528, 1, x("OFY"))
         F, Fn, K, Kn = Fn, F, Kn, K
 
@@ -559,16 +622,18 @@ def rank_program(g, core, T, topo):
         emit(q, lambda: Q[q].dma_start(dst, src), [], [a], ("dout", 16 * stored[0], 16))
 
     quant("QF", "QFS", F, 256)
-    mm("PP", "QVC", "QVS", "QF", "QFS")
+    for h, p in enumerate(("PP", "PQ")):
+        mm(p, "QVC", "QVS", "QF", "QFS", 128, 0, 128 * h)
     cp(R("OLT", 256, 512, 1, lpo), IOTA(256, 320))
-    cp(R("YO", 0, 256), R("PP", 0, 256))
-    act(R("OLR", 0, 256), R("OLT", 0, 528, 1, x("OFY")))
+    act(R("YO", 0, 128), R("PP", 0, 128))
+    cp(R("YO", 128, 256), R("PQ", 0, 128))
+    cp(R("OLR", 0, 256), R("OLT", 0, 528, 1, x("OFY")))
     qf = R("QF", 0, 256, 1, None, dt.uint8)
     store("y", T.oc[:, 0:W64], qf, ap(qf))
     for k in range(4):
         store("y", T.osc[4 * k:4 * k + 4, 0:256], R("QFS", 0, 256), T.QFS[32 * k:32 * k + 4, 0:256])
-    store("y", T.y[:, 0:256], R("YO", 0, 256), ap(R("YO", 0, 256)))
-    store("s", T.ol[:, 0:256], R("OLR", 0, 256), T.OLR[0:128:16, 0:256])
+    store("s", T.y[:, 0:256], R("YO", 0, 256), ap(R("YO", 0, 256)))
+    store("y", T.ol[:, 0:256], R("OLR", 0, 256), T.OLR[0:128:16, 0:256])
 
     for q in ("v", "s", "t", "g"):
         if known["g"].get(q, 0) < cnt[q]:

@@ -13,7 +13,7 @@ UP_ = 0.5 - 1.0 / 512
 WHOLE = 1.5 * 2.0 ** 23
 ON_SCALAR = 10
 SUMS_ON_SCALAR = 3
-SIGNS_ON_VECTOR = 3
+SIGNS_ON_VECTOR = 2
 
 SCRATCH = {}
 
@@ -44,16 +44,15 @@ _decl("PS0 PS1 PS2 PS3 PP PQ PD0 PD1", "psum", [128, 512], "float32")
 _decl("IOTA", "sbuf", [128, 512], "float32")
 _decl("KA KB OLT", "sbuf", [128, 528], "float32")
 _decl("SRC SEQ HR O2", "sbuf", [128, 640], "float32")
-_decl("JM MASK DMASK RMIN TRIW LBM LBK TMP TMY YS PR XWS OLR YO", "sbuf", [128, 256], "float32")
+_decl("JM MASK DMASK RMIN LBM LBK TMP TMY YS PR OLR YO", "sbuf", [128, 256], "float32")
 _decl("SEQS SC", "sbuf", [128, 208], "float32")
-_decl("Z LROW KST", "sbuf", [128, 192], "float32")
+_decl("Z LROW KST KAT", "sbuf", [128, 192], "float32")
 _decl("CF", "sbuf", [128, 256], "float32")
-_decl("ARS", "sbuf", [128, 64], "float32")
-_decl("C8 X8 S2A", "sbuf", [128, 128], "float32")
+_decl("C8 X8 S2A A8 B8", "sbuf", [128, 128], "float32")
 _decl("O1 S3A O3", "sbuf", [128, 80], "float32")
 _decl("LL AOS ARC BIGS NR C4 X4 S1A J64", "sbuf", [128, 64], "float32")
 SMALL = ("RB C1C C12 IW M16 M17 CNT RK KI0 ENC INV EN2 SP AR1 RST4 CN S4 CN4 ZX ZM C45 HC WT TB CT AX NI TTA AC C2I TTS IW5 "
-         "S16 S161 N16 N161 CA CB PA PB PC PD C4C C8C LB0 OFS O16 O17 T1 C12P P1 P2 HB HW").split()
+         "S16 S161 N16 N161 CA CB PA PB PC PD C4C C8C LB0 OFS O16 O17 T1 C12P P1 P2 P3 P4 C32 HB HW").split()
 _decl("SMALLS", "sbuf", [128, 32 * len(SMALL)], "float32")
 _decl("INTS", "sbuf", [128, 16 * 11], "int32")
 _decl("LW0 LW1 LW2 LP0 LP1 LP2", "sbuf", [128, 4], "uint16")
@@ -61,7 +60,7 @@ _decl("LISTS", "sbuf", [128, 16 * 12], "uint16")
 _decl("XP0 XP1 XP2 XP3", "sbuf", [128, 208], "bfloat16")
 _decl("CMQ", "sbuf", [128, 512], "bfloat16")
 _decl("STEP", "sbuf", [128, 192], "float32")
-_decl("FLT", "sbuf", [128, 640], "float32")
+_decl("FLT", "sbuf", [128, 640], "bfloat16")
 PIECE = {n: ("SMALLS", 32 * i) for i, n in enumerate(SMALL)}
 PIECE.update({n: ("INTS", 16 * i) for i, n in enumerate("PI SI I2 I3 I4 I8 KI KA4 KB4 UI H3".split())})
 PIECE.update({n: ("LISTS", 16 * i) for i, n in enumerate("RKU HU QV0 QD TU TBU AL UL OFY AU L4 L8".split())})
@@ -242,8 +241,8 @@ def rank_program(g, core, T, topo):
         lands("aq%d" % r, 2 * engines, [R("LQ%d" % r, 0, 256), R("LS%d" % r, 0, 256)])
         lands("al%d" % r, engines, [R("LP%d" % r, 0, 4)])
 
+    load("y", R("UT", 0, 512), T.u[:], "du")
     load("y", R("XT", 0, 768), T.x[:], "dx")
-    load("s", R("UT", 0, 512), T.u[:], "du")
     load("y", R("WQ", 0, 512, 1, None, dt.uint8), T.wc[:], "dw")
     load("y", R("WS", 0, 512), T.ws[:], "dws")
     load("y", R("VT", 0, 512), T.v[:], "dv")
@@ -264,30 +263,48 @@ def rank_program(g, core, T, topo):
     iota(R("JM", 0, 256), [[0, 16], [1, 16]])
     iota(x("UI", 0, 8), [[16, 8]])
     iota(x("M16"), [[16, 16]])
-    iota(x("C12"), [[12, 16]])
     iota(x("C4C", 0, 4), [[4, 4]])
     iota(x("C8C", 0, 8), [[8, 8]])
-    iota(x("C1C"), [[0, 4], [1, 4]])
+    fill(ONE(528), 1.0)
+    for k, c in enumerate((2, -2, 96, 0)):
+        iota(R("B8", k, 128, 4), [[0, 32]], c)
+    for k, (pattern, c) in enumerate((([[0, 16], [2, 2]], 0), ([[0, 16], [-2, 2]], 32), ([[1536, 16], [96, 2]], 63), ([[0, 32]], 0))):
+        iota(R("A8", k, 128, 4), pattern, c)
     for b in range(4):
         const("XP%d" % b, (192, 208), 0)
-    fill(ONE(528), 1.0)
-    iota(R("HR", 0, 192), [[4, 64], [1, 3]])
-    iota(R("S1A", 0, 64), [[0, 16], [1, 4]])
-    iota(R("S2A", 0, 128), [[0, 64], [1, 2]])
-    iota(R("J64", 0, 64), [[1, 64]])
-    const("S3A", (0, 80), 0)
-    const("RB", (0, 24), 0)
-    const("O1", (64, 68), 0)
-    const("O1", (68, 72), 1)
-    const("C4", (0, 64), 1)
-    const("HB", (0, 8), 0)
-    const("FLT", (192, 640), 0)
-    const("SEQ", (192, 640), 512)
-    for b in range(4):
-        const("AD%d" % b, (512, 528), 0)
-    for n, b in (("EA", 2), ("EB", 3)):
-        o = R(n, 0, 516)
-        emit("g", lambda: g.affine_select(ap(o), ap(ONE(516)), [[-1, 516]], A.is_equal, 0.0, b, 4), [o], [ONE(516)])
+
+    def later_constants():
+        iota(R("HR", 0, 192), [[4, 64], [1, 3]])
+        for b in range(4):
+            const("AD%d" % b, (512, 528), 0)
+        for n, b in (("EA", 2), ("EB", 3)):
+            o = R(n, 0, 516)
+            emit("g", lambda: g.affine_select(ap(o), ap(ONE(516)), [[-1, 516]], A.is_equal, 0.0, b, 4), [o], [ONE(516)])
+        const("STEP", (0, 64), 0)
+        const("STEP", (64, 192), 1)
+        const("FLT", (192, 640), 0)
+        const("SEQ", (192, 640), 512)
+        iota(R("S2A", 0, 128), [[0, 64], [1, 2]])
+        iota(R("J64", 0, 64), [[1, 64]])
+
+    def last_constants():
+        iota(x("C12P"), [[12, 16]], 12)
+        iota(x("C32", 0, 8), [[32, 8]], 80)
+        const("HB", (0, 8), 0)
+        const("RB", (0, 24), 0)
+        const("HC", (0, 8), 0)
+        iota(x("RST4"), [[0, 4], [1000, 4]])
+        const("C4", (0, 64), 4)
+        iota(R("C4", 0, 64, 4), [[0, 4], [1, 4]])
+        iota(R("C4", 1, 64, 4), [[0, 4], [-1, 4]], 4)
+        iota(R("S1A", 0, 64), [[0, 16], [1, 4]])
+        iota(R("S1A", 2, 64, 4), [[0, 16]], -1)
+        const("O1", (64, 68), 0)
+        const("O1", (68, 72), 1)
+        const("C45", (0, 32), -5)
+        iota(R("S3A", 0, 80), [[0, 16], [2, 5]], -5)
+        iota(R("S3A", 0, 80, 5), [[0, 16]])
+        iota(R("O2", 23, 640, 40), [[0, 16]], int(WHOLE))
 
     scan(IOTA(0, 512), ONE(512), ONE(512), A.mult, A.add, -1.0)
     ts(x("SI", 0, 1), x("PI", 0, 1), 15, None, A.bitwise_and)
@@ -301,93 +318,70 @@ def rank_program(g, core, T, topo):
     act(R("DMASK", 0, 192), MASK(192), IDENT, 2 * BIG, -BIG)
 
     def tables_a():
-        act(x("LB0", 0, 1), s, IDENT, 16.0, 15.5)
-        act(x("S16", 0, 1), s, COPY, 1.0 / 16)
-        act(x("N16", 0, 1), s, IDENT, -1.0 / 16, 1.0)
-        act(x("S161", 0, 1), s, IDENT, 1.0 / 16, 1.0 / 16)
-        act(x("N161", 0, 1), s, IDENT, -1.0 / 16, 15.0 / 16)
-        act(x("CA", 0, 1), s, IDENT, 0.75, UP_)
-        act(x("CB", 0, 1), s, IDENT, 0.75, 0.75 + UP_)
-        act(R("LBM", 0, 256), IOTA(0, 256), SIGN, -1.0, x("LB0", 0, 1))
-        act(R("SC", 192, 208), ONE(16), COPY, BIG)
-        act(R("XWS", 0, 256), MASK(256), COPY, -4096.0)
-        act(R("SRC", 0, 1), ONE(1), COPY, 0.0)
-        act(R("SRC", 1, 257), MASK(256), COPY, 1024.0)
-
-    def tables_b():
-        for i, n in ((0, "S16"), (1, "N16"), (4, "S161"), (5, "N161")):
-            act(R("C8", i, 128, 8), ONE(16), COPY, x(n, 0, 1))
-        act(R("C8", 2, 128, 8), x("C12"), IDENT, 1.0, x("CA", 0, 1))
-        act(R("C8", 6, 128, 8), x("C12"), IDENT, 1.0, x("CB", 0, 1))
-        act(R("C8", 3, 128, 4), ONE(32), COPY, WHOLE)
-        act(R("LBM", 0, 256), R("LBM", 0, 256), COPY, BIG)
+        act(R("CF", 0, 256), MASK(256), IDENT, -33.0 * 1024, 1024.0)
+        act(R("CFB", 0, 256), MASK(256), IDENT, -65.0, 1.0)
+        act(R("LBM", 0, 256), IOTA(0, 256), IDENT, -BIG / 2, x("LB0", 0, 1))
+        act(R("X8", 0, 128), R("B8", 0, 128), COPY, s)
 
     def tables_c():
-        act(R("BIGS", 0, 64), ONE(64), COPY, BIG)
-        for n in ("KA", "KB"):
-            act(R(n, 512, 528), ONE(16), COPY, BIG)
         act(R("CMN", 192, 4 * 208, 208), x("IW", 0, 4))
         act(x("IW5", 0, 8), x("IW", 0, 8), IDENT, 1.0, 0.5)
         act(x("C2I", 0, SIGNS_ON_VECTOR), x("IW", 0, SIGNS_ON_VECTOR), COPY, 2.0)
         act(x("C2I", SIGNS_ON_VECTOR, 8), x("IW", SIGNS_ON_VECTOR, 8), IDENT, 2.0, 64.0)
-        act(x("RST4"), x("C1C"), SIGN)
-        act(R("STEP", 0, 64), ONE(64), COPY, 0.0)
-        act(R("STEP", 64, 192), ONE(128))
-
-    def tables_d():
-        act(x("O17", 0, 1), x("O16", 0, 1), IDENT, 1.0, 1.0)
-        act(x("T1"), x("IW"), IDENT, 1.0, 192.0)
-        act(x("C12P"), x("C12"), IDENT, 1.0, 12.0)
-        act(x("CT"), x("T1"), COPY, x("O17", 0, 1))
         act(x("T1"), x("IW"), IDENT, 1.0, 193.0)
-        act(R("C4", 0, 64, 4), x("C1C"), COPY, 0.25)
-        act(R("C4", 1, 64, 4), x("C1C"), IDENT, -0.25, 1.0)
-        act(R("S1A", 2, 64, 4), ONE(16), COPY, -1.0)
-        act(R("S3A", 2, 80, 5), ONE(16), COPY, -1.0)
         act(R("O2", 7, 640, 40), x("IW"), IDENT, 1.0, 192.0)
-        act(R("O2", 23, 640, 40), ONE(16), COPY, WHOLE)
-        act(R("S3A", 3, 80, 5), ONE(16))
-        act(x("C45", 0, 32), ONE(32), COPY, -4.5)
+        act(R("C8", 0, 128), R("A8", 0, 128), COPY, 1.0 / 128)
 
-    def lists():
-        ts(x("OFS", 0, 1), s, 14.5, -1024.0, A.is_lt, A.mult)
-        ts(x("O16", 0, 1), s, 14.5, 16.0, A.is_lt, A.mult)
-        ts(x("I2", 0, 1), x("SI", 0, 1), 12, None, A.bitwise_and)
-        ts(x("I3", 0, 1), x("SI", 0, 1), 3, None, A.bitwise_and)
-        ts(x("I4", 0, 1), x("SI", 0, 1), 2, None, A.arith_shift_right)
-        ts(x("I8", 0, 1), x("SI", 0, 1), 8, None, A.bitwise_and)
-        ts(x("AL", 0, 1), x("I2", 0, 1), 3.0, None, A.add)
-        ts(x("PA", 0, 1), x("I3", 0, 1), 0.0, 4.0, A.is_equal, A.mult)
-        ts(x("PB", 0, 1), x("I3", 0, 1), 1.5, None, A.is_gt)
-        ts(x("PD", 0, 1), x("I3", 0, 1), 1.5, None, A.is_lt)
-        ts(x("PC", 0, 1), x("I8", 0, 1), 0.5, -65.0, A.mult, A.add)
-        ts(x("INV", 0, 1), x("I4", 0, 1), x("PB", 0, 1), x("PA", 0, 1), A.mult, A.add)
-        ts(x("EN2", 0, 8), x("C8C", 0, 8), x("PC", 0, 1), x("PA", 0, 1), A.add, A.add)
-        ts(x("L4", 0, 4), x("C4C", 0, 4), x("INV", 0, 1), None, A.add)
-        ts(x("L8", 0, 8), x("EN2", 0, 8), x("PD", 0, 1), 68.0, A.mult, A.add)
+    spare = [
+        lambda: fill(R("KA", 512, 528), BIG),
+        lambda: fill(R("KB", 512, 528), BIG),
+        lambda: tt(R("A8", 0, 128), R("A8", 0, 128), R("X8", 0, 128), A.add),
+        lambda: ts(x("PA", 0, 1), x("I3", 0, 1), 0.0, 4.0, A.is_equal, A.mult),
+        lambda: ts(x("PB", 0, 1), x("I3", 0, 1), 1.5, None, A.is_gt),
+        lambda: ts(x("PC", 0, 1), x("I8", 0, 1), 0.5, -65.0, A.mult, A.add),
+        lambda: ts(x("PD", 0, 1), x("I3", 0, 1), 1.5, None, A.is_lt),
+        lambda: ts(x("AL", 0, 1), x("I2", 0, 1), 3.0, None, A.add),
+        lambda: ts(x("INV", 0, 1), x("I4", 0, 1), x("PB", 0, 1), x("PA", 0, 1), A.mult, A.add),
+        lambda: ts(x("EN2", 0, 8), x("C8C", 0, 8), x("PC", 0, 1), x("PA", 0, 1), A.add, A.add),
+        lambda: ts(x("CT"), x("IW"), 192.0, x("O17", 0, 1), A.add, A.mult),
+        lambda: ts(x("L4", 0, 4), x("C4C", 0, 4), x("INV", 0, 1), None, A.add),
+        lambda: ts(x("L8", 0, 8), x("EN2", 0, 8), x("PD", 0, 1), 68.0, A.mult, A.add),
+        lambda: fill(R("C8", 3, 128, 4), WHOLE),
+    ]
 
-    lists()
+    def meanwhile(n):
+        for _ in range(min(n, len(spare))):
+            spare.pop(0)()
+
+    ts(x("LB0", 0, 1), s, 15.5 / 16, 8 * BIG, A.add, A.mult)
     cp(x("KI"), x("IW"))
-    fill(R("SEQS", 192, 208), 192.0)
     ts(x("H3"), x("IW"), 1.0 / 3, -1.0 / 3, A.mult, A.add)
+    ts(x("OFS", 0, 1), s, -15.0, 1024.0, A.add, A.mult)
+    ts(x("O17", 0, 1), s, -1.0, 16.0, A.mult, A.add)
     ts(x("KA4"), x("KI"), 2, None, A.arith_shift_right)
     ts(x("KB4"), x("KI"), 3, None, A.bitwise_and)
-    tables_a()
-    quant("QU", "QUS", "UT", 128)
     tt(x("M17"), x("IW"), x("H3"), A.add)
+    fill(R("SEQS", 192, 208), 192.0)
     ts(x("KI0"), x("KA4"), 3.0, -192.0, A.mult, A.add)
     ts(x("INV"), x("KB4"), 2.5, None, A.is_lt)
+    for n, k, op in (("I2", 12, A.bitwise_and), ("I3", 3, A.bitwise_and), ("I4", 2, A.arith_shift_right), ("I8", 8, A.bitwise_and)):
+        ts(x(n, 0, 1), x("SI", 0, 1), k, None, op)
+    tables_a()
+    quant("QU", "QUS", "UT", 128)
+    tt(x("ENC"), x("KI0"), x("KB4"), A.add)
+    cp(x("HU", 0, 12), x("M17", 0, 12))
     cp(R("UR", 0, 128, 1, None, dt.uint32), R("QU", 0, 128, 1, R("UL", 0, 8), dt.uint32))
-    act(R("URS", 0, 128), R("QUS", 0, 128, 1, R("UL", 0, 8)))
+    cp(R("URS", 0, 128), R("QUS", 0, 128, 1, R("UL", 0, 8)))
     quant("QX", "QXS", "XT", 192)
     mm("PP", "UR", "URS", "QX", "QXS", 192)
     send_codes("UP", "UPS", "UR", "URS", 128, "au")
+    later_constants()
     for b in range(4):
         act(R("XP%d" % b, 0, 192), R("XT", b, 768, 4))
-    tables_b()
-    tt(x("ENC"), x("KI0"), x("KB4"), A.add)
-    cp(x("HU", 0, 12), x("M17", 0, 12))
     tt(x("EN2"), x("ENC"), x("INV"), A.mult)
+    fill(R("SC", 192, 208), BIG)
+    fill(R("BIGS", 0, 64), BIG)
+    ts(x("QD"), x("EN2"), 192.0, None, A.add)
 
     def ranks(row, diag):
         for a in (0, 96):
@@ -424,14 +418,17 @@ def rank_program(g, core, T, topo):
 
     ranks("PP", lambda a: R("PP", a, a + 96))
     act(R("SC", 0, 192), R("PP", 0, 192))
-    ts(x("QD"), x("EN2"), 192.0, None, A.add)
     ranks_end()
-    tables_c()
-    tables_d()
+    meanwhile(2)
     cp(R("SEQS", 0, 192, 1, x("RKU", 0, 12)), IOTA(0, 192))
+    meanwhile(1)
+    tables_c()
     tt(R("TMB", 0, 256), R("SEQS", 0, 208, 1, x("QD")), MASK(256), A.mult)
+    meanwhile(2)
     scan(R("YB", 0, 256), RST(256), R("TMB", 0, 256))
+    meanwhile(2)
     cp(x("OFY"), own("YB", 256))
+    meanwhile(2)
     for t in range(4):
         o, a = R("FA", t, W64, 4), R("XP%d" % t, 0, 208, 1, x("OFY"))
         if t < 2:
@@ -447,6 +444,13 @@ def rank_program(g, core, T, topo):
     r0, r1 = x("RB", 0, 16), x("RB", 1, 17)
     nsel = R("S1A", 3, 64, 4)
 
+    def pick(t, a, b):
+        o, w = R(Fn, 64 * a + t, 64 * b, 4), R("AD%d" % t, 0, 528, 1, x("OFY", a, b))
+        if t < 2:
+            act(o, w, COPY, 0.015625)
+        else:
+            ts(o, w, 0.015625, None, A.mult)
+
     def places(a, b, skip=False):
         if not skip:
             cp(R("HR", 0, 640, 1, x("QD", a, b)), IOTA(16 * a, 16 * b))
@@ -459,10 +463,8 @@ def rank_program(g, core, T, topo):
             mm("PS%d" % b, "WQ", "WS", "QF", "QFS", 256, 128 * b)
         for b in range(4):
             act(R("GI", b, W64, 4), R(F, b, W64, 4), COPY, 64.0)
-        if r == 0:
-            tt(R("CF", 0, 256), R("XWS", 0, 256), R("SRC", 0, 256), A.add)
-        else:
-            places(8, 16)
+        places(8, 16, r == 0)
+        meanwhile(5)
         for b in range(3):
             tt(R("AD%d" % b, 0, 256), R("PS%d" % b, 0, 256), R("GI", b, W64, 4), A.add)
             if b < 2:
@@ -472,8 +474,6 @@ def rank_program(g, core, T, topo):
         ts(R("TI", 2, W64, 4), R("AD2", 0, 256), 0.015625, None, A.mult)
         for h in range(2):
             ts(R("TI", 512 * h + 3, 512 * h + 512, 4), R("AD3", 128 * h, 128 * h + 128), 0.015625, None, A.mult)
-        if r > 0:
-            scan(R("YS", 0, 192), R("CF", 0, 192), R("HR", 0, 192), A.add, A.max)
 
         for h, p in enumerate(("PP", "PQ")):
             quant(qt, qts, "TI", 128, 512 * h, 128 * h)
@@ -482,11 +482,12 @@ def rank_program(g, core, T, topo):
         act(R(K, 0, 256), keys)
         act(R("PR", 0, 128), R("PP", 0, 128))
         if r == 0:
-            act(R("CFB", 0, 256), R("CF", 0, 256), COPY, 1.0 / 64)
+            last_constants()
         else:
-            ts(hu, own("YS"), x("OFS", 0, 1), None, A.add)
+            fold(hu, "YS", "HR", 192)
         cp(R("PR", 128, 256), R("PQ", 0, 128))
         act(R("SC", 0, 192), R("PR", 0, 256, 1, hu))
+        act(R("KAT", 0, 192), R(K, 0, 256, 1, hu))
         ranks("SC", lambda a: R("PR", 0, 256, 1, x("HU", a // 16, a // 16 + 6)))
         ranks_end()
         lpo = R(lp, 0, 4)
@@ -502,13 +503,13 @@ def rank_program(g, core, T, topo):
             act(R("AD%d" % b, 256, 512), R(p, 0, 256), COPY, 64.0)
 
         def before(c):
-            ts(R("CMN", 208 * c, 208 * c + 192), R("KST", 0, 192), R("AOS", 16 * c + 15, 16 * c + 16), None, A.is_le)
+            ts(R("CMN", 208 * c + 64, 208 * c + 192), R("KST", 0, 128), R("AOS", 16 * c + 15, 16 * c + 16), None, A.is_le)
             if c >= 4 - SUMS_ON_SCALAR:
-                total(x("TTA", c, c + 1), R("CMN", 208 * c, 208 * c + 193), 193)
+                total(x("TTA", c, c + 1), R("CMN", 208 * c + 64, 208 * c + 193), 129)
 
         def before_sum(c):
             if c < 4 - SUMS_ON_SCALAR:
-                red(x("TTA", c, c + 1), R("CMN", 208 * c, 208 * c + 193), A.add)
+                red(x("TTA", c, c + 1), R("CMN", 208 * c + 64, 208 * c + 193), A.add)
 
         def behind(c):
             if c < SIGNS_ON_VECTOR:
@@ -518,41 +519,48 @@ def rank_program(g, core, T, topo):
             if c < SIGNS_ON_VECTOR:
                 red(x("AC", c, c + 1), R("CMQ", 64 * c, 64 * c + 64), A.add)
 
+        def stay(a, b):
+            for c in range(a, b):
+                total(x("P3", c, c + 1), R("CUM", 16 * c, 16 * c + 80), 80, x("IW5", c, c + 1))
+
         units(0)
         cp(R("LROW", 0, 192, 1, x("RKU", 0, 12)), R("HR", 0, 192))
         act(R("FLT", 0, 192), R("STEP", 0, 192, 1, x("RKU", 0, 12)))
         act(R("SFP", 0, 256), R("FLT", 0, 640, 1, x("QD")))
-        mm("PQ", "UP", "UPS", lq, ls)
-        act(R(K, 256, 512), R("PQ", 0, 256))
         units(1)
+        scan(R("CUM", 0, 192), ONE(192), R("FLT", 0, 192))
+        stay(0, 8)
         scan(R("LL", 0, 64), R("CF", 0, 64), R("LROW", 0, 64), A.add, A.max)
         units(2)
         ts(R(lw, 0, 4), own("LL", 64), x("OFS", 0, 1), None, A.add)
         send(R(lp, 0, 4), R(lw, 0, 4), "al%d" % r)
         units(3)
+        if r == 0:
+            iota(R("OLT", 0, 512), [[1, 512]])
+            const("OLT", (512, 528), -1)
         if last:
             quant("QVC", "QVS", "VT", 128)
         scan(R("CSP", 0, 256), ONE(256), R("SFP", 0, 256))
         cp(R(K, 0, 256, 1, R(lw, 0, 4)), R("BIGS", 0, 64))
-        act(R("KST", 0, 192), R(K, 0, 256, 1, hu))
-        unpack(0)
-        unpack(1)
+        mm("PQ", "UP", "UPS", lq, ls)
+        act(R(K, 256, 512), R("PQ", 0, 256))
         scan(R("TMB", 0, 256), R("CFB", 0, 256), R("CSP", 0, 256), A.add, A.max)
         scan(R("YB", 0, 256), R("CFB", 0, 256), R("SFP", 0, 256), A.add, A.max)
         tt(h1, own("CSP", 256), x("C12P"), A.subtract)
         tt(x("P2"), own("TMB", 256), x("CT"), A.add)
         tt(x("P1"), own("YB", 256), x("T1"), A.mult)
         scan(R("LBK", 0, 256), R(K, 0, 256), R("LBM", 0, 256), A.min, A.max, BIG)
+        tt(x("P4", 0, 8), x("P3", 0, 8), x("C32", 0, 8), A.add)
         tt(x("TB"), x("P2"), x("P1"), A.subtract)
-        tt(x("HC"), h1, h0, A.subtract)
-        cp(x("TBU"), x("TB"))
+        ts(x("TBU", 0, 8), x("P4", 0, 8), 0.5, None, A.mult)
+        act(R("KST", 0, 128), R("KAT", 0, 192, 1, x("TBU", 0, 8)))
+        act(R("SRC", 0, 128), R("HR", 0, 192, 1, x("TBU", 0, 8)))
         tt(x("WT"), x("TB"), h0, A.subtract)
-        cp(R("SRC", 0, 640, 1, x("TBU")), IOTA(0, 256))
         tt(R("TMP", 0, 64), arr, MASK(64), A.mult)
         ts(R("ARC", 0, 64), arr, R("LBK", 255, 256), None, A.is_lt)
         scan(R("AOS", 0, 64), RST(64), R("TMP", 0, 64))
         red(x("AR1", 0, 1), R("ARC", 0, 64), A.add)
-        act(R("ARS", 0, 64), IOTA(256, 512, lpo))
+        act(R("SRC", 128, 192), IOTA(256, 512, lpo))
         before(3)
         cp(x("AU", 0, 1), x("AR1", 0, 1))
         before(2)
@@ -560,58 +568,54 @@ def rank_program(g, core, T, topo):
         before(1)
         tt(x("CN"), r1, r0, A.subtract)
         before(0)
-        scan(x("S4"), x("RST4"), x("CN"), A.mult, A.max)
+        scan(x("S4"), x("RST4"), x("CN"), A.min, A.max)
+        tt(R("X4", 0, 64), R("RB", 0, 24, 1, x("L4", 0, 4)), R("C4", 0, 64), A.mult)
         before_sum(1)
         before_sum(0)
-        unpack(2)
+        act(x("HC", 1, 17), IOTA(0, 72, x("AU", 0, 1)))
         ts(nsel, R("S4", 0, 16, 1, x("AL", 0, 1)), 2.5, -1.0, A.is_gt, A.mult)
-        tt(R("X4", 0, 64), R("RB", 0, 24, 1, x("L4", 0, 4)), R("C4", 0, 64), A.mult)
-        cp(x("TU", 8, 12), x("TTA", 0, 4))
         tt(x("CN4", 0, 4), x("RB", 4, 17, 4), x("RB", 0, 13, 4), A.subtract)
-        tt(x("AX"), x("CN"), x("HC"), A.subtract)
+        cp(x("TU", 8, 12), x("TTA", 0, 4))
         scan(R("O1", 0, 64), R("S1A", 0, 64), R("X4", 0, 64))
+        tt(x("ZX", 0, 4), x("CN4", 0, 4), R("S1A", 3, 64, 16), A.mult)
         tt(R("NR", 0, 64), IOTA(0, 192, x("TU", 8, 12)), R("J64", 0, 64), A.subtract)
         for c in range(SIGNS_ON_VECTOR, 8):
             total(x("AC", c, c + 1), R("NR", 0, 64), 64, x("IW5", c, c + 1))
-        unpack(3)
-        tt(x("ZX", 0, 4), x("CN4", 0, 4), R("S1A", 3, 64, 16), A.mult)
-        tt(R("X8", 0, 128), R("O1", 0, 72, 1, x("L8", 0, 8)), R("C8", 0, 128), A.mult)
         red(x("ZM", 0, 1), x("ZX", 0, 4), A.min)
-        for c in range(3):
-            behind(c)
+        tt(R("X8", 0, 128), R("O1", 0, 72, 1, x("L8", 0, 8)), R("C8", 0, 128), A.mult)
         ts(R("S2A", 2, 128, 4), x("C45", 0, 32), x("ZM", 0, 1), None, A.is_lt)
-        for c in range(3):
-            behind_sum(c)
+        for c in range(SIGNS_ON_VECTOR):
+            behind(c)
+        tt(x("AX"), x("HC", 1, 17), x("HC"), A.subtract)
         scan(R("O2", 0, 640, 5), R("S2A", 0, 128), R("X8", 0, 128))
-        tt(x("TTS", 0, 7), x("AC", 0, 7), x("C2I", 0, 7), A.add)
-        tt(R("S3A", 1, 80, 5), R("O2", 35, 640, 40), R("O2", 15, 640, 40), A.is_le)
+        for c in range(SIGNS_ON_VECTOR):
+            behind_sum(c)
+        for b in range(4):
+            unpack(b)
         tt(x("NI"), x("AX"), nsel, A.subtract)
+        tt(R("S3A", 1, 80, 5), R("O2", 35, 640, 40), R("O2", 15, 640, 40), A.is_le)
         tt(R("O2", 39, 640, 40), x("WT"), r0, A.add)
-        ts(x("TU", 0, 7), x("TTS", 0, 7), 0.5, None, A.mult)
-        ts(x("TU", 7, 8), x("AC", 7, 8), x("C2I", 7, 8), 0.5, A.add, A.mult)
         ts(R("S3A", 4, 80, 5), x("NI"), R("S2A", 2, 3), -1.0, A.is_ge, A.mult)
+        tt(x("TTS", 0, 7), x("AC", 0, 7), x("C2I", 0, 7), A.add)
         tt(R("O2", 31, 640, 40), x("WT"), r0, A.add)
-        if last:
-            act(R("OLT", 0, 512), IOTA(0, 512))
-            act(R("OLT", 512, 528), ONE(16), COPY, -1.0)
-        cp(R("SEQ", 0, 192, 1, x("TU", 8, 12)), R("ARS", 0, 64))
+        ts(x("TU", 7, 8), x("AC", 7, 8), x("C2I", 7, 8), 0.5, A.add, A.mult)
+        ts(x("TU", 0, 7), x("TTS", 0, 7), 0.5, None, A.mult)
         scan(R("O3", 0, 80), R("S3A", 0, 80), R("O2", 7, 640, 8))
-        cp(R("SEQ", 0, 192, 1, x("TU", 0, 8)), R("SRC", 0, 128))
+        cp(R("SEQ", 0, 192, 1, x("TU", 0, 12)), R("SRC", 0, 192))
         cp(x("QD"), R("O3", 4, 80, 5))
         cp(R("TMY", 0, 128), R("SEQ", 0, 640, 1, x("QD", 0, 8)))
         act(R("TMY", 128, 256), R("SEQ", 0, 640, 1, x("QD", 8, 16)))
         places(0, 2, last)
+        if last:
+            cp(R("OLT", 256, 512, 1, lpo), IOTA(256, 320))
         scan(R("YS", 0, 256), R("CF", 0, 256), R("TMY", 0, 256), A.add, A.max)
         places(2, 4, last)
         ts(x("OFY"), own("YS", 256), x("OFS", 0, 1), None, A.add)
         places(4, 6, last)
-        for t in range(4):
-            o, a = R(Fn, t, W64, 4), R("AD%d" % t, 0, 528, 1, x("OFY"))
-            if t < 2:
-                act(o, a, COPY, 0.015625)
-            else:
-                ts(o, a, 0.015625, None, A.mult)
-        places(6, 8, last)
+        if not last:
+            for t in range(4):
+                pick(t, 0, 16)
+            places(6, 8)
         keys = R(K, 0, 528, 1, x("OFY"))
         F, Fn, K, Kn = Fn, F, Kn, K
 
@@ -621,19 +625,34 @@ def rank_program(g, core, T, topo):
         stored[0] += 1
         emit(q, lambda: Q[q].dma_start(dst, src), [], [a], ("dout", 16 * stored[0], 16))
 
-    quant("QF", "QFS", F, 256)
-    for h, p in enumerate(("PP", "PQ")):
-        mm(p, "QVC", "QVS", "QF", "QFS", 128, 0, 128 * h)
-    cp(R("OLT", 256, 512, 1, lpo), IOTA(256, 320))
+    def half(h):
+        quant("QF", "QFS", F, 128, 512 * h, 128 * h)
+        mm(("PP", "PQ")[h], "QVC", "QVS", "QF", "QFS", 128, 0, 128 * h)
+        qf = R("QF", 128 * h, 128 * h + 128, 1, None, dt.uint8)
+        store("y", T.oc[:, 512 * h:512 * h + 512], qf, ap(qf))
+
+    Fn = F
+    for t in range(4):
+        pick(t, 0, 8)
+    for t in range(3):
+        pick(t, 8, 16)
+    half(0)
+    pick(3, 8, 16)
+    half(1)
+
+    def scales(q, k):
+        store(q, T.osc[4 * k:4 * k + 4, 0:256], R("QFS", 0, 256), T.QFS[32 * k:32 * k + 4, 0:256])
+
     act(R("YO", 0, 128), R("PP", 0, 128))
-    cp(R("YO", 128, 256), R("PQ", 0, 128))
     cp(R("OLR", 0, 256), R("OLT", 0, 528, 1, x("OFY")))
-    qf = R("QF", 0, 256, 1, None, dt.uint8)
-    store("y", T.oc[:, 0:W64], qf, ap(qf))
-    for k in range(4):
-        store("y", T.osc[4 * k:4 * k + 4, 0:256], R("QFS", 0, 256), T.QFS[32 * k:32 * k + 4, 0:256])
-    store("s", T.y[:, 0:256], R("YO", 0, 256), ap(R("YO", 0, 256)))
-    store("y", T.ol[:, 0:256], R("OLR", 0, 256), T.OLR[0:128:16, 0:256])
+    scales("y", 0)
+    scales("y", 1)
+    store("s", T.y[:, 0:128], R("YO", 0, 128), ap(R("YO", 0, 128)))
+    scales("s", 2)
+    scales("s", 3)
+    cp(R("YO", 128, 256), R("PQ", 0, 128))
+    store("y", T.y[:, 128:256], R("YO", 128, 256), ap(R("YO", 128, 256)))
+    store("s", T.ol[:, 0:256], R("OLR", 0, 256), T.OLR[0:128:16, 0:256])
 
     for q in ("v", "s", "t", "g"):
         if known["g"].get(q, 0) < cnt[q]:

@@ -9,11 +9,10 @@ SIGN = ActivationFunctionType.Sign
 BIG = 2.0 ** 96
 ROUNDS = 3
 W64 = 4 * 256
-UP_ = 0.5 - 1.0 / 512
+UP_ = 0.5 - 1.0 / 128
 WHOLE = 1.5 * 2.0 ** 23
+SMALL_ = 2.0 ** 17
 ON_SCALAR = 10
-SUMS_ON_SCALAR = 3
-SIGNS_ON_VECTOR = 2
 
 SCRATCH = {}
 
@@ -26,7 +25,7 @@ def _decl(names, where, shape, dtype):
 _decl("XT", "sbuf", [128, 768], "bfloat16")
 _decl("UT VT", "sbuf", [128, 512], "bfloat16")
 _decl("EA EB ONEB AD0 AD1 AD2 AD3", "sbuf", [128, 528], "bfloat16")
-_decl("TI FA FB GI", "sbuf", [128, 1024], "bfloat16")
+_decl("TI FA GI", "sbuf", [128, 1024], "bfloat16")
 _decl("CMP", "sbuf", [128, 2304], "bfloat16")
 _decl("JNK", "sbuf", [128, 8 * 272], "bfloat16")
 _decl("CMN", "sbuf", [128, 4 * 272], "bfloat16")
@@ -46,11 +45,11 @@ _decl("KA KB OLT", "sbuf", [128, 528], "float32")
 _decl("SRC SEQ HR O2", "sbuf", [128, 640], "float32")
 _decl("JM MASK DMASK RMIN LBM LBK TMP TMY YS PR OLR YO", "sbuf", [128, 256], "float32")
 _decl("SEQS SC", "sbuf", [128, 208], "float32")
-_decl("Z LROW KST KAT", "sbuf", [128, 192], "float32")
+_decl("Z LROW KST KAT SQA", "sbuf", [128, 192], "float32")
 _decl("CF", "sbuf", [128, 256], "float32")
-_decl("C8 X8 S2A A8 B8", "sbuf", [128, 128], "float32")
-_decl("O1 S3A O3", "sbuf", [128, 80], "float32")
-_decl("LL AOS ARC BIGS NR C4 X4 S1A J64", "sbuf", [128, 64], "float32")
+_decl("X10 S2A", "sbuf", [128, 160], "float32")
+_decl("O1 S3A O3", "sbuf", [128, 104], "float32")
+_decl("LL AOS BIGS NR C4 X4 S1A", "sbuf", [128, 64], "float32")
 SMALL = ("RB C1C C12 IW M16 M17 CNT RK KI0 ENC INV EN2 SP AR1 RST4 CN S4 CN4 ZX ZM C45 HC WT TB CT AX NI TTA AC C2I TTS IW5 "
          "S16 S161 N16 N161 CA CB PA PB PC PD C4C C8C LB0 OFS O16 O17 T1 C12P P1 P2 P3 P4 C32 HB HW").split()
 _decl("SMALLS", "sbuf", [128, 32 * len(SMALL)], "float32")
@@ -58,12 +57,12 @@ _decl("INTS", "sbuf", [128, 16 * 11], "int32")
 _decl("LW0 LW1 LW2 LP0 LP1 LP2", "sbuf", [128, 4], "uint16")
 _decl("LISTS", "sbuf", [128, 16 * 12], "uint16")
 _decl("XP0 XP1 XP2 XP3", "sbuf", [128, 208], "bfloat16")
-_decl("CMQ", "sbuf", [128, 512], "bfloat16")
+_decl("FLA", "sbuf", [128, 256], "bfloat16")
 _decl("STEP", "sbuf", [128, 192], "float32")
 _decl("FLT", "sbuf", [128, 640], "bfloat16")
 PIECE = {n: ("SMALLS", 32 * i) for i, n in enumerate(SMALL)}
 PIECE.update({n: ("INTS", 16 * i) for i, n in enumerate("PI SI I2 I3 I4 I8 KI KA4 KB4 UI H3".split())})
-PIECE.update({n: ("LISTS", 16 * i) for i, n in enumerate("RKU HU QV0 QD TU TBU AL UL OFY AU L4 L8".split())})
+PIECE.update({n: ("LISTS", 16 * i) for i, n in enumerate("RKU HU QV0 QD TU TBU AL UL OFY AU L4 L10".split())})
 
 SEMAPHORES = ["sv", "ss", "st", "sg", "dx", "du", "dw", "dws", "dv", "dout", "loc", "au",
               "aq0", "aq1", "aq2", "al0", "al1", "al2"]
@@ -264,12 +263,12 @@ def rank_program(g, core, T, topo):
     iota(x("UI", 0, 8), [[16, 8]])
     iota(x("M16"), [[16, 16]])
     iota(x("C4C", 0, 4), [[4, 4]])
-    iota(x("C8C", 0, 8), [[8, 8]])
+    iota(x("C12"), [[12, 16]])
     fill(ONE(528), 1.0)
-    for k, c in enumerate((2, -2, 96, 0)):
-        iota(R("B8", k, 128, 4), [[0, 32]], c)
-    for k, (pattern, c) in enumerate((([[0, 16], [2, 2]], 0), ([[0, 16], [-2, 2]], 32), ([[1536, 16], [96, 2]], 63), ([[0, 32]], 0))):
-        iota(R("A8", k, 128, 4), pattern, c)
+    for k, (pattern, c) in enumerate((([[4, 16], [0, 2]], 7), ([[4, 16], [0, 2]], 3), ([[4, 16], [0, 2]], 3), ([[1, 16], [16, 2]], 72), ([[0, 32]], 68))):
+        iota(R("X10", k, 160, 5), pattern, c)
+    for k, c in ((0, 0), (1, -1), (4, 1)):
+        iota(R("S2A", k, 160, 5), [[0, 32]], c)
     for b in range(4):
         const("XP%d" % b, (192, 208), 0)
 
@@ -280,12 +279,8 @@ def rank_program(g, core, T, topo):
         for n, b in (("EA", 2), ("EB", 3)):
             o = R(n, 0, 516)
             emit("g", lambda: g.affine_select(ap(o), ap(ONE(516)), [[-1, 516]], A.is_equal, 0.0, b, 4), [o], [ONE(516)])
-        const("STEP", (0, 64), 0)
-        const("STEP", (64, 192), 1)
         const("FLT", (192, 640), 0)
         const("SEQ", (192, 640), 512)
-        iota(R("S2A", 0, 128), [[0, 64], [1, 2]])
-        iota(R("J64", 0, 64), [[1, 64]])
 
     def last_constants():
         iota(x("C12P"), [[12, 16]], 12)
@@ -300,11 +295,10 @@ def rank_program(g, core, T, topo):
         iota(R("S1A", 0, 64), [[0, 16], [1, 4]])
         iota(R("S1A", 2, 64, 4), [[0, 16]], -1)
         const("O1", (64, 68), 0)
-        const("O1", (68, 72), 1)
+        const("O1", (68, 72), int(WHOLE))
         const("C45", (0, 32), -5)
-        iota(R("S3A", 0, 80), [[0, 16], [2, 5]], -5)
-        iota(R("S3A", 0, 80, 5), [[0, 16]])
-        iota(R("O2", 23, 640, 40), [[0, 16]], int(WHOLE))
+        const("S3A", (0, 96), 1)
+        iota(R("S3A", 0, 96, 6), [[0, 16]])
 
     scan(IOTA(0, 512), ONE(512), ONE(512), A.mult, A.add, -1.0)
     ts(x("SI", 0, 1), x("PI", 0, 1), 15, None, A.bitwise_and)
@@ -320,33 +314,41 @@ def rank_program(g, core, T, topo):
     def tables_a():
         act(R("CF", 0, 256), MASK(256), IDENT, -33.0 * 1024, 1024.0)
         act(R("CFB", 0, 256), MASK(256), IDENT, -65.0, 1.0)
-        act(R("LBM", 0, 256), IOTA(0, 256), IDENT, -BIG / 2, x("LB0", 0, 1))
-        act(R("X8", 0, 128), R("B8", 0, 128), COPY, s)
 
     def tables_c():
+        act(R("LBM", 0, 256), IOTA(0, 256), IDENT, -BIG / 2, x("LB0", 0, 1))
+        act(x("S16", 0, 1), s, COPY, -1.0 / 16)
+        act(x("S161", 0, 1), s, IDENT, -1.0 / 16, -1.0 / 16)
+        act(x("CA", 0, 1), s, IDENT, 0.75, UP_)
+        act(x("CB", 0, 1), s, IDENT, 0.75, 0.75 + UP_)
+        act(R("STEP", 0, 64), ONE(64), COPY, 0.0)
+        act(R("STEP", 64, 192), ONE(128))
+        act(R("SQA", 0, 192), ONE(192), COPY, -1.0)
+
+    def tables_d():
         act(R("CMN", 192, 4 * 208, 208), x("IW", 0, 4))
         act(x("IW5", 0, 8), x("IW", 0, 8), IDENT, 1.0, 0.5)
-        act(x("C2I", 0, SIGNS_ON_VECTOR), x("IW", 0, SIGNS_ON_VECTOR), COPY, 2.0)
-        act(x("C2I", SIGNS_ON_VECTOR, 8), x("IW", SIGNS_ON_VECTOR, 8), IDENT, 2.0, 64.0)
         act(x("T1"), x("IW"), IDENT, 1.0, 193.0)
-        act(R("O2", 7, 640, 40), x("IW"), IDENT, 1.0, 192.0)
-        act(R("C8", 0, 128), R("A8", 0, 128), COPY, 1.0 / 128)
+        act(R("O2", 7, 480, 30), x("IW"), IDENT, 1.0, 192.0)
+        act(R("S2A", 2, 160, 10), ONE(16), COPY, x("S16", 0, 1))
+        act(R("S2A", 7, 160, 10), ONE(16), COPY, x("S161", 0, 1))
+        act(R("O1", 72, 88), x("C12"), IDENT, 1.0, x("CA", 0, 1))
+        act(R("O1", 88, 104), x("C12"), IDENT, 1.0, x("CB", 0, 1))
 
     spare = [
         lambda: fill(R("KA", 512, 528), BIG),
         lambda: fill(R("KB", 512, 528), BIG),
-        lambda: tt(R("A8", 0, 128), R("A8", 0, 128), R("X8", 0, 128), A.add),
+        lambda: scan(R("YS", 0, 160), R("CF", 0, 160), R("X10", 0, 160), A.add, A.max),
         lambda: ts(x("PA", 0, 1), x("I3", 0, 1), 0.0, 4.0, A.is_equal, A.mult),
         lambda: ts(x("PB", 0, 1), x("I3", 0, 1), 1.5, None, A.is_gt),
-        lambda: ts(x("PC", 0, 1), x("I8", 0, 1), 0.5, -65.0, A.mult, A.add),
-        lambda: ts(x("PD", 0, 1), x("I3", 0, 1), 1.5, None, A.is_lt),
+        lambda: ts(x("L10", 0, 10), own("YS", 160), x("OFS", 0, 1), None, A.add),
         lambda: ts(x("AL", 0, 1), x("I2", 0, 1), 3.0, None, A.add),
         lambda: ts(x("INV", 0, 1), x("I4", 0, 1), x("PB", 0, 1), x("PA", 0, 1), A.mult, A.add),
-        lambda: ts(x("EN2", 0, 8), x("C8C", 0, 8), x("PC", 0, 1), x("PA", 0, 1), A.add, A.add),
-        lambda: ts(x("CT"), x("IW"), 192.0, x("O17", 0, 1), A.add, A.mult),
+        lambda: ts(x("M17"), x("IW"), 192.0, x("O17", 0, 1), A.add, A.mult),
+        lambda: ts(x("O16", 0, 1), s, WHOLE - 16.0, None, A.add),
         lambda: ts(x("L4", 0, 4), x("C4C", 0, 4), x("INV", 0, 1), None, A.add),
-        lambda: ts(x("L8", 0, 8), x("EN2", 0, 8), x("PD", 0, 1), 68.0, A.mult, A.add),
-        lambda: fill(R("C8", 3, 128, 4), WHOLE),
+        lambda: ts(x("CT"), x("M17"), WHOLE, None, A.add),
+        lambda: fill(R("O2", 2, 488, 30), 0.0),
     ]
 
     def meanwhile(n):
@@ -364,14 +366,12 @@ def rank_program(g, core, T, topo):
     fill(R("SEQS", 192, 208), 192.0)
     ts(x("KI0"), x("KA4"), 3.0, -192.0, A.mult, A.add)
     ts(x("INV"), x("KB4"), 2.5, None, A.is_lt)
-    for n, k, op in (("I2", 12, A.bitwise_and), ("I3", 3, A.bitwise_and), ("I4", 2, A.arith_shift_right), ("I8", 8, A.bitwise_and)):
-        ts(x(n, 0, 1), x("SI", 0, 1), k, None, op)
     tables_a()
     quant("QU", "QUS", "UT", 128)
     tt(x("ENC"), x("KI0"), x("KB4"), A.add)
     cp(x("HU", 0, 12), x("M17", 0, 12))
     cp(R("UR", 0, 128, 1, None, dt.uint32), R("QU", 0, 128, 1, R("UL", 0, 8), dt.uint32))
-    cp(R("URS", 0, 128), R("QUS", 0, 128, 1, R("UL", 0, 8)))
+    act(R("URS", 0, 128), R("QUS", 0, 128, 1, R("UL", 0, 8)))
     quant("QX", "QXS", "XT", 192)
     mm("PP", "UR", "URS", "QX", "QXS", 192)
     send_codes("UP", "UPS", "UR", "URS", 128, "au")
@@ -382,6 +382,8 @@ def rank_program(g, core, T, topo):
     fill(R("SC", 192, 208), BIG)
     fill(R("BIGS", 0, 64), BIG)
     ts(x("QD"), x("EN2"), 192.0, None, A.add)
+    for n, k, op in (("I2", 12, A.bitwise_and), ("I3", 3, A.bitwise_and), ("I4", 2, A.arith_shift_right)):
+        ts(x(n, 0, 1), x("SI", 0, 1), k, None, op)
 
     def ranks(row, diag):
         for a in (0, 96):
@@ -397,20 +399,20 @@ def rank_program(g, core, T, topo):
                 ts(R("CMP", 192 * c + e, 192 * c + 192), R(row, e, 192), k, None, A.is_lt)
             if i < ON_SCALAR:
                 total(x("CNT", c, c + 1), R("CMP", 192 * c, 192 * c + 192), 192)
-            if i == 4:
+            if i == 7:
                 tt(R("EQR", 0, 192), R("Z", 0, 192), R(row, 0, 192), A.is_equal)
-            if i == 5:
+            if i == 8:
                 scan(R("YB", 0, 192), RST(192), R("EQR", 0, 192))
-        for c in range(12 - ON_SCALAR):
-            scan(R("CUM", 192 * c, 192 * c + 192), ONE(192), R("CMP", 192 * c, 192 * c + 192))
 
     def ranks_end():
         n = 12 - ON_SCALAR
         tt(x("RK", n, 11), x("CNT", n, 11), R("YB", 16 * n + 15, 176, 16), A.subtract)
         for c in range(n):
-            ts(x("RKU", c, c + 1), R("CUM", 192 * c + 191, 192 * c + 192), R("YB", 16 * c + 15, 16 * c + 16), None, A.subtract)
+            scan(R("CUM", 192 * c, 192 * c + 192), ONE(192), R("CMP", 192 * c, 192 * c + 192))
         cp(x("RKU", n, 11), x("RK", n, 11))
-        ts(x("RKU", 11, 12), x("CNT", 11, 12), R("YB", 191, 192), None, A.subtract)
+        for c in (0, 11) + tuple(range(1, n)):
+            a = x("CNT", c, c + 1) if c >= n else R("CUM", 192 * c + 191, 192 * c + 192)
+            ts(x("RKU", c, c + 1), a, R("YB", 16 * c + 15, 16 * c + 16), None, A.subtract)
 
     def fold(o, y, a, n):
         scan(R(y, 0, n), R("CF", 0, n), R(a, 0, n), A.add, A.max)
@@ -423,20 +425,15 @@ def rank_program(g, core, T, topo):
     cp(R("SEQS", 0, 192, 1, x("RKU", 0, 12)), IOTA(0, 192))
     meanwhile(1)
     tables_c()
+    tables_d()
     tt(R("TMB", 0, 256), R("SEQS", 0, 208, 1, x("QD")), MASK(256), A.mult)
     meanwhile(2)
     scan(R("YB", 0, 256), RST(256), R("TMB", 0, 256))
     meanwhile(2)
     cp(x("OFY"), own("YB", 256))
     meanwhile(2)
-    for t in range(4):
-        o, a = R("FA", t, W64, 4), R("XP%d" % t, 0, 208, 1, x("OFY"))
-        if t < 2:
-            act(o, a)
-        else:
-            cp(o, a)
 
-    F, Fn = "FA", "FB"
+    F = "FA"
     K, Kn = "KA", "KB"
     keys = R("SC", 0, 208, 1, x("OFY"))
     hu = x("HU", 0, 12)
@@ -444,12 +441,15 @@ def rank_program(g, core, T, topo):
     r0, r1 = x("RB", 0, 16), x("RB", 1, 17)
     nsel = R("S1A", 3, 64, 4)
 
-    def pick(t, a, b):
-        o, w = R(Fn, 64 * a + t, 64 * b, 4), R("AD%d" % t, 0, 528, 1, x("OFY", a, b))
+    def pick(t, a, b, first=False):
+        o = R(F, 64 * a + t, 64 * b, 4)
+        w, k = (R("XP%d" % t, 0, 208, 1, x("OFY", a, b)), 1.0) if first else (R("AD%d" % t, 0, 528, 1, x("OFY", a, b)), 0.015625)
         if t < 2:
-            act(o, w, COPY, 0.015625)
+            act(o, w, COPY, k)
+        elif first:
+            cp(o, w)
         else:
-            ts(o, w, 0.015625, None, A.mult)
+            ts(o, w, k, None, A.mult)
 
     def places(a, b, skip=False):
         if not skip:
@@ -458,34 +458,48 @@ def rank_program(g, core, T, topo):
     for r in range(ROUNDS):
         last = r == ROUNDS - 1
         qt, qts, lq, ls, lw, lp = ["%s%d" % (n, r) for n in ("QT", "QTS", "LQ", "LS", "LW", "LP")]
-        quant("QF", "QFS", F, 256)
+
+        def add(b, k, l, bank):
+            tt(R("AD%d" % b, k, l), R(bank, 0, l - k), R("GI", 4 * k + b, 4 * l, 4), A.add)
+
+        def tile(b, k, l):
+            o, a = R("TI", 4 * k + b, 4 * l, 4), R("AD%d" % b, k, l)
+            if b < 2:
+                act(o, a, COPY, 0.015625)
+            else:
+                ts(o, a, 0.015625, None, A.mult)
+
+        for t in range(4):
+            pick(t, 0, 16, r == 0)
+        places(6, 8, r == 0)
+        banks = ("PS0", "PP", "PS1", "PQ", "PS2", "PD1", "PS3", "PD0")
+        for h in range(2):
+            quant("QF", "QFS", F, 128, 512 * h, 128 * h)
         for b in range(4):
-            mm("PS%d" % b, "WQ", "WS", "QF", "QFS", 256, 128 * b)
-        for b in range(4):
+            for h in range(2):
+                mm(banks[2 * b + h], "WQ", "WS", "QF", "QFS", 128, 128 * b, 128 * h)
             act(R("GI", b, W64, 4), R(F, b, W64, 4), COPY, 64.0)
         places(8, 16, r == 0)
         meanwhile(5)
-        for b in range(3):
-            tt(R("AD%d" % b, 0, 256), R("PS%d" % b, 0, 256), R("GI", b, W64, 4), A.add)
+        for b in range(4):
+            for h in range(2):
+                add(b, 128 * h, 128 * h + 128, banks[2 * b + h])
             if b < 2:
-                act(R("TI", b, W64, 4), R("AD%d" % b, 0, 256), COPY, 0.015625)
+                tile(b, 0, 256)
         for h in range(2):
-            tt(R("AD3", 128 * h, 128 * h + 128), R("PS3", 128 * h, 128 * h + 128), R("GI", 512 * h + 3, 512 * h + 512, 4), A.add)
-        ts(R("TI", 2, W64, 4), R("AD2", 0, 256), 0.015625, None, A.mult)
-        for h in range(2):
-            ts(R("TI", 512 * h + 3, 512 * h + 512, 4), R("AD3", 128 * h, 128 * h + 128), 0.015625, None, A.mult)
-
-        for h, p in enumerate(("PP", "PQ")):
+            tile(2, 128 * h, 128 * h + 128)
+            tile(3, 128 * h, 128 * h + 128)
+        for h, p in enumerate(("PS0", "PS1")):
             quant(qt, qts, "TI", 128, 512 * h, 128 * h)
             mm(p, "UR", "URS", qt, qts, 128, 0, 128 * h)
         send_codes(lq, ls, qt, qts, 256, "aq%d" % r)
         act(R(K, 0, 256), keys)
-        act(R("PR", 0, 128), R("PP", 0, 128))
+        act(R("PR", 0, 128), R("PS0", 0, 128))
         if r == 0:
             last_constants()
         else:
             fold(hu, "YS", "HR", 192)
-        cp(R("PR", 128, 256), R("PQ", 0, 128))
+        cp(R("PR", 128, 256), R("PS1", 0, 128))
         act(R("SC", 0, 192), R("PR", 0, 256, 1, hu))
         act(R("KAT", 0, 192), R(K, 0, 256, 1, hu))
         ranks("SC", lambda a: R("PR", 0, 256, 1, x("HU", a // 16, a // 16 + 6)))
@@ -504,20 +518,7 @@ def rank_program(g, core, T, topo):
 
         def before(c):
             ts(R("CMN", 208 * c + 64, 208 * c + 192), R("KST", 0, 128), R("AOS", 16 * c + 15, 16 * c + 16), None, A.is_le)
-            if c >= 4 - SUMS_ON_SCALAR:
-                total(x("TTA", c, c + 1), R("CMN", 208 * c + 64, 208 * c + 193), 129)
-
-        def before_sum(c):
-            if c < 4 - SUMS_ON_SCALAR:
-                red(x("TTA", c, c + 1), R("CMN", 208 * c + 64, 208 * c + 193), A.add)
-
-        def behind(c):
-            if c < SIGNS_ON_VECTOR:
-                ts(R("CMQ", 64 * c, 64 * c + 64), R("NR", 0, 64), x("IW5", c, c + 1), 2.0, A.is_lt, A.mult)
-
-        def behind_sum(c):
-            if c < SIGNS_ON_VECTOR:
-                red(x("AC", c, c + 1), R("CMQ", 64 * c, 64 * c + 64), A.add)
+            total(x("TTA", c, c + 1), R("CMN", 208 * c + 64, 208 * c + 193), 129)
 
         def stay(a, b):
             for c in range(a, b):
@@ -529,7 +530,9 @@ def rank_program(g, core, T, topo):
         act(R("SFP", 0, 256), R("FLT", 0, 640, 1, x("QD")))
         units(1)
         scan(R("CUM", 0, 192), ONE(192), R("FLT", 0, 192))
-        stay(0, 8)
+        stay(0, 7)
+        mm("PQ", "UP", "UPS", lq, ls)
+        act(R(K, 256, 512), R("PQ", 0, 256))
         scan(R("LL", 0, 64), R("CF", 0, 64), R("LROW", 0, 64), A.add, A.max)
         units(2)
         ts(R(lw, 0, 4), own("LL", 64), x("OFS", 0, 1), None, A.add)
@@ -540,71 +543,68 @@ def rank_program(g, core, T, topo):
             const("OLT", (512, 528), -1)
         if last:
             quant("QVC", "QVS", "VT", 128)
-        scan(R("CSP", 0, 256), ONE(256), R("SFP", 0, 256))
+        ts(R("CMP", 0, 80), R("CUM", 112, 192), x("IW5", 7, 8), None, A.is_lt)
         cp(R(K, 0, 256, 1, R(lw, 0, 4)), R("BIGS", 0, 64))
-        mm("PQ", "UP", "UPS", lq, ls)
-        act(R(K, 256, 512), R("PQ", 0, 256))
-        scan(R("TMB", 0, 256), R("CFB", 0, 256), R("CSP", 0, 256), A.add, A.max)
+        red(x("P3", 7, 8), R("CMP", 0, 80), A.add)
+        scan(R("CSP", 0, 256), ONE(256), R("SFP", 0, 256))
+        scan(R("LBK", 0, 256), R(K, 0, 256), R("LBM", 0, 256), A.min, A.max, BIG)
+        ts(x("TBU", 7, 8), x("P3", 7, 8), 112.0, None, A.add)
         scan(R("YB", 0, 256), R("CFB", 0, 256), R("SFP", 0, 256), A.add, A.max)
         tt(h1, own("CSP", 256), x("C12P"), A.subtract)
-        tt(x("P2"), own("TMB", 256), x("CT"), A.add)
-        tt(x("P1"), own("YB", 256), x("T1"), A.mult)
-        scan(R("LBK", 0, 256), R(K, 0, 256), R("LBM", 0, 256), A.min, A.max, BIG)
-        tt(x("P4", 0, 8), x("P3", 0, 8), x("C32", 0, 8), A.add)
-        tt(x("TB"), x("P2"), x("P1"), A.subtract)
-        ts(x("TBU", 0, 8), x("P4", 0, 8), 0.5, None, A.mult)
+        tt(x("P4", 0, 6), x("P3", 0, 6), x("C32", 0, 6), A.add)
+        scan(R("TMB", 0, 256), R("CFB", 0, 256), R("CSP", 0, 256), A.add, A.max)
+        ts(x("TBU", 0, 6), x("P4", 0, 6), 0.5, None, A.mult)
+        ts(x("TBU", 6, 7), x("P3", 6, 7), 80.0 + 32 * 6, 0.5, A.add, A.mult)
         act(R("KST", 0, 128), R("KAT", 0, 192, 1, x("TBU", 0, 8)))
-        act(R("SRC", 0, 128), R("HR", 0, 192, 1, x("TBU", 0, 8)))
-        tt(x("WT"), x("TB"), h0, A.subtract)
+        ts(R("FLA", 0, 256), R(K, 256, 512), R("LBK", 255, 256), None, A.is_lt)
+        total(x("AR1", 0, 1), R("FLA", 0, 256, 1, lpo), 64)
+        act(R("NR", 0, 64), IOTA(256, 512, lpo), COPY, 1.0 / SMALL_)
+        unpack(0)
         tt(R("TMP", 0, 64), arr, MASK(64), A.mult)
-        ts(R("ARC", 0, 64), arr, R("LBK", 255, 256), None, A.is_lt)
+        tt(x("P1"), own("YB", 256), x("T1"), A.mult)
+        tt(x("P2"), own("TMB", 256), x("CT"), A.add)
         scan(R("AOS", 0, 64), RST(64), R("TMP", 0, 64))
-        red(x("AR1", 0, 1), R("ARC", 0, 64), A.add)
-        act(R("SRC", 128, 192), IOTA(256, 512, lpo))
-        before(3)
         cp(x("AU", 0, 1), x("AR1", 0, 1))
-        before(2)
+        before(3)
         tt(r1, IOTA(0, 72, x("AU", 0, 1)), h1, A.add)
+        before(2)
         before(1)
         tt(x("CN"), r1, r0, A.subtract)
         before(0)
+        tt(x("TB"), x("P2"), x("P1"), A.subtract)
         scan(x("S4"), x("RST4"), x("CN"), A.min, A.max)
         tt(R("X4", 0, 64), R("RB", 0, 24, 1, x("L4", 0, 4)), R("C4", 0, 64), A.mult)
-        before_sum(1)
-        before_sum(0)
         act(x("HC", 1, 17), IOTA(0, 72, x("AU", 0, 1)))
         ts(nsel, R("S4", 0, 16, 1, x("AL", 0, 1)), 2.5, -1.0, A.is_gt, A.mult)
         tt(x("CN4", 0, 4), x("RB", 4, 17, 4), x("RB", 0, 13, 4), A.subtract)
-        cp(x("TU", 8, 12), x("TTA", 0, 4))
         scan(R("O1", 0, 64), R("S1A", 0, 64), R("X4", 0, 64))
+        act(R("X10", 0, 160), R("O1", 0, 104, 1, x("L10", 0, 10)))
         tt(x("ZX", 0, 4), x("CN4", 0, 4), R("S1A", 3, 64, 16), A.mult)
-        tt(R("NR", 0, 64), IOTA(0, 192, x("TU", 8, 12)), R("J64", 0, 64), A.subtract)
-        for c in range(SIGNS_ON_VECTOR, 8):
-            total(x("AC", c, c + 1), R("NR", 0, 64), 64, x("IW5", c, c + 1))
+        cp(x("TU", 0, 4), x("TTA", 0, 4))
+        tt(R("O2", 22, 480, 30), x("TB"), x("HC"), A.add)
+        act(R("O2", 17, 480, 30), R("O2", 22, 480, 30), COPY, -1.0)
+        act(R("SRC", 0, 128), R("HR", 0, 192, 1, x("TBU", 0, 8)))
         red(x("ZM", 0, 1), x("ZX", 0, 4), A.min)
-        tt(R("X8", 0, 128), R("O1", 0, 72, 1, x("L8", 0, 8)), R("C8", 0, 128), A.mult)
-        ts(R("S2A", 2, 128, 4), x("C45", 0, 32), x("ZM", 0, 1), None, A.is_lt)
-        for c in range(SIGNS_ON_VECTOR):
-            behind(c)
-        tt(x("AX"), x("HC", 1, 17), x("HC"), A.subtract)
-        scan(R("O2", 0, 640, 5), R("S2A", 0, 128), R("X8", 0, 128))
-        for c in range(SIGNS_ON_VECTOR):
-            behind_sum(c)
-        for b in range(4):
+        cp(R("SQA", 0, 192, 1, x("TU", 0, 4)), R("NR", 0, 64))
+        ts(R("S2A", 3, 160, 5), x("C45", 0, 32), x("ZM", 0, 1), 0.25, A.is_lt, A.mult)
+        act(x("NI"), nsel, IDENT, 1.0, R("S2A", 3, 4))
+        act(R("KAT", 0, 192), R("SQA", 0, 192), RELU, SMALL_)
+        for b in range(1, 4):
             unpack(b)
-        tt(x("NI"), x("AX"), nsel, A.subtract)
-        tt(R("S3A", 1, 80, 5), R("O2", 35, 640, 40), R("O2", 15, 640, 40), A.is_le)
-        tt(R("O2", 39, 640, 40), x("WT"), r0, A.add)
-        ts(R("S3A", 4, 80, 5), x("NI"), R("S2A", 2, 3), -1.0, A.is_ge, A.mult)
-        tt(x("TTS", 0, 7), x("AC", 0, 7), x("C2I", 0, 7), A.add)
-        tt(R("O2", 31, 640, 40), x("WT"), r0, A.add)
-        ts(x("TU", 7, 8), x("AC", 7, 8), x("C2I", 7, 8), 0.5, A.add, A.mult)
-        ts(x("TU", 0, 7), x("TTS", 0, 7), 0.5, None, A.mult)
-        scan(R("O3", 0, 80), R("S3A", 0, 80), R("O2", 7, 640, 8))
-        cp(R("SEQ", 0, 192, 1, x("TU", 0, 12)), R("SRC", 0, 192))
-        cp(x("QD"), R("O3", 4, 80, 5))
+        tt(x("AX"), x("HC", 1, 17), x("HC"), A.subtract)
+        scan(R("Z", 0, 192), ONE(192), R("SQA", 0, 192), A.mult, A.subtract)
+        scan(R("O2", 0, 480, 3), R("S2A", 0, 160), R("X10", 0, 160))
+        scan(R("LROW", 0, 192), R("CFB", 0, 192), R("Z", 0, 192), A.add, A.max)
+        tt(R("S3A", 1, 96, 6), R("O2", 27, 480, 30), R("O2", 12, 480, 30), A.is_le)
+        tt(R("S3A", 3, 96, 6), x("AX"), x("NI"), A.is_ge)
+        ts(x("RKU", 0, 12), own("LROW"), x("O16", 0, 1), -WHOLE, A.add, A.add)
+        scan(R("O3", 0, 96), R("S3A", 0, 96), R("O2", 7, 487, 5))
+        tt(R("SEQ", 0, 192), R("SRC", 0, 128, 1, x("RKU", 0, 12)), R("KAT", 0, 192), A.max)
+        ts(x("QD"), R("O3", 3, 96, 6), -WHOLE, None, A.add)
         cp(R("TMY", 0, 128), R("SEQ", 0, 640, 1, x("QD", 0, 8)))
         act(R("TMY", 128, 256), R("SEQ", 0, 640, 1, x("QD", 8, 16)))
+        if not last:
+            act(R("SQA", 0, 192), ONE(192), COPY, -1.0)
         places(0, 2, last)
         if last:
             cp(R("OLT", 256, 512, 1, lpo), IOTA(256, 320))
@@ -612,12 +612,8 @@ def rank_program(g, core, T, topo):
         places(2, 4, last)
         ts(x("OFY"), own("YS", 256), x("OFS", 0, 1), None, A.add)
         places(4, 6, last)
-        if not last:
-            for t in range(4):
-                pick(t, 0, 16)
-            places(6, 8)
         keys = R(K, 0, 528, 1, x("OFY"))
-        F, Fn, K, Kn = Fn, F, Kn, K
+        K, Kn = Kn, K
 
     stored = [0]
 
@@ -631,13 +627,12 @@ def rank_program(g, core, T, topo):
         qf = R("QF", 128 * h, 128 * h + 128, 1, None, dt.uint8)
         store("y", T.oc[:, 512 * h:512 * h + 512], qf, ap(qf))
 
-    Fn = F
     for t in range(4):
         pick(t, 0, 8)
     for t in range(3):
         pick(t, 8, 16)
-    half(0)
     pick(3, 8, 16)
+    half(0)
     half(1)
 
     def scales(q, k):

import math
from concourse.mybir import dt, AluOpType, AxisListType, ActivationFunctionType

A = AluOpType
COPY = ActivationFunctionType.Copy
IDENT = ActivationFunctionType.Identity
RELU = ActivationFunctionType.Relu
SIGN = ActivationFunctionType.Sign
BIG = 2.0 ** 96
ROUNDS = 3
W64 = 4 * 256
UP_ = 0.5 - 1.0 / 128
WHOLE = 1.5 * 2.0 ** 23
SMALL_ = 2.0 ** 17
ON_SCALAR = 10

SCRATCH = {}


def _decl(names, where, shape, dtype):
    for n in names.split():
        SCRATCH[n] = (where, shape, dtype)


_decl("XT", "sbuf", [128, 768], "bfloat16")
_decl("UT VT", "sbuf", [128, 512], "bfloat16")
_decl("EA EB ONEB AD0 AD1 AD2 AD3", "sbuf", [128, 528], "bfloat16")
_decl("TI FA GI", "sbuf", [128, 1024], "bfloat16")
_decl("CMP", "sbuf", [128, 2304], "bfloat16")
_decl("JNK", "sbuf", [128, 8 * 272], "bfloat16")
_decl("CMN", "sbuf", [128, 4 * 272], "bfloat16")
_decl("RST SFP CFB EQR YB TMB CSP", "sbuf", [128, 256], "bfloat16")
_decl("CUM", "sbuf", [128, 4 * 192], "bfloat16")
_decl("QX", "sbuf", [128, 192], "float8_e4m3fn_x4")
_decl("QXS", "sbuf", [128, 192], "uint8")
_decl("QU QVC UR UP EQ0 EQ1 EQ2 EQ3", "sbuf", [128, 128], "float8_e4m3fn_x4")
_decl("QUS QVS URS UPS EQS0 EQS1 EQS2 EQS3", "sbuf", [128, 128], "uint8")
_decl("WQ", "sbuf", [128, 512], "float8_e4m3fn_x4")
_decl("WS", "sbuf", [128, 512], "uint8")
_decl("QF QT0 QT1 QT2 LQ0 LQ1 LQ2", "sbuf", [128, 256], "float8_e4m3fn_x4")
_decl("QFS QTS0 QTS1 QTS2 LS0 LS1 LS2", "sbuf", [128, 256], "uint8")
_decl("PS0 PS1 PS2 PS3 PP PQ PD0 PD1", "psum", [128, 512], "float32")
_decl("IOTA", "sbuf", [128, 512], "float32")
_decl("KA KB OLT", "sbuf", [128, 528], "float32")
_decl("SRC SEQ HR O2", "sbuf", [128, 640], "float32")
_decl("JM MASK DMASK RMIN LBM LBK TMP TMY YS PR OLR YO", "sbuf", [128, 256], "float32")
_decl("SEQS SC", "sbuf", [128, 208], "float32")
_decl("Z LROW KST KAT SQA", "sbuf", [128, 192], "float32")
_decl("CF", "sbuf", [128, 256], "float32")
_decl("X10 S2A", "sbuf", [128, 160], "float32")
_decl("O1 S3A O3", "sbuf", [128, 104], "float32")
_decl("LL AOS BIGS NR C4 X4 S1A", "sbuf", [128, 64], "float32")
SMALL = ("RB C1C C12 IW M16 M17 CNT RK KI0 ENC INV EN2 SP AR1 RST4 CN S4 CN4 ZX ZM C45 HC WT TB CT AX NI TTA AC C2I TTS IW5 "
         "S16 S161 N16 N161 CA CB PA PB PC PD C4C C8C LB0 OFS O16 O17 T1 C12P P1 P2 P3 P4 C32 HB HW").split()
_decl("SMALLS", "sbuf", [128, 32 * len(SMALL)], "float32")
_decl("INTS", "sbuf", [128, 16 * 11], "int32")
_decl("LW0 LW1 LW2 LP0 LP1 LP2", "sbuf", [128, 4], "uint16")
_decl("LISTS", "sbuf", [128, 16 * 12], "uint16")
_decl("XP0 XP1 XP2 XP3", "sbuf", [128, 208], "bfloat16")
_decl("FLA", "sbuf", [128, 256], "bfloat16")
_decl("STEP", "sbuf", [128, 192], "float32")
_decl("FLT", "sbuf", [128, 640], "bfloat16")
PIECE = {n: ("SMALLS", 32 * i) for i, n in enumerate(SMALL)}
PIECE.update({n: ("INTS", 16 * i) for i, n in enumerate("PI SI I2 I3 I4 I8 KI KA4 KB4 UI H3".split())})
PIECE.update({n: ("LISTS", 16 * i) for i, n in enumerate("RKU HU QV0 QD TU TBU AL UL OFY AU L4 L10".split())})

SEMAPHORES = ["sv", "ss", "st", "sg", "dx", "du", "dw", "dws", "dv", "dout", "loc", "au",
              "aq0", "aq1", "aq2", "al0", "al1", "al2"]


def R(name, a=0, b=16, st=1, off=None, bc=None):
    n, k = PIECE.get(name, (name, 0))
    return (n, k + a, k + b, st, off, bc)


def rank_program(g, core, T, topo):
    rank = T.rank_of(core)
    if rank is None:
        return
    nxt = T.cores[(rank + 1) % len(T.cores)]

    Q = {"v": g.vector, "s": g.scalar, "t": g.tensor, "g": g, "y": g.sync}
    sem_of = {"v": "sv", "s": "ss", "t": "st", "g": "sg"}
    cnt = {q: 0 for q in Q}
    known = {q: {} for q in Q}
    clocks = {}
    hist = {}

    def ap(r):
        n, a, b, st, off, bc = r
        x = T[n][:, a:b] if st == 1 else T[n][:, a:b:st]
        if bc is not None:
            x = x.bitcast(bc)
        if off is not None:
            x = x.indirect(ap(off))
        return x

    def meet(h, r):
        if h[0] >= r[2] or r[1] >= h[1]:
            return False
        return (h[0] - r[1]) % math.gcd(h[2], r[3]) == 0

    def wait(q, src, val):
        if known[q].get(src, 0) >= val:
            return
        Q[q].wait_ge(T.sem[sem_of.get(src, src)], val)
        for s, v in clocks[(src, val)].items():
            if known[q].get(s, 0) < v:
                known[q][s] = v

    def psum(n):
        return n in SCRATCH and SCRATCH[n][0] == "psum"

    def note(src, val, writes, reads):
        for w in writes:
            h = hist.setdefault(w[0], [])
            if w[3] == 1 and w[4] is None:
                h[:] = [e for e in h if not (w[1] <= e[0] and e[1] <= w[2])]
            h.append((w[1], w[2], w[3], True, src, val))
        for r in reads:
            hist.setdefault(r[0], []).append((r[1], r[2], r[3], psum(r[0]), src, val))

    def emit(q, call, writes, reads, event=None):
        reads = list(reads)
        for r in list(reads) + list(writes):
            if r[4] is not None:
                reads.append(r[4])
        need = {}
        for r in reads:
            for h in hist.get(r[0], ()):
                if meet(h, r) and h[3] and not (psum(r[0]) and h[4] == q):
                    need[h[4]] = max(need.get(h[4], 0), h[5])
        for w in writes:
            for h in hist.get(w[0], ()):
                if meet(h, w):
                    need[h[4]] = max(need.get(h[4], 0), h[5])
        for src in sorted(need, key=lambda s: -len(clocks[(s, need[s])])):
            wait(q, src, need[src])
        i = call()
        if event is None:
            cnt[q] += 1
            i.then_inc(T.sem[sem_of[q]], 1)
            src, val = q, cnt[q]
        else:
            src, val, inc = event
            i.then_inc(T.sem[src], inc)
        clocks[(src, val)] = dict(known[q])
        clocks[(src, val)][src] = val
        note(src, val, writes, reads)

    def lands(src, val, writes):
        clocks[(src, val)] = {src: val}
        note(src, val, writes, [])

    def isr(x):
        return isinstance(x, tuple)

    def val(x):
        return ap(x) if isr(x) else x

    def tt(o, a, b, op):
        emit("v", lambda: g.vector.tensor_tensor(ap(o), ap(a), ap(b), op), [o], [a, b])

    def ts(o, a, s1, s2, op0, op1=None):
        rd = [a] + [x for x in (s1, s2) if isr(x)]
        if op1 is None:
            emit("v", lambda: g.vector.tensor_scalar(ap(o), ap(a), val(s1), None, op0), [o], rd)
        else:
            emit("v", lambda: g.vector.tensor_scalar(ap(o), ap(a), val(s1), val(s2), op0, op1), [o], rd)

    def cp(o, a):
        emit("v", lambda: g.vector.tensor_copy(ap(o), ap(a)), [o], [a])

    def scan(o, d0, d1, op0=A.mult, op1=A.add, init=0.0):
        emit("v", lambda: g.vector.tensor_tensor_scan(ap(o), ap(d0), ap(d1), init, op0, op1), [o], [d0, d1])

    def red(o, a, op):
        emit("v", lambda: g.vector.tensor_reduce(ap(o), ap(a), AxisListType.X, op), [o], [a])

    def fill(o, c):
        emit("v", lambda: g.vector.memset(ap(o), c), [o], [])

    def quant(o, s, a, n, at=0, to=0):
        o, s, a = R(o, to, to + n), R(s, to, to + n), R(a, at, at + 4 * n)
        emit("v", lambda: g.vector.quantize_mx(ap(o), ap(s), ap(a)), [o, s], [a])

    def act(o, a, func=COPY, scale=1.0, bias=0.0):
        rd = [a] + [x for x in (scale, bias) if isr(x)]
        if func == COPY and not isr(scale) and scale == 1.0:
            emit("s", lambda: g.scalar.activation(ap(o), ap(a), COPY), [o], rd)
        elif func == COPY:
            emit("s", lambda: g.scalar.activation(ap(o), ap(a), COPY, scale=val(scale)), [o], rd)
        else:
            emit("s", lambda: g.scalar.activation(ap(o), ap(a), func, bias=val(bias), scale=val(scale)), [o], rd)

    turns = [0]

    def total(o, a, n, bias=None):
        j = R("JNK", 272 * (turns[0] % 8), 272 * (turns[0] % 8) + n)
        turns[0] += 1
        if bias is None:
            emit("s", lambda: g.scalar.activation(ap(j), ap(a), COPY, accum_out=ap(o)), [j, o], [a])
        else:
            emit("s", lambda: g.scalar.activation(ap(j), ap(a), SIGN, bias=ap(bias), scale=-1.0, accum_out=ap(o)), [j, o], [a, bias])

    def mm(o, l, ls, r, rs, n=256, c=0, at=0):
        o, l, ls, r, rs = R(o, 0, n), R(l, c, c + 128), R(ls, c, c + 128), R(r, at, at + n), R(rs, at, at + n)
        emit("t", lambda: g.tensor.matmul_mx(ap(o), ap(l), ap(ls), ap(r), ap(rs), True, True), [o], [l, ls, r, rs])

    def iota(o, pattern, base=0, cm=0):
        if SCRATCH[o[0]][2] == "int32":
            emit("g", lambda: g.iota(ap(o), pattern, base, cm), [o], [])
        else:
            emit("g", lambda: g.iota(ap(o), pattern, base, cm, allow_small_or_imprecise_dtypes=True), [o], [])

    def load(q, o, src, sem):
        emit(q, lambda: Q[q].dma_start(ap(o), src), [o], [], (sem, 16, 16))

    sent = [0]
    engines = len(topo.engines(core, nxt))
    rid, pid = topo.addr(nxt)[:2]

    def send(o, a, sem):
        need = {}
        for h in hist.get(a[0], ()):
            if meet(h, a) and h[3]:
                need[h[4]] = max(need.get(h[4], 0), h[5])
        for src in need:
            wait("g", src, need[src])
        g.remote_dma(out_ap=ap(o), in_ap=ap(a), remote_sem=T.sem[sem], local_sem=T.sem["loc"], pid=pid, routing_id=rid,
                     dma_engine_mask=topo.mask(core, nxt))
        sent[0] += engines

    def send_codes(o, os, a, s, n, sem):
        send(R(o, 0, n, 1, None, dt.uint8), R(a, 0, n, 1, None, dt.uint8), sem)
        send(R(os, 0, n), R(s, 0, n), sem)

    lands("au", 2 * engines, [R("UP", 0, 128), R("UPS", 0, 128)])
    for r in range(ROUNDS):
        lands("aq%d" % r, 2 * engines, [R("LQ%d" % r, 0, 256), R("LS%d" % r, 0, 256)])
        lands("al%d" % r, engines, [R("LP%d" % r, 0, 4)])

    load("y", R("UT", 0, 512), T.u[:], "du")
    load("y", R("XT", 0, 768), T.x[:], "dx")
    load("y", R("WQ", 0, 512, 1, None, dt.uint8), T.wc[:], "dw")
    load("y", R("WS", 0, 512), T.ws[:], "dws")
    load("y", R("VT", 0, 512), T.v[:], "dv")

    x = R
    ONE = lambda n: R("ONEB", 0, n)
    MASK = lambda n: R("MASK", 0, n)
    RST = lambda n: R("RST", 0, n)
    IOTA = lambda a, b, off=None: R("IOTA", a, b, 1, off)

    def own(o, n=192):
        return R(o, 15, n, 16)

    def const(o, n, c):
        iota(R(o, *n), [[0, n[1] - n[0]]], c)

    iota(x("PI", 0, 1), [[1, 1]], 0, 1)
    iota(R("JM", 0, 256), [[0, 16], [1, 16]])
    iota(x("UI", 0, 8), [[16, 8]])
    iota(x("M16"), [[16, 16]])
    iota(x("C4C", 0, 4), [[4, 4]])
    iota(x("C12"), [[12, 16]])
    fill(ONE(528), 1.0)
    for k, (pattern, c) in enumerate((([[4, 16], [0, 2]], 7), ([[4, 16], [0, 2]], 3), ([[4, 16], [0, 2]], 3), ([[1, 16], [16, 2]], 72), ([[0, 32]], 68))):
        iota(R("X10", k, 160, 5), pattern, c)
    for k, c in ((0, 0), (1, -1), (4, 1)):
        iota(R("S2A", k, 160, 5), [[0, 32]], c)
    for b in range(4):
        const("XP%d" % b, (192, 208), 0)

    def later_constants():
        iota(R("HR", 0, 192), [[4, 64], [1, 3]])
        for b in range(4):
            const("AD%d" % b, (512, 528), 0)
        for n, b in (("EA", 2), ("EB", 3)):
            o = R(n, 0, 516)
            emit("g", lambda: g.affine_select(ap(o), ap(ONE(516)), [[-1, 516]], A.is_equal, 0.0, b, 4), [o], [ONE(516)])
        const("FLT", (192, 640), 0)
        const("SEQ", (192, 640), 512)

    def last_constants():
        iota(x("C12P"), [[12, 16]], 12)
        iota(x("C32", 0, 8), [[32, 8]], 80)
        const("HB", (0, 8), 0)
        const("RB", (0, 24), 0)
        const("HC", (0, 8), 0)
        iota(x("RST4"), [[0, 4], [1000, 4]])
        const("C4", (0, 64), 4)
        iota(R("C4", 0, 64, 4), [[0, 4], [1, 4]])
        iota(R("C4", 1, 64, 4), [[0, 4], [-1, 4]], 4)
        iota(R("S1A", 0, 64), [[0, 16], [1, 4]])
        iota(R("S1A", 2, 64, 4), [[0, 16]], -1)
        const("O1", (64, 68), 0)
        const("O1", (68, 72), int(WHOLE))
        const("C45", (0, 32), -5)
        const("S3A", (0, 96), 1)
        iota(R("S3A", 0, 96, 6), [[0, 16]])

    scan(IOTA(0, 512), ONE(512), ONE(512), A.mult, A.add, -1.0)
    ts(x("SI", 0, 1), x("PI", 0, 1), 15, None, A.bitwise_and)
    ts(RST(256), R("JM", 0, 256), 0.0, None, A.not_equal)
    cp(x("SP", 0, 1), x("SI", 0, 1))
    s = x("SP", 0, 1)
    cp(x("UL", 0, 8), x("UI", 0, 8))
    ts(MASK(256), R("JM", 0, 256), s, None, A.is_equal)
    act(x("IW"), x("M16"), IDENT, 1.0, s)
    act(R("RMIN", 0, 192), RST(192), IDENT, 2 * BIG, -BIG)
    act(R("DMASK", 0, 192), MASK(192), IDENT, 2 * BIG, -BIG)

    def tables_a():
        act(R("CF", 0, 256), MASK(256), IDENT, -33.0 * 1024, 1024.0)
        act(R("CFB", 0, 256), MASK(256), IDENT, -65.0, 1.0)

    def tables_c():
        act(R("LBM", 0, 256), IOTA(0, 256), IDENT, -BIG / 2, x("LB0", 0, 1))
        act(x("S16", 0, 1), s, COPY, -1.0 / 16)
        act(x("S161", 0, 1), s, IDENT, -1.0 / 16, -1.0 / 16)
        act(x("CA", 0, 1), s, IDENT, 0.75, UP_)
        act(x("CB", 0, 1), s, IDENT, 0.75, 0.75 + UP_)
        act(R("STEP", 0, 64), ONE(64), COPY, 0.0)
        act(R("STEP", 64, 192), ONE(128))
        act(R("SQA", 0, 192), ONE(192), COPY, -1.0)

    def tables_d():
        act(R("CMN", 192, 4 * 208, 208), x("IW", 0, 4))
        act(x("IW5", 0, 8), x("IW", 0, 8), IDENT, 1.0, 0.5)
        act(x("T1"), x("IW"), IDENT, 1.0, 193.0)
        act(R("O2", 7, 480, 30), x("IW"), IDENT, 1.0, 192.0)
        act(R("S2A", 2, 160, 10), ONE(16), COPY, x("S16", 0, 1))
        act(R("S2A", 7, 160, 10), ONE(16), COPY, x("S161", 0, 1))
        act(R("O1", 72, 88), x("C12"), IDENT, 1.0, x("CA", 0, 1))
        act(R("O1", 88, 104), x("C12"), IDENT, 1.0, x("CB", 0, 1))

    spare = [
        lambda: fill(R("KA", 512, 528), BIG),
        lambda: fill(R("KB", 512, 528), BIG),
        lambda: scan(R("YS", 0, 160), R("CF", 0, 160), R("X10", 0, 160), A.add, A.max),
        lambda: ts(x("PA", 0, 1), x("I3", 0, 1), 0.0, 4.0, A.is_equal, A.mult),
        lambda: ts(x("PB", 0, 1), x("I3", 0, 1), 1.5, None, A.is_gt),
        lambda: ts(x("L10", 0, 10), own("YS", 160), x("OFS", 0, 1), None, A.add),
        lambda: ts(x("AL", 0, 1), x("I2", 0, 1), 3.0, None, A.add),
        lambda: ts(x("INV", 0, 1), x("I4", 0, 1), x("PB", 0, 1), x("PA", 0, 1), A.mult, A.add),
        lambda: ts(x("M17"), x("IW"), 192.0, x("O17", 0, 1), A.add, A.mult),
        lambda: ts(x("O16", 0, 1), s, WHOLE - 16.0, None, A.add),
        lambda: ts(x("L4", 0, 4), x("C4C", 0, 4), x("INV", 0, 1), None, A.add),
        lambda: ts(x("CT"), x("M17"), WHOLE, None, A.add),
        lambda: fill(R("O2", 2, 488, 30), 0.0),
    ]

    def meanwhile(n):
        for _ in range(min(n, len(spare))):
            spare.pop(0)()

    ts(x("LB0", 0, 1), s, 15.5 / 16, 8 * BIG, A.add, A.mult)
    cp(x("KI"), x("IW"))
    ts(x("H3"), x("IW"), 1.0 / 3, -1.0 / 3, A.mult, A.add)
    ts(x("OFS", 0, 1), s, -15.0, 1024.0, A.add, A.mult)
    ts(x("O17", 0, 1), s, -1.0, 16.0, A.mult, A.add)
    ts(x("KA4"), x("KI"), 2, None, A.arith_shift_right)
    ts(x("KB4"), x("KI"), 3, None, A.bitwise_and)
    tt(x("M17"), x("IW"), x("H3"), A.add)
    fill(R("SEQS", 192, 208), 192.0)
    ts(x("KI0"), x("KA4"), 3.0, -192.0, A.mult, A.add)
    ts(x("INV"), x("KB4"), 2.5, None, A.is_lt)
    tables_a()
    quant("QU", "QUS", "UT", 128)
    tt(x("ENC"), x("KI0"), x("KB4"), A.add)
    cp(x("HU", 0, 12), x("M17", 0, 12))
    cp(R("UR", 0, 128, 1, None, dt.uint32), R("QU", 0, 128, 1, R("UL", 0, 8), dt.uint32))
    act(R("URS", 0, 128), R("QUS", 0, 128, 1, R("UL", 0, 8)))
    quant("QX", "QXS", "XT", 192)
    mm("PP", "UR", "URS", "QX", "QXS", 192)
    send_codes("UP", "UPS", "UR", "URS", 128, "au")
    later_constants()
    for b in range(4):
        act(R("XP%d" % b, 0, 192), R("XT", b, 768, 4))
    tt(x("EN2"), x("ENC"), x("INV"), A.mult)
    fill(R("SC", 192, 208), BIG)
    fill(R("BIGS", 0, 64), BIG)
    ts(x("QD"), x("EN2"), 192.0, None, A.add)
    for n, k, op in (("I2", 12, A.bitwise_and), ("I3", 3, A.bitwise_and), ("I4", 2, A.arith_shift_right)):
        ts(x(n, 0, 1), x("SI", 0, 1), k, None, op)

    def ranks(row, diag):
        for a in (0, 96):
            tt(R("TMP", a, a + 96), diag(a), R("DMASK", 0, 96), A.min)
        for a in (0, 96):
            scan(R("Z", a, a + 96), R("RMIN", 0, 96), R("TMP", a, a + 96), A.min, A.max, -BIG)
        for i in range(12):
            c = (i + 12 - ON_SCALAR) % 12
            k = R("Z", 16 * c + 15, 16 * c + 16)
            e = 16 * c + 16
            ts(R("CMP", 192 * c, 192 * c + e), R(row, 0, e), k, None, A.is_le)
            if e < 192:
                ts(R("CMP", 192 * c + e, 192 * c + 192), R(row, e, 192), k, None, A.is_lt)
            if i < ON_SCALAR:
                total(x("CNT", c, c + 1), R("CMP", 192 * c, 192 * c + 192), 192)
            if i == 7:
                tt(R("EQR", 0, 192), R("Z", 0, 192), R(row, 0, 192), A.is_equal)
            if i == 8:
                scan(R("YB", 0, 192), RST(192), R("EQR", 0, 192))

    def ranks_end():
        n = 12 - ON_SCALAR
        tt(x("RK", n, 11), x("CNT", n, 11), R("YB", 16 * n + 15, 176, 16), A.subtract)
        for c in range(n):
            scan(R("CUM", 192 * c, 192 * c + 192), ONE(192), R("CMP", 192 * c, 192 * c + 192))
        cp(x("RKU", n, 11), x("RK", n, 11))
        for c in (0, 11) + tuple(range(1, n)):
            a = x("CNT", c, c + 1) if c >= n else R("CUM", 192 * c + 191, 192 * c + 192)
            ts(x("RKU", c, c + 1), a, R("YB", 16 * c + 15, 16 * c + 16), None, A.subtract)

    def fold(o, y, a, n):
        scan(R(y, 0, n), R("CF", 0, n), R(a, 0, n), A.add, A.max)
        ts(o, own(y, n), x("OFS", 0, 1), None, A.add)

    ranks("PP", lambda a: R("PP", a, a + 96))
    act(R("SC", 0, 192), R("PP", 0, 192))
    ranks_end()
    meanwhile(2)
    cp(R("SEQS", 0, 192, 1, x("RKU", 0, 12)), IOTA(0, 192))
    meanwhile(1)
    tables_c()
    tables_d()
    tt(R("TMB", 0, 256), R("SEQS", 0, 208, 1, x("QD")), MASK(256), A.mult)
    meanwhile(2)
    scan(R("YB", 0, 256), RST(256), R("TMB", 0, 256))
    meanwhile(2)
    cp(x("OFY"), own("YB", 256))
    meanwhile(2)

    F = "FA"
    K, Kn = "KA", "KB"
    keys = R("SC", 0, 208, 1, x("OFY"))
    hu = x("HU", 0, 12)
    h0, h1 = x("HB", 0, 16), x("HB", 1, 17)
    r0, r1 = x("RB", 0, 16), x("RB", 1, 17)
    nsel = R("S1A", 3, 64, 4)

    def pick(t, a, b, first=False):
        o = R(F, 64 * a + t, 64 * b, 4)
        w, k = (R("XP%d" % t, 0, 208, 1, x("OFY", a, b)), 1.0) if first else (R("AD%d" % t, 0, 528, 1, x("OFY", a, b)), 0.015625)
        if t < 2:
            act(o, w, COPY, k)
        elif first:
            cp(o, w)
        else:
            ts(o, w, k, None, A.mult)

    def places(a, b, skip=False):
        if not skip:
            cp(R("HR", 0, 640, 1, x("QD", a, b)), IOTA(16 * a, 16 * b))

    for r in range(ROUNDS):
        last = r == ROUNDS - 1
        qt, qts, lq, ls, lw, lp = ["%s%d" % (n, r) for n in ("QT", "QTS", "LQ", "LS", "LW", "LP")]

        def add(b, k, l, bank):
            tt(R("AD%d" % b, k, l), R(bank, 0, l - k), R("GI", 4 * k + b, 4 * l, 4), A.add)

        def tile(b, k, l):
            o, a = R("TI", 4 * k + b, 4 * l, 4), R("AD%d" % b, k, l)
            if b < 2:
                act(o, a, COPY, 0.015625)
            else:
                ts(o, a, 0.015625, None, A.mult)

        for t in range(4):
            pick(t, 0, 16, r == 0)
        places(6, 8, r == 0)
        banks = ("PS0", "PP", "PS1", "PQ", "PS2", "PD1", "PS3", "PD0")
        for h in range(2):
            quant("QF", "QFS", F, 128, 512 * h, 128 * h)
        for b in range(4):
            for h in range(2):
                mm(banks[2 * b + h], "WQ", "WS", "QF", "QFS", 128, 128 * b, 128 * h)
            act(R("GI", b, W64, 4), R(F, b, W64, 4), COPY, 64.0)
        places(8, 16, r == 0)
        meanwhile(5)
        for b in range(4):
            for h in range(2):
                add(b, 128 * h, 128 * h + 128, banks[2 * b + h])
            if b < 2:
                tile(b, 0, 256)
        for h in range(2):
            tile(2, 128 * h, 128 * h + 128)
            tile(3, 128 * h, 128 * h + 128)
        for h, p in enumerate(("PS0", "PS1")):
            quant(qt, qts, "TI", 128, 512 * h, 128 * h)
            mm(p, "UR", "URS", qt, qts, 128, 0, 128 * h)
        send_codes(lq, ls, qt, qts, 256, "aq%d" % r)
        act(R(K, 0, 256), keys)
        act(R("PR", 0, 128), R("PS0", 0, 128))
        if r == 0:
            last_constants()
        else:
            fold(hu, "YS", "HR", 192)
        cp(R("PR", 128, 256), R("PS1", 0, 128))
        act(R("SC", 0, 192), R("PR", 0, 256, 1, hu))
        act(R("KAT", 0, 192), R(K, 0, 256, 1, hu))
        ranks("SC", lambda a: R("PR", 0, 256, 1, x("HU", a // 16, a // 16 + 6)))
        ranks_end()
        lpo = R(lp, 0, 4)
        arr = R(K, 256, 512, 1, lpo)

        def units(b):
            if r == 0:
                quant("EQ%d" % b, "EQS%d" % b, "EB" if b % 2 else "EA", 128, 2 - b // 2 * 2)

        def unpack(b):
            p = ("PD0", "PD1", "PS2", "PS3")[b]
            mm(p, "EQ%d" % b, "EQS%d" % b, lq, ls)
            act(R("AD%d" % b, 256, 512), R(p, 0, 256), COPY, 64.0)

        def before(c):
            ts(R("CMN", 208 * c + 64, 208 * c + 192), R("KST", 0, 128), R("AOS", 16 * c + 15, 16 * c + 16), None, A.is_le)
            total(x("TTA", c, c + 1), R("CMN", 208 * c + 64, 208 * c + 193), 129)

        def stay(a, b):
            for c in range(a, b):
                total(x("P3", c, c + 1), R("CUM", 16 * c, 16 * c + 80), 80, x("IW5", c, c + 1))

        units(0)
        cp(R("LROW", 0, 192, 1, x("RKU", 0, 12)), R("HR", 0, 192))
        act(R("FLT", 0, 192), R("STEP", 0, 192, 1, x("RKU", 0, 12)))
        act(R("SFP", 0, 256), R("FLT", 0, 640, 1, x("QD")))
        units(1)
        scan(R("CUM", 0, 192), ONE(192), R("FLT", 0, 192))
        stay(0, 7)
        mm("PQ", "UP", "UPS", lq, ls)
        act(R(K, 256, 512), R("PQ", 0, 256))
        scan(R("LL", 0, 64), R("CF", 0, 64), R("LROW", 0, 64), A.add, A.max)
        units(2)
        ts(R(lw, 0, 4), own("LL", 64), x("OFS", 0, 1), None, A.add)
        send(R(lp, 0, 4), R(lw, 0, 4), "al%d" % r)
        units(3)
        if r == 0:
            iota(R("OLT", 0, 512), [[1, 512]])
            const("OLT", (512, 528), -1)
        if last:
            quant("QVC", "QVS", "VT", 128)
        ts(R("CMP", 0, 80), R("CUM", 112, 192), x("IW5", 7, 8), None, A.is_lt)
        cp(R(K, 0, 256, 1, R(lw, 0, 4)), R("BIGS", 0, 64))
        red(x("P3", 7, 8), R("CMP", 0, 80), A.add)
        scan(R("CSP", 0, 256), ONE(256), R("SFP", 0, 256))
        scan(R("LBK", 0, 256), R(K, 0, 256), R("LBM", 0, 256), A.min, A.max, BIG)
        ts(x("TBU", 7, 8), x("P3", 7, 8), 112.0, None, A.add)
        scan(R("YB", 0, 256), R("CFB", 0, 256), R("SFP", 0, 256), A.add, A.max)
        tt(h1, own("CSP", 256), x("C12P"), A.subtract)
        tt(x("P4", 0, 6), x("P3", 0, 6), x("C32", 0, 6), A.add)
        scan(R("TMB", 0, 256), R("CFB", 0, 256), R("CSP", 0, 256), A.add, A.max)
        ts(x("TBU", 0, 6), x("P4", 0, 6), 0.5, None, A.mult)
        ts(x("TBU", 6, 7), x("P3", 6, 7), 80.0 + 32 * 6, 0.5, A.add, A.mult)
        act(R("KST", 0, 128), R("KAT", 0, 192, 1, x("TBU", 0, 8)))
        ts(R("FLA", 0, 256), R(K, 256, 512), R("LBK", 255, 256), None, A.is_lt)
        total(x("AR1", 0, 1), R("FLA", 0, 256, 1, lpo), 64)
        act(R("NR", 0, 64), IOTA(256, 512, lpo), COPY, 1.0 / SMALL_)
        unpack(0)
        tt(R("TMP", 0, 64), arr, MASK(64), A.mult)
        tt(x("P1"), own("YB", 256), x("T1"), A.mult)
        tt(x("P2"), own("TMB", 256), x("CT"), A.add)
        scan(R("AOS", 0, 64), RST(64), R("TMP", 0, 64))
        cp(x("AU", 0, 1), x("AR1", 0, 1))
        before(3)
        tt(r1, IOTA(0, 72, x("AU", 0, 1)), h1, A.add)
        before(2)
        before(1)
        tt(x("CN"), r1, r0, A.subtract)
        before(0)
        tt(x("TB"), x("P2"), x("P1"), A.subtract)
        scan(x("S4"), x("RST4"), x("CN"), A.min, A.max)
        tt(R("X4", 0, 64), R("RB", 0, 24, 1, x("L4", 0, 4)), R("C4", 0, 64), A.mult)
        act(x("HC", 1, 17), IOTA(0, 72, x("AU", 0, 1)))
        ts(nsel, R("S4", 0, 16, 1, x("AL", 0, 1)), 2.5, -1.0, A.is_gt, A.mult)
        tt(x("CN4", 0, 4), x("RB", 4, 17, 4), x("RB", 0, 13, 4), A.subtract)
        scan(R("O1", 0, 64), R("S1A", 0, 64), R("X4", 0, 64))
        act(R("X10", 0, 160), R("O1", 0, 104, 1, x("L10", 0, 10)))
        tt(x("ZX", 0, 4), x("CN4", 0, 4), R("S1A", 3, 64, 16), A.mult)
        cp(x("TU", 0, 4), x("TTA", 0, 4))
        tt(R("O2", 22, 480, 30), x("TB"), x("HC"), A.add)
        act(R("O2", 17, 480, 30), R("O2", 22, 480, 30), COPY, -1.0)
        act(R("SRC", 0, 128), R("HR", 0, 192, 1, x("TBU", 0, 8)))
        red(x("ZM", 0, 1), x("ZX", 0, 4), A.min)
        cp(R("SQA", 0, 192, 1, x("TU", 0, 4)), R("NR", 0, 64))
        ts(R("S2A", 3, 160, 5), x("C45", 0, 32), x("ZM", 0, 1), 0.25, A.is_lt, A.mult)
        act(x("NI"), nsel, IDENT, 1.0, R("S2A", 3, 4))
        act(R("KAT", 0, 192), R("SQA", 0, 192), RELU, SMALL_)
        for b in range(1, 4):
            unpack(b)
        tt(x("AX"), x("HC", 1, 17), x("HC"), A.subtract)
        scan(R("Z", 0, 192), ONE(192), R("SQA", 0, 192), A.mult, A.subtract)
        scan(R("O2", 0, 480, 3), R("S2A", 0, 160), R("X10", 0, 160))
        scan(R("LROW", 0, 192), R("CFB", 0, 192), R("Z", 0, 192), A.add, A.max)
        tt(R("S3A", 1, 96, 6), R("O2", 27, 480, 30), R("O2", 12, 480, 30), A.is_le)
        tt(R("S3A", 3, 96, 6), x("AX"), x("NI"), A.is_ge)
        ts(x("RKU", 0, 12), own("LROW"), x("O16", 0, 1), -WHOLE, A.add, A.add)
        scan(R("O3", 0, 96), R("S3A", 0, 96), R("O2", 7, 487, 5))
        tt(R("SEQ", 0, 192), R("SRC", 0, 128, 1, x("RKU", 0, 12)), R("KAT", 0, 192), A.max)
        ts(x("QD"), R("O3", 3, 96, 6), -WHOLE, None, A.add)
        cp(R("TMY", 0, 128), R("SEQ", 0, 640, 1, x("QD", 0, 8)))
        act(R("TMY", 128, 256), R("SEQ", 0, 640, 1, x("QD", 8, 16)))
        if not last:
            act(R("SQA", 0, 192), ONE(192), COPY, -1.0)
        places(0, 2, last)
        if last:
            cp(R("OLT", 256, 512, 1, lpo), IOTA(256, 320))
        scan(R("YS", 0, 256), R("CF", 0, 256), R("TMY", 0, 256), A.add, A.max)
        places(2, 4, last)
        ts(x("OFY"), own("YS", 256), x("OFS", 0, 1), None, A.add)
        places(4, 6, last)
        keys = R(K, 0, 528, 1, x("OFY"))
        K, Kn = Kn, K

    stored = [0]

    def store(q, dst, a, src):
        stored[0] += 1
        emit(q, lambda: Q[q].dma_start(dst, src), [], [a], ("dout", 16 * stored[0], 16))

    def half(h):
        quant("QF", "QFS", F, 128, 512 * h, 128 * h)
        mm(("PP", "PQ")[h], "QVC", "QVS", "QF", "QFS", 128, 0, 128 * h)
        qf = R("QF", 128 * h, 128 * h + 128, 1, None, dt.uint8)
        store("y", T.oc[:, 512 * h:512 * h + 512], qf, ap(qf))

    for t in range(4):
        pick(t, 0, 8)
    for t in range(3):
        pick(t, 8, 16)
    pick(3, 8, 16)
    half(0)
    half(1)

    def scales(q, k):
        store(q, T.osc[4 * k:4 * k + 4, 0:256], R("QFS", 0, 256), T.QFS[32 * k:32 * k + 4, 0:256])

    act(R("YO", 0, 128), R("PP", 0, 128))
    cp(R("OLR", 0, 256), R("OLT", 0, 528, 1, x("OFY")))
    scales("y", 0)
    scales("y", 1)
    store("s", T.y[:, 0:128], R("YO", 0, 128), ap(R("YO", 0, 128)))
    scales("s", 2)
    scales("s", 3)
    cp(R("YO", 128, 256), R("PQ", 0, 128))
    store("y", T.y[:, 128:256], R("YO", 128, 256), ap(R("YO", 128, 256)))
    store("s", T.ol[:, 0:256], R("OLR", 0, 256), T.OLR[0:128:16, 0:256])

    for q in ("v", "s", "t", "g"):
        if known["g"].get(q, 0) < cnt[q]:
            g.wait_ge(T.sem[sem_of[q]], cnt[q])
    for n in ("dx", "du", "dw", "dws", "dv"):
        g.wait_ge(T.sem[n], 16)
    g.wait_ge(T.sem["dout"], 16 * stored[0])
    g.wait_ge(T.sem["loc"], sent[0])
    g.wait_ge(T.sem["au"], 2 * engines)
    for r in range(ROUNDS):
        g.wait_ge(T.sem["aq%d" % r], 2 * engines)
        g.wait_ge(T.sem["al%d" % r], engines)
